import numpy as np
import ml_dtypes


def mxq(x, axis, fmt="e4m3"):
    dtype, down = {"e4m3": (ml_dtypes.float8_e4m3fn, 7), "e5m2": (ml_dtypes.float8_e5m2, 14)}[fmt]
    v = np.moveaxis(np.asarray(x, np.float32).astype(ml_dtypes.bfloat16).astype(np.float64), axis, -1)
    blocks = v.reshape(v.shape[:-1] + (-1, 32))
    amax = np.abs(blocks).max(-1, keepdims=True)
    byte = np.maximum(np.where(amax > 0, np.frexp(amax)[1] - 1 + 127, 0) - down, 1)
    scale = np.exp2(byte - 127.0)
    codes = (blocks / scale).astype(np.float32).astype(dtype).astype(np.float64)
    return np.moveaxis((codes * scale).reshape(v.shape), -1, axis)


WIDE = False


def mx_kscale(k):
    if not WIDE:
        return np.ones(k)
    levels = np.array([24, -24, 12, -12, 0])
    if k % 512:
        return np.exp2(np.random.permutation(np.resize(levels, k // 32))).repeat(32)
    a = np.empty((k // 512, 16))
    for p in range(k // 512):
        a[p, :8] = np.random.permutation(np.resize(levels, 8))
        for g in range(8):
            far = levels[np.abs(levels - a[p, g]) >= 10]
            a[p, g + 8] = far[np.random.randint(len(far))]
    return np.exp2(a.ravel()).repeat(32)


def f64(x):
    return np.asarray(x).astype(np.float64)


E2M1 = np.array([0.0, 0.5, 1.0, 1.5, 2.0, 3.0, 4.0, 6.0, -0.0, -0.5, -1.0, -1.5, -2.0, -3.0, -4.0, -6.0])


def pack_weight(w, fmt):
    k, n = w.shape
    w = f64(np.asarray(w, np.float32).astype(ml_dtypes.bfloat16)).reshape(k // 32, 32, n)
    amax = np.abs(w).max(1)
    if fmt == "e4m3":
        byte = np.frexp(amax)[1] - 1 + 127 - 7
    else:
        mant, ex = np.frexp(amax / 6.0)
        byte = np.where(mant > 0.5, ex, ex - 1) + 127
    byte = np.clip(np.where(amax > 0, byte, 1), 1, 254)
    scaled = (w * np.exp2(127.0 - byte)[:, None, :]).reshape(k, n).astype(np.float32)
    by_word = np.ascontiguousarray(scaled.reshape(k // 512, 128, 4, n).transpose(0, 1, 3, 2))
    if fmt == "e4m3":
        words = by_word.astype(ml_dtypes.float8_e4m3fn).view(np.uint8)
    else:
        c = by_word.astype(ml_dtypes.float4_e2m1fn).view(np.uint8) & 0xF
        words = (c[..., 0::2] | (c[..., 1::2] << 4)).reshape(k // 512, 128, 2 * n)
    return np.ascontiguousarray(words), np.ascontiguousarray(byte.astype(np.uint8).reshape(k // 512, 16, n))


def unpack_weight(words, scales, fmt):
    g, _, n = scales.shape
    words = np.ascontiguousarray(words).reshape(g, 128, n, -1)
    if fmt == "e4m3":
        vals = words.view(ml_dtypes.float8_e4m3fn).astype(np.float64)
    else:
        nib = np.empty((g, 128, n, 4), np.uint8)
        nib[..., 0::2] = words & 0xF
        nib[..., 1::2] = words >> 4
        vals = E2M1[nib]
    vals = vals * np.repeat(np.exp2(scales.astype(np.float64) - 127.0), 8, axis=1)[..., None]
    return vals.transpose(0, 1, 3, 2).reshape(g * 512, n)


K, N, T = 512, 512, 1024


def setup_inputs():
    n = np.random.standard_normal
    s = mx_kscale(K)[:, None]
    p_wr = pack_weight(n((K, N)) / np.sqrt(4 * K) / s, "e4m3")
    p_wi = pack_weight(n((K, N)) / np.sqrt(4 * K) / s, "e4m3")
    p_wj = pack_weight(n((K, N)) / np.sqrt(4 * K) / s, "e2m1")
    p_wk = pack_weight(n((K, N)) / np.sqrt(4 * K) / s, "e2m1")
    return {
        "xr": (n((K, T)) * s).astype(np.float32),
        "xi": (n((K, T)) * s).astype(np.float32),
        "xj": (n((K, T)) * s).astype(np.float32),
        "xk": (n((K, T)) * s).astype(np.float32),
        "wr_words": p_wr[0],
        "wr_scales": p_wr[1],
        "wi_words": p_wi[0],
        "wi_scales": p_wi[1],
        "wj_words": p_wj[0],
        "wj_scales": p_wj[1],
        "wk_words": p_wk[0],
        "wk_scales": p_wk[1],
        "br": (0.3 * n(N)).astype(np.float32),
        "bi": (0.3 * n(N)).astype(np.float32),
        "bj": (0.3 * n(N)).astype(np.float32),
        "bk": (0.3 * n(N)).astype(np.float32),
    }


def reference(xr, xi, xj, xk, wr_words, wr_scales, wi_words, wi_scales, wj_words, wj_scales, wk_words, wk_scales, br, bi, bj, bk):
    xr_ = mxq(f64(xr), 0, "e4m3")
    xi_ = mxq(f64(xi), 0, "e4m3")
    xj_ = mxq(f64(xj), 0, "e4m3")
    xk_ = mxq(f64(xk), 0, "e4m3")
    wr_ = unpack_weight(wr_words, wr_scales, "e4m3")
    wi_ = unpack_weight(wi_words, wi_scales, "e4m3")
    wj_ = unpack_weight(wj_words, wj_scales, "e2m1")
    wk_ = unpack_weight(wk_words, wk_scales, "e2m1")
    pr = wr_.T @ xr_
    mr = wi_.T @ xi_ + wj_.T @ xj_ + wk_.T @ xk_
    pi = wr_.T @ xi_ + wi_.T @ xr_ + wj_.T @ xk_
    mi = wk_.T @ xj_
    pj = wr_.T @ xj_ + wj_.T @ xr_ + wk_.T @ xi_
    mj = wi_.T @ xk_
    pk = wr_.T @ xk_ + wi_.T @ xj_ + wk_.T @ xr_
    mk = wj_.T @ xi_
    return pr - mr + f64(br)[:, None], pi - mi + f64(bi)[:, None], pj - mj + f64(bj)[:, None], pk - mk + f64(bk)[:, None]

@@ -1,0 +1,255 @@
+from contextlib import ExitStack
+
+import concourse.mybir as mybir
+from concourse.masks import make_identity
+
+K, N, T = 512, 512, 1024
+FLOPS = 16 * 2 * K * N * T
+
+F32 = mybir.dt.float32
+BF16 = mybir.dt.bfloat16
+I32 = mybir.dt.int32
+U32 = mybir.dt.uint32
+U8 = mybir.dt.uint8
+FP8X4 = mybir.dt.float8_e4m3fn_x4
+FP4X4 = mybir.dt.float4_e2m1fn_x4
+ADD = mybir.AluOpType.add
+SUB = mybir.AluOpType.subtract
+
+P = 128
+PACK = 4
+COLS = 512
+HALF = COLS // 2
+TILES = N // P
+BANKS = 8
+RUN = 4
+
+SUMS = {
+    "pr": ("rr",),
+    "mr": ("ii", "jj", "kk"),
+    "pi": ("ir", "ri", "jk"),
+    "mi": ("kj",),
+    "pj": ("jr", "ki", "rj"),
+    "mj": ("ik",),
+    "pk": ("kr", "ij", "rk"),
+    "mk": ("ji",),
+}
+PARTS = "rijk"
+
+
+def tile_mix_quat_bias_kernel(
+    tc, xr, xi, xj, xk,
+    wr_words, wr_scales, wi_words, wi_scales, wj_words, wj_scales, wk_words, wk_scales,
+    br, bi, bj, bk, out_0, out_1, out_2, out_3,
+):
+    nc = tc.nc
+    x_hbm = {"r": xr, "i": xi, "j": xj, "k": xk}
+    words_hbm = {
+        "r": wr_words[0].rearrange("p n t -> p (n t)"),
+        "i": wi_words[0].rearrange("p n t -> p (n t)"),
+        "j": wj_words[0],
+        "k": wk_words[0],
+    }
+    scales_hbm = {"r": wr_scales[0], "i": wi_scales[0], "j": wj_scales[0], "k": wk_scales[0]}
+    bias_hbm = {"r": br, "i": bi, "j": bj, "k": bk}
+    out_hbm = {"r": out_0, "i": out_1, "j": out_2, "k": out_3}
+    word_bytes = {"r": 4, "i": 4, "j": 2, "k": 2}
+    word_dtype = {"r": FP8X4, "i": FP8X4, "j": FP4X4, "k": FP4X4}
+
+    with ExitStack() as ctx:
+        sb = ctx.enter_context(tc.tile_pool(name="sb", bufs=1))
+        ps = ctx.enter_context(tc.psum_pool(name="ps", bufs=1))
+        ctx.enter_context(tc.manual_schedule())
+
+        w_words = {w: sb.tile([P, N * word_bytes[w]], U8, name="words_" + w, align_bytes=64) for w in PARTS}
+        w_scales = {w: sb.tile([P, N], U8, name="scales_" + w, align_bytes=64) for w in PARTS}
+        bias_rows = sb.tile([P, P], F32, name="bias_rows")
+        bias_cols = sb.tile([P, 4 * TILES], F32, name="bias_cols")
+        ident = sb.tile([P, P], F32, name="ident")
+        raw = {}
+        grouped = {}
+        x_codes = {}
+        x_scales = {}
+        for h in range(T // COLS):
+            for x in PARTS:
+                grouped[x, h] = sb.tile([P, COLS * PACK], BF16, name="grouped_%s%d" % (x, h), align_bytes=64)
+                x_codes[x, h] = sb.tile([P, COLS], U32, name="codes_%s%d" % (x, h), align_bytes=64)
+                x_scales[x, h] = sb.tile([P, COLS], U8, name="xscales_%s%d" % (x, h), align_bytes=64)
+
+        def load_x(x, h, c0, c1):
+            t = sb.tile([P, PACK, c1 - c0], F32, name="raw_%s%d_%d" % (x, h, c0))
+            src = x_hbm[x].rearrange("(p j) t -> p j t", j=PACK)[:, :, h * COLS + c0 : h * COLS + c1]
+            nc.sync.dma_start(out=t[:], in_=src)
+            raw.setdefault((x, h), []).append((c0, c1, t))
+
+        def load_words(w):
+            nc.sync.dma_start(out=w_words[w][:].bitcast(I32), in_=words_hbm[w].bitcast(I32))
+
+        def load_scales(w, queue):
+            for q in range(4):
+                queue.dma_start(
+                    out=w_scales[w][32 * q : 32 * q + 4, :].bitcast(I32),
+                    in_=scales_hbm[w][4 * q : 4 * q + 4, :].bitcast(I32),
+                )
+
+        def cast(x, h, c0, c1, on_scalar):
+            s0, s1, t = [piece for piece in raw[x, h] if piece[0] <= c0 and c1 <= piece[1]][0]
+            src = t[:, :, c0 - s0 : c1 - s0].rearrange("p j (c i) -> p c j i", i=RUN)
+            dst = grouped[x, h][:, c0 * PACK : c1 * PACK].rearrange("p (c i j) -> p c j i", i=RUN, j=PACK)
+            if on_scalar:
+                nc.scalar.copy(out=dst, in_=src)
+            else:
+                nc.vector.tensor_copy(out=dst, in_=src)
+
+        def quantize(x, h, c0, c1):
+            nc.vector.quantize_mx(
+                out=x_codes[x, h][:, c0:c1].bitcast(FP8X4),
+                scales=x_scales[x, h][:, c0:c1],
+                in_=grouped[x, h][:, c0 * PACK : c1 * PACK],
+            )
+
+        free_banks = list(range(BANKS))
+        open_sums = {}
+        parked = {}
+
+        def take_bank(shape):
+            bank = free_banks[0]
+            free_banks.remove(bank)
+            return bank, ps.tile(shape, F32, name="bank%d" % bank)
+
+        def product(name, n, h, term, c0=0, c1=COLS):
+            w, x = SUMS[name][term]
+            first = (name, n, h) not in open_sums
+            if first:
+                open_sums[name, n, h] = take_bank([P, COLS])
+            acc = open_sums[name, n, h][1]
+            wb = word_bytes[w]
+            nc.tensor.matmul_mx(
+                out=acc[:, c0:c1],
+                lhsT=w_words[w][:, n * P * wb : (n + 1) * P * wb].bitcast(word_dtype[w]),
+                lhsT_scale=w_scales[w][:, n * P : (n + 1) * P],
+                rhs=x_codes[x, h][:, c0:c1].bitcast(FP8X4),
+                rhs_scale=x_scales[x, h][:, c0:c1],
+                start=first,
+                stop=(term == len(SUMS[name]) - 1 and c1 == COLS),
+            )
+
+        def drain(name, n, h):
+            o = name[1]
+            bank, acc = open_sums[name, n, h]
+            if (o, n, h) not in parked:
+                parked[o, n, h] = sb.tile([P, COLS], F32, name="parked_%s%d%d" % (o, n, h))
+                nc.scalar.copy(out=parked[o, n, h][:], in_=acc[:])
+            else:
+                other = parked[o, n, h]
+                plus, minus = (acc, other) if name[0] == "p" else (other, acc)
+                col = PARTS.index(o) * TILES + n
+                nc.vector.scalar_tensor_tensor(
+                    out=other[:], in0=plus[:], scalar=bias_cols[:, col : col + 1], in1=minus[:], op0=ADD, op1=SUB
+                )
+                nc.sync.dma_start(out=out_hbm[o][n * P : (n + 1) * P, h * COLS : (h + 1) * COLS], in_=other[:])
+            free_banks.append(bank)
+
+        def finish(name, n, h, first_term=0):
+            for term in range(first_term, len(SUMS[name])):
+                product(name, n, h, term)
+            drain(name, n, h)
+
+        nc.vector.memset(bias_rows[:], 0.0)
+        for w in PARTS:
+            nc.vector.memset(w_scales[w][:].bitcast(I32), 0)
+        for o in PARTS:
+            row = PARTS.index(o) * TILES
+            nc.gpsimd.dma_start(out=bias_rows[row : row + TILES, :], in_=bias_hbm[o].rearrange("(c p) -> c p", p=P))
+        make_identity(nc, ident[:])
+        load_scales("i", nc.gpsimd)
+        load_scales("k", nc.gpsimd)
+
+        load_x("r", 0, 0, COLS)
+        load_scales("r", nc.sync)
+        load_words("r")
+        load_words("i")
+        load_x("i", 0, 0, COLS)
+        load_words("j")
+        load_scales("j", nc.sync)
+        load_words("k")
+        load_x("j", 0, 0, COLS)
+        load_x("k", 0, 0, COLS)
+        for x in PARTS:
+            load_x(x, 1, 0, COLS)
+
+        def prepare(x, h, split):
+            cast(x, h, 0, HALF, False)
+            cast(x, h, HALF, split, False)
+            if split < COLS:
+                cast(x, h, split, COLS, True)
+            quantize(x, h, 0, HALF)
+            quantize(x, h, HALF, COLS)
+
+        prepare("r", 0, 352)
+        bank, bias_t = take_bank([P, P])
+        nc.tensor.transpose(bias_t[:], bias_rows[:], ident[:])
+        nc.scalar.copy(out=bias_cols[:], in_=bias_t[:, 0 : 4 * TILES])
+        free_banks.append(bank)
+        for n in range(TILES):
+            product("pr", n, 0, 0)
+        for n in range(TILES):
+            product("pi", n, 0, 0)
+        for n in range(2):
+            drain("pr", n, 0)
+            product("pj", n, 0, 0)
+        prepare("i", 0, 352)
+        for n in range(2, TILES):
+            drain("pr", n, 0)
+
+        for pair in range(2):
+            product("pi", 2 * pair, 0, 1)
+            finish("mk", 2 * pair, 0)
+            finish("mk", 2 * pair + 1, 0)
+            product("pi", 2 * pair + 1, 0, 1)
+            product("pj", pair, 0, 1)
+        for n in range(2, TILES):
+            product("pj", n, 0, 0)
+            product("pj", n, 0, 1)
+
+        prepare("j", 0, COLS)
+        for n in range(TILES):
+            finish("pj", n, 0, 2)
+        prepare("k", 0, COLS)
+        for n in range(TILES):
+            finish("mi", n, 0)
+            for quarter in range(3 * n, 3 * n + 3):
+                c0 = P * (quarter % 4)
+                cast(PARTS[quarter // 4], 1, c0, c0 + P, True)
+            finish("mr", n, 0)
+            finish("pi", n, 0, 2)
+            finish("mj", n, 0)
+            finish("pk", n, 0)
+            if n > 0:
+                quantize(PARTS[n - 1], 1, 0, COLS)
+
+        for n in range(2):
+            finish("pr", n, 1)
+        for name in ("pi", "pj"):
+            for n in range(2):
+                product(name, n, 1, 0)
+        prepare("k", 1, COLS)
+        for n in range(2):
+            finish("mk", n, 1)
+            product("pi", n, 1, 1)
+            product("pj", n, 1, 1)
+        for n in range(2):
+            product("pk", n, 1, 0)
+        for n in range(2):
+            finish("pj", n, 1, 2)
+            product("pk", n, 1, 1)
+        for n in range(2):
+            finish("mi", n, 1)
+            finish("mr", n, 1)
+            finish("pi", n, 1, 2)
+            finish("mj", n, 1)
+            finish("pk", n, 1, 2)
+        for n in range(2, TILES):
+            for lone, triple in (("pr", "mr"), ("mi", "pi"), ("mj", "pj"), ("mk", "pk")):
+                finish(lone, n, 1)
+                finish(triple, n, 1)

@@ -62,7 +62,9 @@ def tile_mix_quat_bias_kernel(
         ctx.enter_context(tc.manual_schedule())
 
         w_words = {w: sb.tile([P, N * word_bytes[w]], U8, name="words_" + w, align_bytes=64) for w in PARTS}
-        w_scales = {w: sb.tile([P, N], U8, name="scales_" + w, align_bytes=64) for w in PARTS}
+        planes = sb.tile([P, 4 * N], U8, name="planes", align_bytes=64)
+        w_scales = {w: planes[:, PARTS.index(w) * N : (PARTS.index(w) + 1) * N] for w in PARTS}
+        scale_rows = sb.tile([4, 4 * 4 * N], U8, name="scale_rows", align_bytes=64)
         bias_rows = sb.tile([P, P], F32, name="bias_rows")
         bias_cols = sb.tile([P, 4 * TILES], F32, name="bias_cols")
         ident = sb.tile([P, P], F32, name="ident")
@@ -85,12 +87,9 @@ def tile_mix_quat_bias_kernel(
         def load_words(w):
             nc.sync.dma_start(out=w_words[w][:].bitcast(I32), in_=words_hbm[w].bitcast(I32))
 
-        def load_scales(w, queue):
-            for q in range(4):
-                queue.dma_start(
-                    out=w_scales[w][32 * q : 32 * q + 4, :].bitcast(I32),
-                    in_=scales_hbm[w][4 * q : 4 * q + 4, :].bitcast(I32),
-                )
+        def load_scales(w):
+            dst = scale_rows[:].bitcast(I32).rearrange("r (q w n) -> r q w n", q=4, w=4)[:, :, PARTS.index(w), :]
+            nc.sync.dma_start(out=dst, in_=scales_hbm[w].bitcast(I32).rearrange("(q r) n -> r q n", r=4))
 
         def cast(x, h, c0, c1, on_scalar):
             s0, s1, t = [piece for piece in raw[x, h] if piece[0] <= c0 and c1 <= piece[1]][0]
@@ -156,22 +155,23 @@ def tile_mix_quat_bias_kernel(
             drain(name, n, h)
 
         nc.vector.memset(bias_rows[:], 0.0)
-        for w in PARTS:
-            nc.vector.memset(w_scales[w][:].bitcast(I32), 0)
-        for o in PARTS:
-            row = PARTS.index(o) * TILES
-            nc.gpsimd.dma_start(out=bias_rows[row : row + TILES, :], in_=bias_hbm[o].rearrange("(c p) -> c p", p=P))
+        nc.vector.memset(planes[:].bitcast(I32), 0)
         make_identity(nc, ident[:])
-        load_scales("i", nc.gpsimd)
-        load_scales("k", nc.gpsimd)
-
+        for w in PARTS:
+            load_scales(w)
         load_x("r", 0, 0, COLS)
-        load_scales("r", nc.sync)
+        for q in range(4):
+            nc.sync.dma_start(
+                out=planes[32 * q : 32 * q + 4, :].bitcast(I32),
+                in_=scale_rows[:, q * 4 * N : (q + 1) * 4 * N].bitcast(I32),
+            )
         load_words("r")
         load_words("i")
         load_x("i", 0, 0, COLS)
         load_words("j")
-        load_scales("j", nc.sync)
+        for o in PARTS:
+            row = PARTS.index(o) * TILES
+            nc.sync.dma_start(out=bias_rows[row : row + TILES, :], in_=bias_hbm[o].rearrange("(c p) -> c p", p=P))
         load_words("k")
         load_x("j", 0, 0, COLS)
         load_x("k", 0, 0, COLS)
@@ -187,10 +187,6 @@ def tile_mix_quat_bias_kernel(
             quantize(x, h, HALF, COLS)
 
         prepare("r", 0, 352)
-        bank, bias_t = take_bank([P, P])
-        nc.tensor.transpose(bias_t[:], bias_rows[:], ident[:])
-        nc.scalar.copy(out=bias_cols[:], in_=bias_t[:, 0 : 4 * TILES])
-        free_banks.append(bank)
         for n in range(TILES):
             product("pr", n, 0, 0)
         for n in range(TILES):
@@ -202,6 +198,10 @@ def tile_mix_quat_bias_kernel(
         for n in range(2, TILES):
             drain("pr", n, 0)
 
+        bank, bias_t = take_bank([P, P])
+        nc.tensor.transpose(bias_t[:], bias_rows[:], ident[:])
+        nc.scalar.copy(out=bias_cols[:], in_=bias_t[:, 0 : 4 * TILES])
+        free_banks.append(bank)
         for pair in range(2):
             product("pi", 2 * pair, 0, 1)
             finish("mk", 2 * pair, 0)

@@ -64,7 +64,7 @@ def tile_mix_quat_bias_kernel(
         w_words = {w: sb.tile([P, N * word_bytes[w]], U8, name="words_" + w, align_bytes=64) for w in PARTS}
         planes = sb.tile([P, 4 * N], U8, name="planes", align_bytes=64)
         w_scales = {w: planes[:, PARTS.index(w) * N : (PARTS.index(w) + 1) * N] for w in PARTS}
-        scale_rows = sb.tile([4, 4 * 4 * N], U8, name="scale_rows", align_bytes=64)
+        scale_rows = sb.tile([P, 4 * N], U8, name="scale_rows", align_bytes=64)
         bias_rows = sb.tile([P, P], F32, name="bias_rows")
         bias_cols = sb.tile([P, 4 * TILES], F32, name="bias_cols")
         ident = sb.tile([P, P], F32, name="ident")
@@ -88,8 +88,10 @@ def tile_mix_quat_bias_kernel(
             nc.sync.dma_start(out=w_words[w][:].bitcast(I32), in_=words_hbm[w].bitcast(I32))
 
         def load_scales(w):
-            dst = scale_rows[:].bitcast(I32).rearrange("r (q w n) -> r q w n", q=4, w=4)[:, :, PARTS.index(w), :]
-            nc.sync.dma_start(out=dst, in_=scales_hbm[w].bitcast(I32).rearrange("(q r) n -> r q n", r=4))
+            c0 = PARTS.index(w) * N
+            nc.sync.dma_start(
+                out=scale_rows[4:P:8, c0 : c0 + N].bitcast(I32), in_=scales_hbm[w].bitcast(I32)
+            )
 
         def cast(x, h, c0, c1, on_scalar):
             s0, s1, t = [piece for piece in raw[x, h] if piece[0] <= c0 and c1 <= piece[1]][0]
@@ -133,7 +135,7 @@ def tile_mix_quat_bias_kernel(
                 stop=(term == len(SUMS[name]) - 1 and c1 == COLS),
             )
 
-        def drain(name, n, h):
+        def drain(name, n, h, pieces=1):
             o = name[1]
             bank, acc = open_sums[name, n, h]
             if (o, n, h) not in parked:
@@ -143,16 +145,21 @@ def tile_mix_quat_bias_kernel(
                 other = parked[o, n, h]
                 plus, minus = (acc, other) if name[0] == "p" else (other, acc)
                 col = PARTS.index(o) * TILES + n
-                nc.vector.scalar_tensor_tensor(
-                    out=other[:], in0=plus[:], scalar=bias_cols[:, col : col + 1], in1=minus[:], op0=ADD, op1=SUB
-                )
-                nc.sync.dma_start(out=out_hbm[o][n * P : (n + 1) * P, h * COLS : (h + 1) * COLS], in_=other[:])
+                width = COLS // pieces
+                for c0 in range(0, COLS, width):
+                    cols = slice(c0, c0 + width)
+                    nc.vector.scalar_tensor_tensor(
+                        out=other[:, cols], in0=plus[:, cols], scalar=bias_cols[:, col : col + 1],
+                        in1=minus[:, cols], op0=ADD, op1=SUB,
+                    )
+                    t0 = h * COLS + c0
+                    nc.sync.dma_start(out=out_hbm[o][n * P : (n + 1) * P, t0 : t0 + width], in_=other[:, cols])
             free_banks.append(bank)
 
-        def finish(name, n, h, first_term=0):
+        def finish(name, n, h, first_term=0, pieces=1):
             for term in range(first_term, len(SUMS[name])):
                 product(name, n, h, term)
-            drain(name, n, h)
+            drain(name, n, h, pieces)
 
         nc.vector.memset(bias_rows[:], 0.0)
         nc.vector.memset(planes[:].bitcast(I32), 0)
@@ -160,12 +167,12 @@ def tile_mix_quat_bias_kernel(
         for w in PARTS:
             load_scales(w)
         load_x("r", 0, 0, COLS)
+        load_words("r")
         for q in range(4):
             nc.sync.dma_start(
                 out=planes[32 * q : 32 * q + 4, :].bitcast(I32),
-                in_=scale_rows[:, q * 4 * N : (q + 1) * 4 * N].bitcast(I32),
+                in_=scale_rows[32 * q + 4 : 32 * q + 32 : 8, :].bitcast(I32),
             )
-        load_words("r")
         load_words("i")
         load_x("i", 0, 0, COLS)
         load_words("j")
@@ -202,29 +209,29 @@ def tile_mix_quat_bias_kernel(
         nc.tensor.transpose(bias_t[:], bias_rows[:], ident[:])
         nc.scalar.copy(out=bias_cols[:], in_=bias_t[:, 0 : 4 * TILES])
         free_banks.append(bank)
-        for pair in range(2):
-            product("pi", 2 * pair, 0, 1)
-            finish("mk", 2 * pair, 0)
-            finish("mk", 2 * pair + 1, 0)
-            product("pi", 2 * pair + 1, 0, 1)
-            product("pj", pair, 0, 1)
-        for n in range(2, TILES):
-            product("pj", n, 0, 0)
+        for n in range(TILES):
+            product("pi", n, 0, 1)
+            finish("mk", n, 0)
+        for n in range(2):
             product("pj", n, 0, 1)
+        product("pj", 2, 0, 0)
+        product("pj", 2, 0, 1)
 
         prepare("j", 0, COLS)
-        for n in range(TILES):
+        for n in range(3):
             finish("pj", n, 0, 2)
         prepare("k", 0, COLS)
         for n in range(TILES):
             finish("mi", n, 0)
+            if n == 0:
+                finish("pj", 3, 0)
             for quarter in range(3 * n, 3 * n + 3):
                 c0 = P * (quarter % 4)
                 cast(PARTS[quarter // 4], 1, c0, c0 + P, True)
             finish("mr", n, 0)
-            finish("pi", n, 0, 2)
             finish("mj", n, 0)
             finish("pk", n, 0)
+            finish("pi", n, 0, 2)
             if n > 0:
                 quantize(PARTS[n - 1], 1, 0, COLS)
 
@@ -252,4 +259,4 @@ def tile_mix_quat_bias_kernel(
         for n in range(2, TILES):
             for lone, triple in (("pr", "mr"), ("mi", "pi"), ("mj", "pj"), ("mk", "pk")):
                 finish(lone, n, 1)
-                finish(triple, n, 1)
+                finish(triple, n, 1, 0, 2 if (n, triple) == (TILES - 1, "pk") else 1)

@@ -22,7 +22,6 @@ COLS = 512
 HALF = COLS // 2
 TILES = N // P
 BANKS = 8
-RUN = 4
 
 SUMS = {
     "pr": ("rr",),
@@ -95,8 +94,8 @@ def tile_mix_quat_bias_kernel(
 
         def cast(x, h, c0, c1, on_scalar):
             s0, s1, t = [piece for piece in raw[x, h] if piece[0] <= c0 and c1 <= piece[1]][0]
-            src = t[:, :, c0 - s0 : c1 - s0].rearrange("p j (c i) -> p c j i", i=RUN)
-            dst = grouped[x, h][:, c0 * PACK : c1 * PACK].rearrange("p (c i j) -> p c j i", i=RUN, j=PACK)
+            src = t[:, :, c0 - s0 : c1 - s0].rearrange("p j c -> p c j")
+            dst = grouped[x, h][:, c0 * PACK : c1 * PACK].rearrange("p (c j) -> p c j", j=PACK)
             if on_scalar:
                 nc.scalar.copy(out=dst, in_=src)
             else:

@@ -19,9 +19,16 @@ SUB = mybir.AluOpType.subtract
 P = 128
 PACK = 4
 COLS = 512
-HALF = COLS // 2
+MID = COLS // 2
 TILES = N // P
 BANKS = 8
+QUADS = 4
+ALIGN = 64
+PARTS = "rijk"
+
+VECTOR_COLS = 384
+QUARTERS = 3
+EARLY_TILES = 2
 
 SUMS = {
     "pr": ("rr",),
@@ -33,7 +40,6 @@ SUMS = {
     "pk": ("kr", "ij", "rk"),
     "mk": ("ji",),
 }
-PARTS = "rijk"
 
 
 def tile_mix_quat_bias_kernel(
@@ -60,12 +66,12 @@ def tile_mix_quat_bias_kernel(
         ps = ctx.enter_context(tc.psum_pool(name="ps", bufs=1))
         ctx.enter_context(tc.manual_schedule())
 
-        w_words = {w: sb.tile([P, N * word_bytes[w]], U8, name="words_" + w, align_bytes=64) for w in PARTS}
-        planes = sb.tile([P, 4 * N], U8, name="planes", align_bytes=64)
+        w_words = {w: sb.tile([P, N * word_bytes[w]], U8, name="words_" + w, align_bytes=ALIGN) for w in PARTS}
+        planes = sb.tile([P, len(PARTS) * N], U8, name="planes", align_bytes=ALIGN)
         w_scales = {w: planes[:, PARTS.index(w) * N : (PARTS.index(w) + 1) * N] for w in PARTS}
-        scale_rows = sb.tile([P, 4 * N], U8, name="scale_rows", align_bytes=64)
+        scale_rows = sb.tile([P, len(PARTS) * N], U8, name="scale_rows", align_bytes=ALIGN)
         bias_rows = sb.tile([P, P], F32, name="bias_rows")
-        bias_cols = sb.tile([P, 4 * TILES], F32, name="bias_cols")
+        bias_cols = sb.tile([P, len(PARTS) * TILES], F32, name="bias_cols")
         ident = sb.tile([P, P], F32, name="ident")
         raw = {}
         grouped = {}
@@ -73,29 +79,33 @@ def tile_mix_quat_bias_kernel(
         x_scales = {}
         for h in range(T // COLS):
             for x in PARTS:
-                grouped[x, h] = sb.tile([P, COLS * PACK], BF16, name="grouped_%s%d" % (x, h), align_bytes=64)
-                x_codes[x, h] = sb.tile([P, COLS], U32, name="codes_%s%d" % (x, h), align_bytes=64)
-                x_scales[x, h] = sb.tile([P, COLS], U8, name="xscales_%s%d" % (x, h), align_bytes=64)
+                grouped[x, h] = sb.tile([P, COLS * PACK], BF16, name="grouped_%s%d" % (x, h), align_bytes=ALIGN)
+                x_codes[x, h] = sb.tile([P, COLS], U32, name="codes_%s%d" % (x, h), align_bytes=ALIGN)
+                x_scales[x, h] = sb.tile([P, COLS], U8, name="xscales_%s%d" % (x, h), align_bytes=ALIGN)
 
-        def load_x(x, h, c0, c1):
-            t = sb.tile([P, PACK, c1 - c0], F32, name="raw_%s%d_%d" % (x, h, c0))
-            src = x_hbm[x].rearrange("(p j) t -> p j t", j=PACK)[:, :, h * COLS + c0 : h * COLS + c1]
-            nc.sync.dma_start(out=t[:], in_=src)
-            raw.setdefault((x, h), []).append((c0, c1, t))
+        def load_x(x, h):
+            raw[x, h] = sb.tile([P, PACK, COLS], F32, name="raw_%s%d" % (x, h))
+            src = x_hbm[x].rearrange("(p j) t -> p j t", j=PACK)[:, :, h * COLS : (h + 1) * COLS]
+            nc.sync.dma_start(out=raw[x, h][:], in_=src)
 
         def load_words(w):
             nc.sync.dma_start(out=w_words[w][:].bitcast(I32), in_=words_hbm[w].bitcast(I32))
 
-        def load_scales(w):
+        def stage_scales(w):
             c0 = PARTS.index(w) * N
             nc.sync.dma_start(
                 out=scale_rows[4:P:8, c0 : c0 + N].bitcast(I32), in_=scales_hbm[w].bitcast(I32)
             )
 
+        def place_scales(q):
+            nc.sync.dma_start(
+                out=planes[32 * q : 32 * q + 4, :].bitcast(I32),
+                in_=scale_rows[32 * q + 4 : 32 * q + 32 : 8, :].bitcast(I32),
+            )
+
         def cast(x, h, c0, c1, on_scalar):
-            s0, s1, t = [piece for piece in raw[x, h] if piece[0] <= c0 and c1 <= piece[1]][0]
-            src = t[:, :, c0 - s0 : c1 - s0].rearrange("p j c -> p c j")
-            dst = grouped[x, h][:, c0 * PACK : c1 * PACK].rearrange("p (c j) -> p c j", j=PACK)
+            src = raw[x, h][:, :, c0:c1].rearrange("p j (c i) -> p c j i", i=4)
+            dst = grouped[x, h][:, c0 * PACK : c1 * PACK].rearrange("p (c i j) -> p c j i", i=4, j=PACK)
             if on_scalar:
                 nc.scalar.copy(out=dst, in_=src)
             else:
@@ -107,6 +117,14 @@ def tile_mix_quat_bias_kernel(
                 scales=x_scales[x, h][:, c0:c1],
                 in_=grouped[x, h][:, c0 * PACK : c1 * PACK],
             )
+
+        def prepare(x, h, vector_cols):
+            cast(x, h, 0, MID, False)
+            cast(x, h, MID, vector_cols, False)
+            if vector_cols < COLS:
+                cast(x, h, vector_cols, COLS, True)
+            quantize(x, h, 0, MID)
+            quantize(x, h, MID, COLS)
 
         free_banks = list(range(BANKS))
         open_sums = {}
@@ -134,12 +152,15 @@ def tile_mix_quat_bias_kernel(
                 stop=(term == len(SUMS[name]) - 1 and c1 == COLS),
             )
 
-        def drain(name, n, h, pieces=1):
+        def drain(name, n, h, pieces=1, park_on_vector=False):
             o = name[1]
             bank, acc = open_sums[name, n, h]
             if (o, n, h) not in parked:
                 parked[o, n, h] = sb.tile([P, COLS], F32, name="parked_%s%d%d" % (o, n, h))
-                nc.scalar.copy(out=parked[o, n, h][:], in_=acc[:])
+                if park_on_vector:
+                    nc.vector.tensor_copy(out=parked[o, n, h][:], in_=acc[:])
+                else:
+                    nc.scalar.copy(out=parked[o, n, h][:], in_=acc[:])
             else:
                 other = parked[o, n, h]
                 plus, minus = (acc, other) if name[0] == "p" else (other, acc)
@@ -164,67 +185,61 @@ def tile_mix_quat_bias_kernel(
         nc.vector.memset(planes[:].bitcast(I32), 0)
         make_identity(nc, ident[:])
         for w in PARTS:
-            load_scales(w)
-        load_x("r", 0, 0, COLS)
+            stage_scales(w)
+        load_x("r", 0)
         load_words("r")
-        for q in range(4):
-            nc.sync.dma_start(
-                out=planes[32 * q : 32 * q + 4, :].bitcast(I32),
-                in_=scale_rows[32 * q + 4 : 32 * q + 32 : 8, :].bitcast(I32),
-            )
+        for q in range(QUADS):
+            place_scales(q)
         load_words("i")
-        load_x("i", 0, 0, COLS)
+        load_x("i", 0)
         load_words("j")
         for o in PARTS:
             row = PARTS.index(o) * TILES
             nc.sync.dma_start(out=bias_rows[row : row + TILES, :], in_=bias_hbm[o].rearrange("(c p) -> c p", p=P))
+        load_x("j", 0)
         load_words("k")
-        load_x("j", 0, 0, COLS)
-        load_x("k", 0, 0, COLS)
+        load_x("k", 0)
         for x in PARTS:
-            load_x(x, 1, 0, COLS)
+            load_x(x, 1)
 
-        def prepare(x, h, split):
-            cast(x, h, 0, HALF, False)
-            cast(x, h, HALF, split, False)
-            if split < COLS:
-                cast(x, h, split, COLS, True)
-            quantize(x, h, 0, HALF)
-            quantize(x, h, HALF, COLS)
-
-        prepare("r", 0, 352)
-        for n in range(TILES):
+        prepare("r", 0, VECTOR_COLS)
+        for c0 in (0, MID):
+            for n in range(2):
+                product("pr", n, 0, 0, c0, c0 + MID)
+        for n in range(2, TILES):
             product("pr", n, 0, 0)
         for n in range(TILES):
             product("pi", n, 0, 0)
         for n in range(2):
-            drain("pr", n, 0)
+            drain("pr", n, 0, park_on_vector=(n == 1))
             product("pj", n, 0, 0)
-        prepare("i", 0, 352)
-        for n in range(2, TILES):
-            drain("pr", n, 0)
+        drain("pr", 2, 0)
+        prepare("i", 0, VECTOR_COLS)
+        drain("pr", 3, 0)
 
         bank, bias_t = take_bank([P, P])
         nc.tensor.transpose(bias_t[:], bias_rows[:], ident[:])
-        nc.scalar.copy(out=bias_cols[:], in_=bias_t[:, 0 : 4 * TILES])
+        nc.scalar.copy(out=bias_cols[:], in_=bias_t[:, 0 : len(PARTS) * TILES])
         free_banks.append(bank)
-        for n in range(TILES):
-            product("pi", n, 0, 1)
-            finish("mk", n, 0)
-        for n in range(2):
-            product("pj", n, 0, 1)
+
+        for pair in range(2):
+            finish("mk", 2 * pair, 0)
+            product("pi", 2 * pair, 0, 1)
+            finish("mk", 2 * pair + 1, 0)
+            product("pi", 2 * pair + 1, 0, 1)
+            product("pj", pair, 0, 1)
         product("pj", 2, 0, 0)
-        product("pj", 2, 0, 1)
 
         prepare("j", 0, COLS)
-        for n in range(3):
+        for n in range(2):
             finish("pj", n, 0, 2)
+        finish("pj", 2, 0, 1)
         prepare("k", 0, COLS)
         for n in range(TILES):
             finish("mi", n, 0)
             if n == 0:
-                finish("pj", 3, 0)
-            for quarter in range(3 * n, 3 * n + 3):
+                finish("pj", TILES - 1, 0)
+            for quarter in range(QUARTERS * n, QUARTERS * (n + 1)):
                 c0 = P * (quarter % 4)
                 cast(PARTS[quarter // 4], 1, c0, c0 + P, True)
             finish("mr", n, 0)
@@ -234,28 +249,27 @@ def tile_mix_quat_bias_kernel(
             if n > 0:
                 quantize(PARTS[n - 1], 1, 0, COLS)
 
-        for n in range(2):
+        for n in range(EARLY_TILES):
             finish("pr", n, 1)
-        for name in ("pi", "pj"):
-            for n in range(2):
-                product(name, n, 1, 0)
-        prepare("k", 1, COLS)
-        for n in range(2):
-            finish("mk", n, 1)
+            product("pi", n, 1, 0)
             product("pi", n, 1, 1)
+            finish("mk", n, 1)
+            product("pj", n, 1, 0)
             product("pj", n, 1, 1)
-        for n in range(2):
+        prepare("k", 1, COLS)
+        for n in range(EARLY_TILES):
             product("pk", n, 1, 0)
-        for n in range(2):
+        for n in range(EARLY_TILES):
             finish("pj", n, 1, 2)
             product("pk", n, 1, 1)
-        for n in range(2):
+        for n in range(EARLY_TILES):
             finish("mi", n, 1)
             finish("mr", n, 1)
             finish("pi", n, 1, 2)
             finish("mj", n, 1)
             finish("pk", n, 1, 2)
-        for n in range(2, TILES):
+        for n in range(EARLY_TILES, TILES):
             for lone, triple in (("pr", "mr"), ("mi", "pi"), ("mj", "pj"), ("mk", "pk")):
                 finish(lone, n, 1)
-                finish(triple, n, 1, 0, 2 if (n, triple) == (TILES - 1, "pk") else 1)
+                last = (n, triple) == (TILES - 1, "pk")
+                finish(triple, n, 1, 0, 2 if last else 1)

@@ -1,7 +1,6 @@
 from contextlib import ExitStack
 
 import concourse.mybir as mybir
-from concourse.masks import make_identity
 
 K, N, T = 512, 512, 1024
 FLOPS = 16 * 2 * K * N * T
@@ -18,27 +17,33 @@ SUB = mybir.AluOpType.subtract
 
 P = 128
 PACK = 4
-COLS = 512
-MID = COLS // 2
+BANK = 512
 TILES = N // P
 BANKS = 8
 QUADS = 4
 ALIGN = 64
 PARTS = "rijk"
-
-VECTOR_COLS = 384
-QUARTERS = 3
-EARLY_TILES = 2
+ARRIVAL = "rjki"
+CHUNKS = ((0, 256), (256, 256), (512, 512))
+UNMERGED = 16
 
 SUMS = {
     "pr": ("rr",),
-    "mr": ("ii", "jj", "kk"),
-    "pi": ("ir", "ri", "jk"),
+    "mr": ("jj", "kk", "ii"),
+    "pi": ("ir", "jk", "ri"),
     "mi": ("kj",),
-    "pj": ("jr", "ki", "rj"),
+    "pj": ("jr", "rj", "ki"),
     "mj": ("ik",),
     "pk": ("kr", "ij", "rk"),
     "mk": ("ji",),
+}
+HALF = BANK // 2
+NARROW = {
+    "pr": ((("pr", 0), ("pr", 1)), (("r", "r", 0, 0), ("r", "r", 1, 1))),
+    "mj": ((("mj", 0), ("mj", 1)), (("i", "k", 0, 0), ("i", "k", 1, 1))),
+    "pjmr": ((("pj", 0), ("mr", 0)), (("j", "rj", 0, 0), ("r", "j", 0, 0), ("k", "ik", 0, 0), ("i", "i", 1, 0))),
+    "pkmi": ((("pk", 0), ("mi", 0)), (("k", "rj", 0, 0), ("i", "j", 0, 0), ("r", "k", 0, 0))),
+    "mkpi": ((("mk", 0), ("pi", 0)), (("j", "ik", 0, 0), ("i", "r", 1, 0), ("r", "i", 1, 0))),
 }
 
 
@@ -70,22 +75,32 @@ def tile_mix_quat_bias_kernel(
         planes = sb.tile([P, len(PARTS) * N], U8, name="planes", align_bytes=ALIGN)
         w_scales = {w: planes[:, PARTS.index(w) * N : (PARTS.index(w) + 1) * N] for w in PARTS}
         scale_rows = sb.tile([P, len(PARTS) * N], U8, name="scale_rows", align_bytes=ALIGN)
-        bias_rows = sb.tile([P, P], F32, name="bias_rows")
-        bias_cols = sb.tile([P, len(PARTS) * TILES], F32, name="bias_cols")
-        ident = sb.tile([P, P], F32, name="ident")
+        bias_rows = sb.tile([P, P], F32, name="bias_rows", align_bytes=ALIGN)
+        bias_cols = sb.tile([P, P], F32, name="bias_cols", align_bytes=ALIGN)
         raw = {}
         grouped = {}
         x_codes = {}
         x_scales = {}
-        for h in range(T // COLS):
+        for h, (t0, width) in enumerate(CHUNKS):
             for x in PARTS:
-                grouped[x, h] = sb.tile([P, COLS * PACK], BF16, name="grouped_%s%d" % (x, h), align_bytes=ALIGN)
-                x_codes[x, h] = sb.tile([P, COLS], U32, name="codes_%s%d" % (x, h), align_bytes=ALIGN)
-                x_scales[x, h] = sb.tile([P, COLS], U8, name="xscales_%s%d" % (x, h), align_bytes=ALIGN)
+                grouped[x, h] = sb.tile([P, width * PACK], BF16, name="grouped_%s%d" % (x, h), align_bytes=ALIGN)
+            for pair in ("rj", "ik"):
+                codes = sb.tile([P, 2 * width], U32, name="codes_%s%d" % (pair, h), align_bytes=ALIGN)
+                scales = sb.tile([P, 2 * width], U8, name="xscales_%s%d" % (pair, h), align_bytes=ALIGN)
+                x_codes[pair, h] = codes[:]
+                x_scales[pair, h] = scales[:]
+                for side in range(2):
+                    x_codes[pair[side], h] = codes[:, side * width : (side + 1) * width]
+                    x_scales[pair[side], h] = scales[:, side * width : (side + 1) * width]
+        result = {}
+        for o in PARTS:
+            for n in range(TILES):
+                result[o, n] = sb.tile([P, T], F32, name="result_%s%d" % (o, n))
 
         def load_x(x, h):
-            raw[x, h] = sb.tile([P, PACK, COLS], F32, name="raw_%s%d" % (x, h))
-            src = x_hbm[x].rearrange("(p j) t -> p j t", j=PACK)[:, :, h * COLS : (h + 1) * COLS]
+            t0, width = CHUNKS[h]
+            raw[x, h] = sb.tile([P, PACK, width], F32, name="raw_%s%d" % (x, h))
+            src = x_hbm[x].rearrange("(p j) t -> p j t", j=PACK)[:, :, t0 : t0 + width]
             nc.sync.dma_start(out=raw[x, h][:], in_=src)
 
         def load_words(w):
@@ -103,6 +118,12 @@ def tile_mix_quat_bias_kernel(
                 in_=scale_rows[32 * q + 4 : 32 * q + 32 : 8, :].bitcast(I32),
             )
 
+        def load_bias(o):
+            nc.sync.dma_start(
+                out=bias_rows[PARTS.index(o) : P : 32, :].rearrange("a (n j) -> a n j", j=32),
+                in_=bias_hbm[o].rearrange("(n a j) -> a n j", a=QUADS, j=32),
+            )
+
         def cast(x, h, c0, c1, on_scalar):
             src = raw[x, h][:, :, c0:c1].rearrange("p j (c i) -> p c j i", i=4)
             dst = grouped[x, h][:, c0 * PACK : c1 * PACK].rearrange("p (c i j) -> p c j i", i=4, j=PACK)
@@ -111,165 +132,267 @@ def tile_mix_quat_bias_kernel(
             else:
                 nc.vector.tensor_copy(out=dst, in_=src)
 
-        def quantize(x, h, c0, c1):
+        def quantize(x, h, c0=0, c1=None):
+            c1 = CHUNKS[h][1] if c1 is None else c1
             nc.vector.quantize_mx(
                 out=x_codes[x, h][:, c0:c1].bitcast(FP8X4),
                 scales=x_scales[x, h][:, c0:c1],
                 in_=grouped[x, h][:, c0 * PACK : c1 * PACK],
             )
 
-        def prepare(x, h, vector_cols):
-            cast(x, h, 0, MID, False)
-            cast(x, h, MID, vector_cols, False)
-            if vector_cols < COLS:
-                cast(x, h, vector_cols, COLS, True)
-            quantize(x, h, 0, MID)
-            quantize(x, h, MID, COLS)
+        def share_cast(x, h, vector_cols):
+            width = CHUNKS[h][1]
+            if vector_cols < width:
+                cast(x, h, vector_cols, width, True)
+            if vector_cols > 0:
+                cast(x, h, 0, vector_cols, False)
 
         free_banks = list(range(BANKS))
         open_sums = {}
         parked = {}
+        terms_done = {}
 
-        def take_bank(shape):
-            bank = free_banks[0]
-            free_banks.remove(bank)
-            return bank, ps.tile(shape, F32, name="bank%d" % bank)
+        def tiles_of(unit, h):
+            per_bank = BANK // CHUNKS[h][1]
+            return range(unit * per_bank, (unit + 1) * per_bank)
 
-        def product(name, n, h, term, c0=0, c1=COLS):
+        def product(name, unit, h, term, cols=None, part=None):
             w, x = SUMS[name][term]
-            first = (name, n, h) not in open_sums
+            width = CHUNKS[h][1]
+            lo, hi = cols or (0, width)
+            p0, p1 = part or (lo, hi)
+            key = name, unit, h, lo
+            lone = len(SUMS[name]) == 1 and part is None
+            first = key not in open_sums
             if first:
-                open_sums[name, n, h] = take_bank([P, COLS])
-            acc = open_sums[name, n, h][1]
+                bank = free_banks[0]
+                free_banks.remove(bank)
+                open_sums[key] = bank, ps.tile([P, BANK], F32, name="bank%d" % bank)
+            acc = open_sums[key][1]
+            if p1 == hi:
+                terms_done[key] = terms_done.get(key, 0) + 1
+            closing = terms_done.get(key, 0) == len(SUMS[name])
             wb = word_bytes[w]
-            nc.tensor.matmul_mx(
-                out=acc[:, c0:c1],
-                lhsT=w_words[w][:, n * P * wb : (n + 1) * P * wb].bitcast(word_dtype[w]),
-                lhsT_scale=w_scales[w][:, n * P : (n + 1) * P],
-                rhs=x_codes[x, h][:, c0:c1].bitcast(FP8X4),
-                rhs_scale=x_scales[x, h][:, c0:c1],
-                start=first,
-                stop=(term == len(SUMS[name]) - 1 and c1 == COLS),
-            )
+            step = P if (wb == 2 and not lone and p1 - p0 < BANK) else p1 - p0
+            passes = [(n, c0) for n in tiles_of(unit, h) for c0 in range(p0, p1, step)]
+            for n, c0 in passes:
+                a0 = (n * width) % BANK + c0
+                nc.tensor.matmul_mx(
+                    out=acc[:, a0 : a0 + step],
+                    lhsT=w_words[w][:, n * P * wb : (n + 1) * P * wb].bitcast(word_dtype[w]),
+                    lhsT_scale=w_scales[w][:, n * P : (n + 1) * P],
+                    rhs=x_codes[x, h][:, c0 : c0 + step].bitcast(FP8X4),
+                    rhs_scale=x_scales[x, h][:, c0 : c0 + step],
+                    start=lone or (first and (n, c0) == passes[0]),
+                    stop=lone or (closing and (n, c0) == passes[-1]),
+                )
 
-        def drain(name, n, h, pieces=1, park_on_vector=False):
+        def store(o, n, c0, c1):
+            nc.sync.dma_start(out=out_hbm[o][n * P : (n + 1) * P, c0:c1], in_=result[o, n][:, c0:c1])
+
+        def drain(name, unit, h, cols=None, park_on_vector=False):
             o = name[1]
-            bank, acc = open_sums[name, n, h]
-            if (o, n, h) not in parked:
-                parked[o, n, h] = sb.tile([P, COLS], F32, name="parked_%s%d%d" % (o, n, h))
-                if park_on_vector:
-                    nc.vector.tensor_copy(out=parked[o, n, h][:], in_=acc[:])
+            t0, width = CHUNKS[h]
+            lo, hi = cols or (0, width)
+            bank, acc = open_sums[name, unit, h, lo]
+            if (o, unit, h) not in parked:
+                if width == BANK:
+                    parked[o, unit, h] = result[o, unit][:, t0 : t0 + width]
                 else:
-                    nc.scalar.copy(out=parked[o, n, h][:], in_=acc[:])
+                    spare = sb.tile([P, BANK], F32, name="parked_%s%d%d" % (o, unit, h))
+                    parked[o, unit, h] = spare[:]
+                if park_on_vector:
+                    nc.vector.tensor_copy(out=parked[o, unit, h], in_=acc[:])
+                else:
+                    nc.scalar.copy(out=parked[o, unit, h], in_=acc[:])
             else:
-                other = parked[o, n, h]
+                other = parked[o, unit, h]
                 plus, minus = (acc, other) if name[0] == "p" else (other, acc)
-                col = PARTS.index(o) * TILES + n
-                width = COLS // pieces
-                for c0 in range(0, COLS, width):
-                    cols = slice(c0, c0 + width)
+                for n in tiles_of(unit, h):
+                    col = 32 * n + PARTS.index(o)
+                    a0 = (n * width) % BANK
                     nc.vector.scalar_tensor_tensor(
-                        out=other[:, cols], in0=plus[:, cols], scalar=bias_cols[:, col : col + 1],
-                        in1=minus[:, cols], op0=ADD, op1=SUB,
+                        out=result[o, n][:, t0 + lo : t0 + hi], in0=plus[:, a0 + lo : a0 + hi],
+                        scalar=bias_cols[:, col : col + 1], in1=minus[:, a0 + lo : a0 + hi], op0=ADD, op1=SUB,
                     )
-                    t0 = h * COLS + c0
-                    nc.sync.dma_start(out=out_hbm[o][n * P : (n + 1) * P, t0 : t0 + width], in_=other[:, cols])
+                    if t0 >= T // 2:
+                        store(o, n, t0 + lo if (o, n) in early else 0, t0 + hi)
             free_banks.append(bank)
 
-        def finish(name, n, h, first_term=0, pieces=1):
+        def finish(name, unit, h, first_term=0, cols=None):
             for term in range(first_term, len(SUMS[name])):
-                product(name, n, h, term)
-            drain(name, n, h, pieces)
+                product(name, unit, h, term, cols)
+            drain(name, unit, h, cols)
 
-        nc.vector.memset(bias_rows[:], 0.0)
+        narrow = {}
+
+        def narrow_pass(kind, unit, h, step):
+            w, xs, side, tile_step = NARROW[kind][1][step]
+            if step == 0:
+                bank = free_banks[0]
+                free_banks.remove(bank)
+                narrow[kind, unit, h] = bank, ps.tile([P, BANK], F32, name="bank%d" % bank)
+            acc = narrow[kind, unit, h][1]
+            n = unit + tile_step
+            wb = word_bytes[w]
+            nc.tensor.matmul_mx(
+                out=acc[:, side * HALF : (side + len(xs)) * HALF],
+                lhsT=w_words[w][:, n * P * wb : (n + 1) * P * wb].bitcast(word_dtype[w]),
+                lhsT_scale=w_scales[w][:, n * P : (n + 1) * P],
+                rhs=x_codes[xs, h].bitcast(FP8X4),
+                rhs_scale=x_scales[xs, h],
+                start=step == 0,
+                stop=step == len(NARROW[kind][1]) - 1,
+            )
+
+        def narrow_drain(kind, unit, h, park_on_vector=False):
+            bank, acc = narrow[kind, unit, h]
+            t0 = CHUNKS[h][0]
+            sums = [(name, unit + tile_step) for name, tile_step in NARROW[kind][0]]
+            if (sums[0][0][1], sums[0][1], h) not in parked:
+                spare = sb.tile([P, BANK], F32, name="parked_%s%d%d" % (kind, unit, h))
+                if park_on_vector:
+                    nc.vector.tensor_copy(out=spare[:], in_=acc[:])
+                else:
+                    nc.scalar.copy(out=spare[:], in_=acc[:])
+                for side, (name, n) in enumerate(sums):
+                    parked[name[1], n, h] = spare[:, side * HALF : (side + 1) * HALF]
+            else:
+                for side, (name, n) in enumerate(sums):
+                    o = name[1]
+                    mine = acc[:, side * HALF : (side + 1) * HALF]
+                    plus, minus = (mine, parked[o, n, h]) if name[0] == "p" else (parked[o, n, h], mine)
+                    col = 32 * n + PARTS.index(o)
+                    nc.vector.scalar_tensor_tensor(
+                        out=result[o, n][:, t0 : t0 + HALF], in0=plus,
+                        scalar=bias_cols[:, col : col + 1], in1=minus, op0=ADD, op1=SUB,
+                    )
+                    if h == 1:
+                        store(o, n, 0, T // 2)
+            free_banks.append(bank)
+
+        def passes(kind, unit, h, first, last):
+            for step in range(first, last):
+                narrow_pass(kind, unit, h, step)
+            if last == len(NARROW[kind][1]):
+                narrow_drain(kind, unit, h)
+
+        def with_weight(w, names, n, h):
+            for name in names:
+                product(name, n, h, [term[0] for term in SUMS[name]].index(w))
+                if terms_done[name, n, h, 0] == len(SUMS[name]):
+                    drain(name, n, h)
+
+        def prepare(x, h, vector_cols):
+            if vector_cols < BANK:
+                cast(x, h, vector_cols, BANK, True)
+            cast(x, h, 0, 256, False)
+            cast(x, h, 256, vector_cols, False)
+            quantize(x, h, 0, 256)
+            quantize(x, h, 256, BANK)
+
+        early = [(o, n) for n in range(TILES) for o in PARTS][-UNMERGED:]
+
         nc.vector.memset(planes[:].bitcast(I32), 0)
-        make_identity(nc, ident[:])
+        nc.vector.memset(bias_rows[:], 0.0)
         for w in PARTS:
             stage_scales(w)
         load_x("r", 0)
         load_words("r")
         for q in range(QUADS):
             place_scales(q)
-        load_words("i")
-        load_x("i", 0)
-        load_words("j")
-        for o in PARTS:
-            row = PARTS.index(o) * TILES
-            nc.sync.dma_start(out=bias_rows[row : row + TILES, :], in_=bias_hbm[o].rearrange("(c p) -> c p", p=P))
         load_x("j", 0)
         load_words("k")
+        load_words("j")
+        load_words("i")
         load_x("k", 0)
-        for x in PARTS:
-            load_x(x, 1)
+        load_x("i", 0)
+        for o in PARTS:
+            load_bias(o)
+        for h in (1, 2):
+            for x in ARRIVAL:
+                load_x(x, h)
 
-        prepare("r", 0, VECTOR_COLS)
-        for c0 in (0, MID):
-            for n in range(2):
-                product("pr", n, 0, 0, c0, c0 + MID)
+        share_cast("r", 0, 160)
+        quantize("r", 0)
+        for n in (0, 2):
+            passes("pr", n, 0, 0, 1)
+            narrow_pass("pr", n, 0, 1)
+        share_cast("j", 0, 160)
+        quantize("j", 0)
+        for n in (0, 2):
+            narrow_drain("pr", n, 0)
+        for kind in ("pkmi", "pjmr"):
+            for n in range(TILES):
+                passes(kind, n, 0, 0, 1)
+        share_cast("k", 0, 160)
+        quantize("k", 0)
+        for kind in ("pjmr", "pkmi"):
+            for n in range(TILES):
+                passes(kind, n, 0, 1, 2)
+        share_cast("i", 0, 160)
+        quantize("i", 0)
+        for n in range(TILES):
+            passes("pkmi", n, 0, 2, 3)
+        share_cast("r", 1, 256)
+        nc.vector.transpose(bias_cols[:], bias_rows[:])
+        quantize("r", 1)
+        for n in range(TILES):
+            passes("pjmr", n, 0, 2, 3)
+        for n in (0, 2):
+            passes("mj", n, 0, 0, 2)
+        share_cast("j", 1, 256)
+        quantize("j", 1)
+        share_cast("k", 1, 0)
+        share_cast("i", 1, 0)
+        for n in range(TILES):
+            passes("pjmr", n, 0, 3, 4)
+            passes("mkpi", n, 0, 0, 3)
+            if n in (1, 2):
+                quantize("ki"[n - 1], 1)
+
+        for n in range(TILES):
+            passes("pkmi", n, 1, 0, 2)
+        for n in range(TILES):
+            passes("pkmi", n, 1, 2, 3)
+        for n in (0, 2):
+            share_cast("rj"[n // 2], 2, 512)
+            passes("pr", n, 1, 0, 2)
+            passes("mj", n, 1, 0, 2)
+            passes("mkpi", n, 1, 0, 3)
+            quantize("rj"[n // 2], 2)
+            if n == 2:
+                share_cast("k", 2, 0)
+            passes("mkpi", n + 1, 1, 0, 3)
+            passes("pjmr", n, 1, 0, 4)
+            passes("pjmr", n + 1, 1, 0, 4)
+
+        for n in range(2):
+            finish("pr", n, 2)
+            product("pk", n, 2, 0)
+            product("pj", n, 2, 0)
+        quantize("k", 2)
+        for n in range(2):
+            product("pk", n, 2, 1)
+            finish("mi", n, 2)
+            product("pj", n, 2, 1)
+        prepare("i", 2, BANK)
+        for n in range(2):
+            product("pi", n, 2, 0)
+        for n in range(2):
+            finish("pk", n, 2, 2)
+            product("pi", n, 2, 1)
+        for n in range(2):
+            finish("mj", n, 2)
+            finish("mr", n, 2)
+            finish("pj", n, 2, 2)
+            finish("mk", n, 2)
+            finish("pi", n, 2, 2)
         for n in range(2, TILES):
-            product("pr", n, 0, 0)
-        for n in range(TILES):
-            product("pi", n, 0, 0)
-        for n in range(2):
-            drain("pr", n, 0, park_on_vector=(n == 1))
-            product("pj", n, 0, 0)
-        drain("pr", 2, 0)
-        prepare("i", 0, VECTOR_COLS)
-        drain("pr", 3, 0)
-
-        bank, bias_t = take_bank([P, P])
-        nc.tensor.transpose(bias_t[:], bias_rows[:], ident[:])
-        nc.scalar.copy(out=bias_cols[:], in_=bias_t[:, 0 : len(PARTS) * TILES])
-        free_banks.append(bank)
-
-        for pair in range(2):
-            finish("mk", 2 * pair, 0)
-            product("pi", 2 * pair, 0, 1)
-            finish("mk", 2 * pair + 1, 0)
-            product("pi", 2 * pair + 1, 0, 1)
-            product("pj", pair, 0, 1)
-        product("pj", 2, 0, 0)
-
-        prepare("j", 0, COLS)
-        for n in range(2):
-            finish("pj", n, 0, 2)
-        finish("pj", 2, 0, 1)
-        prepare("k", 0, COLS)
-        for n in range(TILES):
-            finish("mi", n, 0)
-            if n == 0:
-                finish("pj", TILES - 1, 0)
-            for quarter in range(QUARTERS * n, QUARTERS * (n + 1)):
-                c0 = P * (quarter % 4)
-                cast(PARTS[quarter // 4], 1, c0, c0 + P, True)
-            finish("mr", n, 0)
-            finish("mj", n, 0)
-            finish("pk", n, 0)
-            finish("pi", n, 0, 2)
-            if n > 0:
-                quantize(PARTS[n - 1], 1, 0, COLS)
-
-        for n in range(EARLY_TILES):
-            finish("pr", n, 1)
-            product("pi", n, 1, 0)
-            product("pi", n, 1, 1)
-            finish("mk", n, 1)
-            product("pj", n, 1, 0)
-            product("pj", n, 1, 1)
-        prepare("k", 1, COLS)
-        for n in range(EARLY_TILES):
-            product("pk", n, 1, 0)
-        for n in range(EARLY_TILES):
-            finish("pj", n, 1, 2)
-            product("pk", n, 1, 1)
-        for n in range(EARLY_TILES):
-            finish("mi", n, 1)
-            finish("mr", n, 1)
-            finish("pi", n, 1, 2)
-            finish("mj", n, 1)
-            finish("pk", n, 1, 2)
-        for n in range(EARLY_TILES, TILES):
             for lone, triple in (("pr", "mr"), ("mi", "pi"), ("mj", "pj"), ("mk", "pk")):
-                finish(lone, n, 1)
-                last = (n, triple) == (TILES - 1, "pk")
-                finish(triple, n, 1, 0, 2 if last else 1)
+                finish(lone, n, 2)
+                if (n, triple) == (TILES - 1, "pk"):
+                    finish(triple, n, 2, 0, (0, 256))
+                    finish(triple, n, 2, 0, (256, 512))
+                else:
+                    finish(triple, n, 2)

@@ -21,7 +21,7 @@ BANK = 512
 TILES = N // P
 BANKS = 8
 QUADS = 4
-ALIGN = 64
+ALIGN = 256
 PARTS = "rijk"
 ARRIVAL = "rjki"
 CHUNKS = ((0, 256), (256, 256), (512, 512))
@@ -42,7 +42,8 @@ NARROW = {
     "pr": ((("pr", 0), ("pr", 1)), (("r", "r", 0, 0), ("r", "r", 1, 1))),
     "mj": ((("mj", 0), ("mj", 1)), (("i", "k", 0, 0), ("i", "k", 1, 1))),
     "pjmr": ((("pj", 0), ("mr", 0)), (("j", "rj", 0, 0), ("r", "j", 0, 0), ("k", "ik", 0, 0), ("i", "i", 1, 0))),
-    "pkmi": ((("pk", 0), ("mi", 0)), (("k", "rj", 0, 0), ("i", "j", 0, 0), ("r", "k", 0, 0))),
+    "pkmi": ((("pk", 0), ("mi", 0)), (("k", "rj", 0, 0), ("r", "k", 0, 0), ("i", "j", 0, 0))),
+    "early": ((("pk", 0), ("mi", 0)), (("k", "r", 0, 0), ("k", "j", 1, 0), ("r", "k", 0, 0), ("i", "j", 0, 0))),
     "mkpi": ((("mk", 0), ("pi", 0)), (("j", "ik", 0, 0), ("i", "r", 1, 0), ("r", "i", 1, 0))),
 }
 
@@ -95,11 +96,11 @@ def tile_mix_quat_bias_kernel(
         result = {}
         for o in PARTS:
             for n in range(TILES):
-                result[o, n] = sb.tile([P, T], F32, name="result_%s%d" % (o, n))
+                result[o, n] = sb.tile([P, T], F32, name="result_%s%d" % (o, n), align_bytes=ALIGN)
 
         def load_x(x, h):
             t0, width = CHUNKS[h]
-            raw[x, h] = sb.tile([P, PACK, width], F32, name="raw_%s%d" % (x, h))
+            raw[x, h] = sb.tile([P, PACK, width], F32, name="raw_%s%d" % (x, h), align_bytes=ALIGN)
             src = x_hbm[x].rearrange("(p j) t -> p j t", j=PACK)[:, :, t0 : t0 + width]
             nc.sync.dma_start(out=raw[x, h][:], in_=src)
 
@@ -199,7 +200,7 @@ def tile_mix_quat_bias_kernel(
                 if width == BANK:
                     parked[o, unit, h] = result[o, unit][:, t0 : t0 + width]
                 else:
-                    spare = sb.tile([P, BANK], F32, name="parked_%s%d%d" % (o, unit, h))
+                    spare = sb.tile([P, BANK], F32, name="parked_%s%d%d" % (o, unit, h), align_bytes=ALIGN)
                     parked[o, unit, h] = spare[:]
                 if park_on_vector:
                     nc.vector.tensor_copy(out=parked[o, unit, h], in_=acc[:])
@@ -235,22 +236,24 @@ def tile_mix_quat_bias_kernel(
             acc = narrow[kind, unit, h][1]
             n = unit + tile_step
             wb = word_bytes[w]
-            nc.tensor.matmul_mx(
-                out=acc[:, side * HALF : (side + len(xs)) * HALF],
-                lhsT=w_words[w][:, n * P * wb : (n + 1) * P * wb].bitcast(word_dtype[w]),
-                lhsT_scale=w_scales[w][:, n * P : (n + 1) * P],
-                rhs=x_codes[xs, h].bitcast(FP8X4),
-                rhs_scale=x_scales[xs, h],
-                start=step == 0,
-                stop=step == len(NARROW[kind][1]) - 1,
-            )
+            width = P if (wb == 2 and len(xs) == 1) else len(xs) * HALF
+            for c0 in range(0, len(xs) * HALF, width):
+                nc.tensor.matmul_mx(
+                    out=acc[:, side * HALF + c0 : side * HALF + c0 + width],
+                    lhsT=w_words[w][:, n * P * wb : (n + 1) * P * wb].bitcast(word_dtype[w]),
+                    lhsT_scale=w_scales[w][:, n * P : (n + 1) * P],
+                    rhs=x_codes[xs, h][:, c0 : c0 + width].bitcast(FP8X4),
+                    rhs_scale=x_scales[xs, h][:, c0 : c0 + width],
+                    start=step == 0 and c0 == 0,
+                    stop=step == len(NARROW[kind][1]) - 1,
+                )
 
         def narrow_drain(kind, unit, h, park_on_vector=False):
             bank, acc = narrow[kind, unit, h]
             t0 = CHUNKS[h][0]
             sums = [(name, unit + tile_step) for name, tile_step in NARROW[kind][0]]
             if (sums[0][0][1], sums[0][1], h) not in parked:
-                spare = sb.tile([P, BANK], F32, name="parked_%s%d%d" % (kind, unit, h))
+                spare = sb.tile([P, BANK], F32, name="parked_%s%d%d" % (kind, unit, h), align_bytes=ALIGN)
                 if park_on_vector:
                     nc.vector.tensor_copy(out=spare[:], in_=acc[:])
                 else:
@@ -304,9 +307,9 @@ def tile_mix_quat_bias_kernel(
         load_x("j", 0)
         load_words("k")
         load_words("j")
-        load_words("i")
         load_x("k", 0)
         load_x("i", 0)
+        load_words("i")
         for o in PARTS:
             load_bias(o)
         for h in (1, 2):
@@ -327,11 +330,11 @@ def tile_mix_quat_bias_kernel(
                 passes(kind, n, 0, 0, 1)
         share_cast("k", 0, 160)
         quantize("k", 0)
+        share_cast("i", 0, 160)
+        quantize("i", 0)
         for kind in ("pjmr", "pkmi"):
             for n in range(TILES):
                 passes(kind, n, 0, 1, 2)
-        share_cast("i", 0, 160)
-        quantize("i", 0)
         for n in range(TILES):
             passes("pkmi", n, 0, 2, 3)
         share_cast("r", 1, 256)
@@ -352,13 +355,15 @@ def tile_mix_quat_bias_kernel(
                 quantize("ki"[n - 1], 1)
 
         for n in range(TILES):
-            passes("pkmi", n, 1, 0, 2)
+            passes("pkmi", n, 1, 0, 1)
         for n in range(TILES):
-            passes("pkmi", n, 1, 2, 3)
+            passes("pkmi", n, 1, 1, 3)
         for n in (0, 2):
-            share_cast("rj"[n // 2], 2, 512)
+            cast("rj"[n // 2], 2, 0, BANK if n == 0 else HALF, False)
             passes("pr", n, 1, 0, 2)
             passes("mj", n, 1, 0, 2)
+            if n == 0:
+                cast("j", 2, HALF, BANK, True)
             passes("mkpi", n, 1, 0, 3)
             quantize("rj"[n // 2], 2)
             if n == 2:
@@ -376,7 +381,7 @@ def tile_mix_quat_bias_kernel(
             product("pk", n, 2, 1)
             finish("mi", n, 2)
             product("pj", n, 2, 1)
-        prepare("i", 2, BANK)
+        prepare("i", 2, 384)
         for n in range(2):
             product("pi", n, 2, 0)
         for n in range(2):

@@ -13,6 +13,7 @@ U8 = mybir.dt.uint8
 FP8X4 = mybir.dt.float8_e4m3fn_x4
 FP4X4 = mybir.dt.float4_e2m1fn_x4
 ADD = mybir.AluOpType.add
+MULT = mybir.AluOpType.mult
 SUB = mybir.AluOpType.subtract
 
 P = 128
@@ -43,7 +44,7 @@ NARROW = {
     "mj": ((("mj", 0), ("mj", 1)), (("i", "k", 0, 0), ("i", "k", 1, 1))),
     "pjmr": ((("pj", 0), ("mr", 0)), (("j", "rj", 0, 0), ("r", "j", 0, 0), ("k", "ik", 0, 0), ("i", "i", 1, 0))),
     "pkmi": ((("pk", 0), ("mi", 0)), (("k", "rj", 0, 0), ("r", "k", 0, 0), ("i", "j", 0, 0))),
-    "early": ((("pk", 0), ("mi", 0)), (("k", "r", 0, 0), ("k", "j", 1, 0), ("r", "k", 0, 0), ("i", "j", 0, 0))),
+    "late": ((("pk", 0), ("mi", 0)), (("k", "rj", 0, 0), ("i", "j", 0, 0), ("r", "k", 0, 0))),
     "mkpi": ((("mk", 0), ("pi", 0)), (("j", "ik", 0, 0), ("i", "r", 1, 0), ("r", "i", 1, 0))),
 }
 
@@ -132,6 +133,13 @@ def tile_mix_quat_bias_kernel(
                 nc.scalar.copy(out=dst, in_=src)
             else:
                 nc.vector.tensor_copy(out=dst, in_=src)
+
+        def cast_on_gpsimd(x, h, c0, c1):
+            nc.gpsimd.tensor_scalar(
+                out=grouped[x, h][:, c0 * PACK : c1 * PACK].rearrange("p (c j) -> p c j", j=PACK),
+                in0=raw[x, h][:, :, c0:c1].rearrange("p j c -> p c j"),
+                scalar1=1.0, scalar2=0.0, op0=MULT, op1=ADD,
+            )
 
         def quantize(x, h, c0=0, c1=None):
             c1 = CHUNKS[h][1] if c1 is None else c1
@@ -310,11 +318,12 @@ def tile_mix_quat_bias_kernel(
         load_x("k", 0)
         load_x("i", 0)
         load_words("i")
-        for o in PARTS:
-            load_bias(o)
         for h in (1, 2):
             for x in ARRIVAL:
                 load_x(x, h)
+                if (x, h) == ("j", 1):
+                    for o in PARTS:
+                        load_bias(o)
 
         share_cast("r", 0, 160)
         quantize("r", 0)
@@ -338,37 +347,52 @@ def tile_mix_quat_bias_kernel(
         for n in range(TILES):
             passes("pkmi", n, 0, 2, 3)
         share_cast("r", 1, 256)
-        nc.vector.transpose(bias_cols[:], bias_rows[:])
         quantize("r", 1)
         for n in range(TILES):
             passes("pjmr", n, 0, 2, 3)
         for n in (0, 2):
             passes("mj", n, 0, 0, 2)
         share_cast("j", 1, 256)
+        nc.vector.transpose(bias_cols[:], bias_rows[:])
         quantize("j", 1)
         share_cast("k", 1, 0)
         share_cast("i", 1, 0)
-        for n in range(TILES):
+        for n in range(TILES - 1):
             passes("pjmr", n, 0, 3, 4)
+            if n == 1:
+                quantize("k", 1)
             passes("mkpi", n, 0, 0, 3)
-            if n in (1, 2):
-                quantize("ki"[n - 1], 1)
+            if n == 2:
+                quantize("i", 1)
+        narrow_pass("pjmr", TILES - 1, 0, 3)
+        for step in range(3):
+            narrow_pass("mkpi", TILES - 1, 0, step)
 
-        for n in range(TILES):
-            passes("pkmi", n, 1, 0, 1)
-        for n in range(TILES):
-            passes("pkmi", n, 1, 1, 3)
+        for n in range(TILES - 1):
+            passes("late", n, 1, 0, 2)
+        passes("late", 0, 1, 2, 3)
+        passes("late", TILES - 1, 1, 0, 2)
+        for n in range(1, TILES):
+            passes("late", n, 1, 2, 3)
+        for kind in ("pjmr", "mkpi"):
+            narrow_drain(kind, TILES - 1, 0)
         for n in (0, 2):
-            cast("rj"[n // 2], 2, 0, BANK if n == 0 else HALF, False)
+            if n == 0:
+                for c0 in range(0, BANK, P):
+                    cast_on_gpsimd("r", 2, c0, c0 + P)
+            else:
+                cast("j", 2, 0, HALF, False)
             passes("pr", n, 1, 0, 2)
             passes("mj", n, 1, 0, 2)
             if n == 0:
                 cast("j", 2, HALF, BANK, True)
             passes("mkpi", n, 1, 0, 3)
-            quantize("rj"[n // 2], 2)
             if n == 2:
+                quantize("j", 2)
                 share_cast("k", 2, 0)
             passes("mkpi", n + 1, 1, 0, 3)
+            if n == 0:
+                quantize("r", 2)
             passes("pjmr", n, 1, 0, 4)
             passes("pjmr", n + 1, 1, 0, 4)
 

@@ -44,6 +44,8 @@ NARROW = {
     "mj": ((("mj", 0), ("mj", 1)), (("i", "k", 0, 0), ("i", "k", 1, 1))),
     "pjmr": ((("pj", 0), ("mr", 0)), (("j", "rj", 0, 0), ("r", "j", 0, 0), ("k", "ik", 0, 0), ("i", "i", 1, 0))),
     "pkmi": ((("pk", 0), ("mi", 0)), (("k", "rj", 0, 0), ("r", "k", 0, 0), ("i", "j", 0, 0))),
+    "pk": ((("pk", 0), ("pk", 1)), (("k", "r", 0, 0), ("k", "r", 1, 1), ("r", "k", 0, 0), ("r", "k", 1, 1), ("i", "j", 0, 0), ("i", "j", 1, 1))),
+    "mi": ((("mi", 0), ("mi", 1)), (("k", "j", 0, 0), ("k", "j", 1, 1))),
     "late": ((("pk", 0), ("mi", 0)), (("k", "rj", 0, 0), ("i", "j", 0, 0), ("r", "k", 0, 0))),
     "mkpi": ((("mk", 0), ("pi", 0)), (("j", "ik", 0, 0), ("i", "r", 1, 0), ("r", "i", 1, 0))),
 }
@@ -244,7 +246,8 @@ def tile_mix_quat_bias_kernel(
             acc = narrow[kind, unit, h][1]
             n = unit + tile_step
             wb = word_bytes[w]
-            width = P if (wb == 2 and len(xs) == 1) else len(xs) * HALF
+            lone = kind == "mi"
+            width = P if (wb == 2 and len(xs) == 1 and not lone) else len(xs) * HALF
             for c0 in range(0, len(xs) * HALF, width):
                 nc.tensor.matmul_mx(
                     out=acc[:, side * HALF + c0 : side * HALF + c0 + width],
@@ -252,8 +255,8 @@ def tile_mix_quat_bias_kernel(
                     lhsT_scale=w_scales[w][:, n * P : (n + 1) * P],
                     rhs=x_codes[xs, h][:, c0 : c0 + width].bitcast(FP8X4),
                     rhs_scale=x_scales[xs, h][:, c0 : c0 + width],
-                    start=step == 0 and c0 == 0,
-                    stop=step == len(NARROW[kind][1]) - 1,
+                    start=lone or (step == 0 and c0 == 0),
+                    stop=lone or step == len(NARROW[kind][1]) - 1,
                 )
 
         def narrow_drain(kind, unit, h, park_on_vector=False):
@@ -312,8 +315,8 @@ def tile_mix_quat_bias_kernel(
         load_words("r")
         for q in range(QUADS):
             place_scales(q)
-        load_x("j", 0)
         load_words("k")
+        load_x("j", 0)
         load_words("j")
         load_x("k", 0)
         load_x("i", 0)
@@ -330,28 +333,35 @@ def tile_mix_quat_bias_kernel(
         for n in (0, 2):
             passes("pr", n, 0, 0, 1)
             narrow_pass("pr", n, 0, 1)
+        for n in (0, 2):
+            passes("pk", n, 0, 0, 2)
         share_cast("j", 0, 160)
         quantize("j", 0)
         for n in (0, 2):
             narrow_drain("pr", n, 0)
-        for kind in ("pkmi", "pjmr"):
-            for n in range(TILES):
-                passes(kind, n, 0, 0, 1)
+        for n in range(TILES):
+            passes("pjmr", n, 0, 0, 1)
         share_cast("k", 0, 160)
         quantize("k", 0)
+        for n in (0, 2):
+            narrow_pass("mi", n, 0, 0)
+            narrow_pass("mi", n, 0, 1)
         share_cast("i", 0, 160)
         quantize("i", 0)
-        for kind in ("pjmr", "pkmi"):
-            for n in range(TILES):
-                passes(kind, n, 0, 1, 2)
+        for n in (0, 2):
+            narrow_drain("mi", n, 0)
         for n in range(TILES):
-            passes("pkmi", n, 0, 2, 3)
+            passes("pjmr", n, 0, 1, 2)
+        for n in (0, 2):
+            passes("pk", n, 0, 2, 4)
+        for n in (0, 2):
+            passes("pk", n, 0, 4, 6)
         share_cast("r", 1, 256)
         quantize("r", 1)
-        for n in range(TILES):
-            passes("pjmr", n, 0, 2, 3)
         for n in (0, 2):
             passes("mj", n, 0, 0, 2)
+        for n in range(TILES):
+            passes("pjmr", n, 0, 2, 3)
         share_cast("j", 1, 256)
         nc.vector.transpose(bias_cols[:], bias_rows[:])
         quantize("j", 1)

@@ -26,7 +26,8 @@ ALIGN = 256
 PARTS = "rijk"
 ARRIVAL = "rjki"
 CHUNKS = ((0, 256), (256, 256), (512, 512))
-UNMERGED = 16
+SPLIT = (0, 1)
+WHOLE = (2, 3)
 
 SUMS = {
     "pr": ("rr",),
@@ -281,7 +282,7 @@ def tile_mix_quat_bias_kernel(
                         out=result[o, n][:, t0 : t0 + HALF], in0=plus,
                         scalar=bias_cols[:, col : col + 1], in1=minus, op0=ADD, op1=SUB,
                     )
-                    if h == 1:
+                    if h == 1 and (o, n) in early:
                         store(o, n, 0, T // 2)
             free_banks.append(bank)
 
@@ -305,7 +306,7 @@ def tile_mix_quat_bias_kernel(
             quantize(x, h, 0, 256)
             quantize(x, h, 256, BANK)
 
-        early = [(o, n) for n in range(TILES) for o in PARTS][-UNMERGED:]
+        early = [(o, n) for n in SPLIT for o in PARTS] + [("k", 3), ("i", 3)]
 
         nc.vector.memset(planes[:].bitcast(I32), 0)
         nc.vector.memset(bias_rows[:], 0.0)
@@ -391,6 +392,7 @@ def tile_mix_quat_bias_kernel(
                 for c0 in range(0, BANK, P):
                     cast_on_gpsimd("r", 2, c0, c0 + P)
             else:
+                quantize("r", 2)
                 cast("j", 2, 0, HALF, False)
             passes("pr", n, 1, 0, 2)
             passes("mj", n, 1, 0, 2)
@@ -400,37 +402,50 @@ def tile_mix_quat_bias_kernel(
             if n == 2:
                 quantize("j", 2)
                 share_cast("k", 2, 0)
+                cast("i", 2, 384, BANK, True)
             passes("mkpi", n + 1, 1, 0, 3)
-            if n == 0:
-                quantize("r", 2)
-            passes("pjmr", n, 1, 0, 4)
-            passes("pjmr", n + 1, 1, 0, 4)
+            for m in (n, n + 1):
+                for step in range(4):
+                    narrow_pass("pjmr", m, 1, step)
+                if n == 0:
+                    narrow_drain("pjmr", m, 1)
+        cast("i", 2, 0, 256, False)
+        cast("i", 2, 256, 384, False)
+        quantize("k", 2)
+        quantize("i", 2, 0, 256)
+        quantize("i", 2, 256, BANK)
 
-        for n in range(2):
-            finish("pr", n, 2)
+        first, second = WHOLE
+        for n in WHOLE:
+            product("pr", n, 2, 0)
             product("pk", n, 2, 0)
             product("pj", n, 2, 0)
-        quantize("k", 2)
-        for n in range(2):
+        for m in (2, 3):
+            drain("pr", m, 2)
+        for n in WHOLE:
             product("pk", n, 2, 1)
-            finish("mi", n, 2)
             product("pj", n, 2, 1)
-        prepare("i", 2, 384)
-        for n in range(2):
-            product("pi", n, 2, 0)
-        for n in range(2):
-            finish("pk", n, 2, 2)
-            product("pi", n, 2, 1)
-        for n in range(2):
-            finish("mj", n, 2)
-            finish("mr", n, 2)
-            finish("pj", n, 2, 2)
-            finish("mk", n, 2)
-            finish("pi", n, 2, 2)
-        for n in range(2, TILES):
+        for m in (3, 2):
+            narrow_drain("pjmr", m, 1)
+        finish("pk", first, 2, 2)
+        product("pk", second, 2, 2)
+        finish("mj", first, 2)
+        drain("pk", second, 2)
+        finish("mk", first, 2)
+        finish("mi", first, 2)
+        finish("pj", first, 2, 2)
+        finish("mr", first, 2)
+        finish("pi", first, 2)
+        finish("mj", second, 2)
+        finish("mk", second, 2)
+        finish("pj", second, 2, 2)
+        finish("mi", second, 2)
+        finish("mr", second, 2)
+        finish("pi", second, 2)
+        for n in SPLIT:
             for lone, triple in (("pr", "mr"), ("mi", "pi"), ("mj", "pj"), ("mk", "pk")):
                 finish(lone, n, 2)
-                if (n, triple) == (TILES - 1, "pk"):
+                if (n, triple) == (SPLIT[-1], "pk"):
                     finish(triple, n, 2, 0, (0, 256))
                     finish(triple, n, 2, 0, (256, 512))
                 else:

@@ -88,7 +88,8 @@ def tile_mix_quat_bias_kernel(
         x_scales = {}
         for h, (t0, width) in enumerate(CHUNKS):
             for x in PARTS:
-                grouped[x, h] = sb.tile([P, width * PACK], BF16, name="grouped_%s%d" % (x, h), align_bytes=ALIGN)
+                if (x, h) != ("i", 1):
+                    grouped[x, h] = sb.tile([P, width * PACK], BF16, name="grouped_%s%d" % (x, h), align_bytes=ALIGN)
             for pair in ("rj", "ik"):
                 codes = sb.tile([P, 2 * width], U32, name="codes_%s%d" % (pair, h), align_bytes=ALIGN)
                 scales = sb.tile([P, 2 * width], U8, name="xscales_%s%d" % (pair, h), align_bytes=ALIGN)
@@ -97,6 +98,7 @@ def tile_mix_quat_bias_kernel(
                 for side in range(2):
                     x_codes[pair[side], h] = codes[:, side * width : (side + 1) * width]
                     x_scales[pair[side], h] = scales[:, side * width : (side + 1) * width]
+        grouped["i", 1] = grouped["r", 2][:, : CHUNKS[1][1] * PACK]
         result = {}
         for o in PARTS:
             for n in range(TILES):
@@ -158,6 +160,13 @@ def tile_mix_quat_bias_kernel(
                 cast(x, h, vector_cols, width, True)
             if vector_cols > 0:
                 cast(x, h, 0, vector_cols, False)
+
+        def prepare_first(x):
+            cast(x, 0, 176, HALF, True)
+            cast(x, 0, 0, P, False)
+            cast(x, 0, P, 176, False)
+            quantize(x, 0, 0, P)
+            quantize(x, 0, P, HALF)
 
         free_banks = list(range(BANKS))
         open_sums = {}
@@ -316,8 +325,8 @@ def tile_mix_quat_bias_kernel(
         load_words("r")
         for q in range(QUADS):
             place_scales(q)
-        load_words("k")
         load_x("j", 0)
+        load_words("k")
         load_words("j")
         load_x("k", 0)
         load_x("i", 0)
@@ -336,8 +345,7 @@ def tile_mix_quat_bias_kernel(
             narrow_pass("pr", n, 0, 1)
         for n in (0, 2):
             passes("pk", n, 0, 0, 2)
-        share_cast("j", 0, 160)
-        quantize("j", 0)
+        prepare_first("j")
         for n in (0, 2):
             narrow_drain("pr", n, 0)
         for n in range(TILES):

@@ -318,6 +318,20 @@ def tile_mix_quat_bias_kernel(
         early = [(o, n) for n in SPLIT for o in PARTS] + [("k", 3), ("i", 3)]
 
         nc.vector.memset(planes[:].bitcast(I32), 0)
+        warm_codes = x_codes["i", 2]
+        warm_scales = x_scales["i", 2]
+        for c0 in (0, HALF):
+            nc.vector.quantize_mx(
+                out=warm_codes[:, c0 : c0 + HALF].bitcast(FP8X4),
+                scales=warm_scales[:, c0 : c0 + HALF],
+                in_=planes[:].bitcast(BF16),
+            )
+        warm_bank = ps.tile([P, BANK], F32, name="bank%d" % (BANKS - 1))
+        for rep in range(5):
+            nc.tensor.matmul_mx(
+                out=warm_bank[:], lhsT=warm_codes[:, :P].bitcast(FP8X4), lhsT_scale=warm_scales[:, :P],
+                rhs=warm_codes.bitcast(FP8X4), rhs_scale=warm_scales, start=True, stop=True,
+            )
         nc.vector.memset(bias_rows[:], 0.0)
         for w in PARTS:
             stage_scales(w)

@@ -79,7 +79,6 @@ def tile_mix_quat_bias_kernel(
         w_words = {w: sb.tile([P, N * word_bytes[w]], U8, name="words_" + w, align_bytes=ALIGN) for w in PARTS}
         planes = sb.tile([P, len(PARTS) * N], U8, name="planes", align_bytes=ALIGN)
         w_scales = {w: planes[:, PARTS.index(w) * N : (PARTS.index(w) + 1) * N] for w in PARTS}
-        scale_rows = sb.tile([P, len(PARTS) * N], U8, name="scale_rows", align_bytes=ALIGN)
         bias_rows = sb.tile([P, P], F32, name="bias_rows", align_bytes=ALIGN)
         bias_cols = sb.tile([P, P], F32, name="bias_cols", align_bytes=ALIGN)
         raw = {}
@@ -114,16 +113,10 @@ def tile_mix_quat_bias_kernel(
             nc.sync.dma_start(out=w_words[w][:].bitcast(I32), in_=words_hbm[w].bitcast(I32))
 
         def stage_scales(w):
-            c0 = PARTS.index(w) * N
-            nc.sync.dma_start(
-                out=scale_rows[4:P:8, c0 : c0 + N].bitcast(I32), in_=scales_hbm[w].bitcast(I32)
-            )
+            nc.sync.dma_start(out=w_scales[w][0:P:8, :].bitcast(I32), in_=scales_hbm[w].bitcast(I32))
 
-        def place_scales(q):
-            nc.sync.dma_start(
-                out=planes[32 * q : 32 * q + 4, :].bitcast(I32),
-                in_=scale_rows[32 * q + 4 : 32 * q + 32 : 8, :].bitcast(I32),
-            )
+        def place_scales(r):
+            nc.sync.dma_start(out=planes[r:P:32, :].bitcast(I32), in_=planes[8 * r : P : 32, :].bitcast(I32))
 
         def load_bias(o):
             nc.sync.dma_start(
@@ -318,28 +311,14 @@ def tile_mix_quat_bias_kernel(
         early = [(o, n) for n in SPLIT for o in PARTS] + [("k", 3), ("i", 3)]
 
         nc.vector.memset(planes[:].bitcast(I32), 0)
-        warm_codes = x_codes["i", 2]
-        warm_scales = x_scales["i", 2]
-        for c0 in (0, HALF):
-            nc.vector.quantize_mx(
-                out=warm_codes[:, c0 : c0 + HALF].bitcast(FP8X4),
-                scales=warm_scales[:, c0 : c0 + HALF],
-                in_=planes[:].bitcast(BF16),
-            )
-        warm_bank = ps.tile([P, BANK], F32, name="bank%d" % (BANKS - 1))
-        for rep in range(5):
-            nc.tensor.matmul_mx(
-                out=warm_bank[:], lhsT=warm_codes[:, :P].bitcast(FP8X4), lhsT_scale=warm_scales[:, :P],
-                rhs=warm_codes.bitcast(FP8X4), rhs_scale=warm_scales, start=True, stop=True,
-            )
         nc.vector.memset(bias_rows[:], 0.0)
+        load_words("r")
         for w in PARTS:
             stage_scales(w)
         load_x("r", 0)
-        load_words("r")
-        for q in range(QUADS):
-            place_scales(q)
         load_x("j", 0)
+        for r in range(1, QUADS):
+            place_scales(r)
         load_words("k")
         load_words("j")
         load_x("k", 0)
@@ -351,6 +330,23 @@ def tile_mix_quat_bias_kernel(
                 if (x, h) == ("j", 1):
                     for o in PARTS:
                         load_bias(o)
+
+        warm_codes = x_codes["i", 2]
+        warm_scales = x_scales["i", 2]
+        zeros = grouped["i", 2][:, : HALF * PACK]
+        nc.vector.memset(zeros.bitcast(I32), 0)
+        for c0 in (0, HALF):
+            nc.vector.quantize_mx(
+                out=warm_codes[:, c0 : c0 + HALF].bitcast(FP8X4),
+                scales=warm_scales[:, c0 : c0 + HALF],
+                in_=zeros,
+            )
+        warm_bank = ps.tile([P, BANK], F32, name="bank%d" % (BANKS - 1))
+        for rep in range(5):
+            nc.tensor.matmul_mx(
+                out=warm_bank[:], lhsT=w_words["r"][:, : 4 * P].bitcast(FP8X4), lhsT_scale=warm_scales[:, :P],
+                rhs=warm_codes.bitcast(FP8X4), rhs_scale=warm_scales, start=True, stop=True,
+            )
 
         share_cast("r", 0, 160)
         quantize("r", 0)

@@ -9,6 +9,7 @@ F32 = mybir.dt.float32
 BF16 = mybir.dt.bfloat16
 I32 = mybir.dt.int32
 U32 = mybir.dt.uint32
+U16 = mybir.dt.uint16
 U8 = mybir.dt.uint8
 FP8X4 = mybir.dt.float8_e4m3fn_x4
 FP4X4 = mybir.dt.float4_e2m1fn_x4
@@ -19,36 +20,34 @@ SUB = mybir.AluOpType.subtract
 P = 128
 PACK = 4
 BANK = 512
+HALF = BANK // 2
 TILES = N // P
 BANKS = 8
 QUADS = 4
 ALIGN = 256
-PARTS = "rijk"
-ARRIVAL = "rjki"
-CHUNKS = ((0, 256), (256, 256), (512, 512))
-SPLIT = (0, 1)
-WHOLE = (2, 3)
+RUN = 4
+PARTS = "rjki"
+FIRST, SECOND, WIDE = 0, 1, 2
+CHUNKS = ((0, HALF), (HALF, HALF), (BANK, BANK))
+WARM_PASSES = 5
+QUAD = P // QUADS
+LINE = 16
 
-SUMS = {
-    "pr": ("rr",),
-    "mr": ("jj", "kk", "ii"),
-    "pi": ("ir", "jk", "ri"),
-    "mi": ("kj",),
-    "pj": ("jr", "rj", "ki"),
-    "mj": ("ik",),
-    "pk": ("kr", "ij", "rk"),
-    "mk": ("ji",),
+WEIGHT = {
+    "pr": {"r": "r"},
+    "mr": {"j": "j", "k": "k", "i": "i"},
+    "pi": {"r": "i", "k": "j", "i": "r"},
+    "mi": {"j": "k"},
+    "pj": {"r": "j", "j": "r", "i": "k"},
+    "mj": {"k": "i"},
+    "pk": {"r": "k", "j": "i", "k": "r"},
+    "mk": {"i": "j"},
 }
-HALF = BANK // 2
-NARROW = {
-    "pr": ((("pr", 0), ("pr", 1)), (("r", "r", 0, 0), ("r", "r", 1, 1))),
-    "mj": ((("mj", 0), ("mj", 1)), (("i", "k", 0, 0), ("i", "k", 1, 1))),
-    "pjmr": ((("pj", 0), ("mr", 0)), (("j", "rj", 0, 0), ("r", "j", 0, 0), ("k", "ik", 0, 0), ("i", "i", 1, 0))),
-    "pkmi": ((("pk", 0), ("mi", 0)), (("k", "rj", 0, 0), ("r", "k", 0, 0), ("i", "j", 0, 0))),
-    "pk": ((("pk", 0), ("pk", 1)), (("k", "r", 0, 0), ("k", "r", 1, 1), ("r", "k", 0, 0), ("r", "k", 1, 1), ("i", "j", 0, 0), ("i", "j", 1, 1))),
-    "mi": ((("mi", 0), ("mi", 1)), (("k", "j", 0, 0), ("k", "j", 1, 1))),
-    "late": ((("pk", 0), ("mi", 0)), (("k", "rj", 0, 0), ("i", "j", 0, 0), ("r", "k", 0, 0))),
-    "mkpi": ((("mk", 0), ("pi", 0)), (("j", "ik", 0, 0), ("i", "r", 1, 0), ("r", "i", 1, 0))),
+TWIN = {
+    ("pk", "mi"): (("k", "rj", 0), ("i", "j", 0), ("r", "k", 0)),
+    ("pr", "mj"): (("r", "r", 0), ("i", "k", 1)),
+    ("mk", "pi"): (("j", "ik", 0), ("i", "r", 1), ("r", "i", 1)),
+    ("pj", "mr"): (("j", "rj", 0), ("r", "j", 0), ("k", "ik", 0), ("i", "i", 1)),
 }
 
 
@@ -76,18 +75,19 @@ def tile_mix_quat_bias_kernel(
         ps = ctx.enter_context(tc.psum_pool(name="ps", bufs=1))
         ctx.enter_context(tc.manual_schedule())
 
+        landed = {w: sb.tile([P, N * word_bytes[w]], U8, name="landed_" + w, align_bytes=ALIGN) for w in PARTS}
         w_words = {w: sb.tile([P, N * word_bytes[w]], U8, name="words_" + w, align_bytes=ALIGN) for w in PARTS}
-        planes = sb.tile([P, len(PARTS) * N], U8, name="planes", align_bytes=ALIGN)
-        w_scales = {w: planes[:, PARTS.index(w) * N : (PARTS.index(w) + 1) * N] for w in PARTS}
-        bias_rows = sb.tile([P, P], F32, name="bias_rows", align_bytes=ALIGN)
-        bias_cols = sb.tile([P, P], F32, name="bias_cols", align_bytes=ALIGN)
-        raw = {}
-        grouped = {}
-        x_codes = {}
-        x_scales = {}
+        staged = {w: sb.tile([P, QUADS, N], U8, name="staged_" + w, align_bytes=ALIGN) for w in PARTS}
+        w_scales = {w: sb.tile([P, N], U8, name="plane_" + w, align_bytes=ALIGN) for w in PARTS}
+        bias_cols = {o: sb.tile([P, TILES], F32, name="bias_" + o) for o in PARTS}
+        zeros = sb.tile([P, HALF * PACK], BF16, name="zeros", align_bytes=ALIGN)
+        warm_codes = sb.tile([P, BANK], U32, name="warm_codes", align_bytes=ALIGN)
+        warm_scales = sb.tile([P, BANK], U8, name="warm_scales", align_bytes=ALIGN)
+        raw, grouped, x_codes, x_scales = {}, {}, {}, {}
         for h, (t0, width) in enumerate(CHUNKS):
             for x in PARTS:
-                if (x, h) != ("i", 1):
+                raw[x, h] = sb.tile([P, PACK, width], F32, name="raw_%s%d" % (x, h), align_bytes=ALIGN)
+                if (x, h) != ("i", SECOND):
                     grouped[x, h] = sb.tile([P, width * PACK], BF16, name="grouped_%s%d" % (x, h), align_bytes=ALIGN)
             for pair in ("rj", "ik"):
                 codes = sb.tile([P, 2 * width], U32, name="codes_%s%d" % (pair, h), align_bytes=ALIGN)
@@ -97,37 +97,69 @@ def tile_mix_quat_bias_kernel(
                 for side in range(2):
                     x_codes[pair[side], h] = codes[:, side * width : (side + 1) * width]
                     x_scales[pair[side], h] = scales[:, side * width : (side + 1) * width]
-        grouped["i", 1] = grouped["r", 2][:, : CHUNKS[1][1] * PACK]
+        grouped["i", SECOND] = grouped["r", WIDE][:, : HALF * PACK]
         result = {}
         for o in PARTS:
-            for n in range(TILES):
-                result[o, n] = sb.tile([P, T], F32, name="result_%s%d" % (o, n), align_bytes=ALIGN)
+            for half in range(2):
+                result[o, half] = sb.tile([P, TILES, BANK], F32, name="result_%s%d" % (o, half), align_bytes=ALIGN)
+
+        def result_cols(o, n, h):
+            t0, width = CHUNKS[h]
+            return result[o, t0 // BANK][:, n, t0 % BANK : t0 % BANK + width]
 
         def load_x(x, h):
             t0, width = CHUNKS[h]
-            raw[x, h] = sb.tile([P, PACK, width], F32, name="raw_%s%d" % (x, h), align_bytes=ALIGN)
             src = x_hbm[x].rearrange("(p j) t -> p j t", j=PACK)[:, :, t0 : t0 + width]
             nc.sync.dma_start(out=raw[x, h][:], in_=src)
 
         def load_words(w):
-            nc.sync.dma_start(out=w_words[w][:].bitcast(I32), in_=words_hbm[w].bitcast(I32))
+            nc.sync.dma_start(out=landed[w][:].bitcast(I32), in_=words_hbm[w].bitcast(I32))
+
+        def clear_scales(w):
+            nc.vector.memset(staged[w][:, 0, :].bitcast(I32), 0)
 
         def stage_scales(w):
-            nc.sync.dma_start(out=w_scales[w][0:P:8, :].bitcast(I32), in_=scales_hbm[w].bitcast(I32))
-
-        def place_scales(r):
-            nc.sync.dma_start(out=planes[r:P:32, :].bitcast(I32), in_=planes[8 * r : P : 32, :].bitcast(I32))
-
-        def load_bias(o):
             nc.sync.dma_start(
-                out=bias_rows[PARTS.index(o) : P : 32, :].rearrange("a (n j) -> a n j", j=32),
-                in_=bias_hbm[o].rearrange("(n a j) -> a n j", a=QUADS, j=32),
+                out=staged[w][:PACK, :, :].bitcast(I32),
+                in_=scales_hbm[w].bitcast(I32).rearrange("(q r) n -> r q n", r=PACK),
             )
 
-        def cast(x, h, c0, c1, on_scalar):
-            src = raw[x, h][:, :, c0:c1].rearrange("p j (c i) -> p c j i", i=4)
-            dst = grouped[x, h][:, c0 * PACK : c1 * PACK].rearrange("p (c i j) -> p c j i", i=4, j=PACK)
-            if on_scalar:
+        def deal(dst, src, run):
+            return (
+                dst.rearrange("p (j c i) -> p c j i", j=TILES, i=run),
+                src.rearrange("p (c i j) -> p c j i", j=TILES, i=run),
+            )
+
+        def place_scales(w):
+            for q in range(1, QUADS):
+                nc.vector.tensor_copy(
+                    out=staged[w][QUAD * q : QUAD * q + PACK, 0, :].bitcast(I32),
+                    in_=staged[w][:PACK, q, :].bitcast(I32),
+                )
+
+        def deal_scales(w):
+            dst, src = deal(w_scales[w][:], staged[w][:, 0, :], LINE)
+            nc.vector.tensor_copy(out=dst, in_=src)
+
+        def deal_words(w, engine):
+            if engine == "scalar":
+                word = U32 if word_bytes[w] == 4 else U16
+                dst, src = deal(w_words[w][:].bitcast(word), landed[w][:].bitcast(word), LINE // word_bytes[w])
+                nc.scalar.copy(out=dst, in_=src)
+            else:
+                dst, src = deal(w_words[w][:].bitcast(I32), landed[w][:].bitcast(I32), RUN)
+                nc.vector.tensor_copy(out=dst, in_=src)
+
+        def load_bias(o):
+            nc.sync.dma_start(out=bias_cols[o][:], in_=bias_hbm[o].rearrange("(p j) -> p j", j=TILES))
+
+        def bias(o, n):
+            return bias_cols[o][:, n : n + 1]
+
+        def cast(engine, x, h, c0, c1):
+            src = raw[x, h][:, :, c0:c1].rearrange("p j (c i) -> p c j i", i=RUN)
+            dst = grouped[x, h][:, c0 * PACK : c1 * PACK].rearrange("p (c i j) -> p c j i", i=RUN, j=PACK)
+            if engine == "scalar":
                 nc.scalar.copy(out=dst, in_=src)
             else:
                 nc.vector.tensor_copy(out=dst, in_=src)
@@ -139,6 +171,13 @@ def tile_mix_quat_bias_kernel(
                 scalar1=1.0, scalar2=0.0, op0=MULT, op1=ADD,
             )
 
+        def share_cast(x, h, split, c0=0, c1=None):
+            c1 = CHUNKS[h][1] if c1 is None else c1
+            if split < c1:
+                cast("scalar", x, h, split, c1)
+            if split > c0:
+                cast("vector", x, h, c0, split)
+
         def quantize(x, h, c0=0, c1=None):
             c1 = CHUNKS[h][1] if c1 is None else c1
             nc.vector.quantize_mx(
@@ -147,324 +186,281 @@ def tile_mix_quat_bias_kernel(
                 in_=grouped[x, h][:, c0 * PACK : c1 * PACK],
             )
 
-        def share_cast(x, h, vector_cols):
-            width = CHUNKS[h][1]
-            if vector_cols < width:
-                cast(x, h, vector_cols, width, True)
-            if vector_cols > 0:
-                cast(x, h, 0, vector_cols, False)
-
-        def prepare_first(x):
-            cast(x, 0, 176, HALF, True)
-            cast(x, 0, 0, P, False)
-            cast(x, 0, P, 176, False)
-            quantize(x, 0, 0, P)
-            quantize(x, 0, P, HALF)
-
         free_banks = list(range(BANKS))
-        open_sums = {}
+        held = {}
         parked = {}
-        terms_done = {}
+        head_tags = ["zeros", "warm_codes", "landed_r", "landed_i"] + ["staged_" + w for w in PARTS]
 
-        def tiles_of(unit, h):
-            per_bank = BANK // CHUNKS[h][1]
-            return range(unit * per_bank, (unit + 1) * per_bank)
+        def take_bank(key):
+            bank = free_banks[0]
+            free_banks.remove(bank)
+            held[key] = bank, ps.tile([P, BANK], F32, name="bank%d" % bank)
 
-        def product(name, unit, h, term, cols=None, part=None):
-            w, x = SUMS[name][term]
-            width = CHUNKS[h][1]
-            lo, hi = cols or (0, width)
-            p0, p1 = part or (lo, hi)
-            key = name, unit, h, lo
-            lone = len(SUMS[name]) == 1 and part is None
-            first = key not in open_sums
-            if first:
-                bank = free_banks[0]
-                free_banks.remove(bank)
-                open_sums[key] = bank, ps.tile([P, BANK], F32, name="bank%d" % bank)
-            acc = open_sums[key][1]
-            if p1 == hi:
-                terms_done[key] = terms_done.get(key, 0) + 1
-            closing = terms_done.get(key, 0) == len(SUMS[name])
+        def mx_pass(key, col, w, n, xs, h, start, stop, cols=None):
             wb = word_bytes[w]
-            step = P if (wb == 2 and not lone and p1 - p0 < BANK) else p1 - p0
-            passes = [(n, c0) for n in tiles_of(unit, h) for c0 in range(p0, p1, step)]
-            for n, c0 in passes:
-                a0 = (n * width) % BANK + c0
-                nc.tensor.matmul_mx(
-                    out=acc[:, a0 : a0 + step],
-                    lhsT=w_words[w][:, n * P * wb : (n + 1) * P * wb].bitcast(word_dtype[w]),
-                    lhsT_scale=w_scales[w][:, n * P : (n + 1) * P],
-                    rhs=x_codes[x, h][:, c0 : c0 + step].bitcast(FP8X4),
-                    rhs_scale=x_scales[x, h][:, c0 : c0 + step],
-                    start=lone or (first and (n, c0) == passes[0]),
-                    stop=lone or (closing and (n, c0) == passes[-1]),
-                )
+            cols = cols or slice(0, len(xs) * CHUNKS[h][1])
+            width = cols.stop - cols.start
+            nc.tensor.matmul_mx(
+                out=held[key][1][:, col : col + width],
+                lhsT=w_words[w][:, n * P * wb : (n + 1) * P * wb].bitcast(word_dtype[w]),
+                lhsT_scale=w_scales[w][:, n * P : (n + 1) * P],
+                rhs=x_codes[xs, h][:, cols].bitcast(FP8X4),
+                rhs_scale=x_scales[xs, h][:, cols],
+                start=start,
+                stop=stop,
+            )
 
-        def store(o, n, c0, c1):
-            nc.sync.dma_start(out=out_hbm[o][n * P : (n + 1) * P, c0:c1], in_=result[o, n][:, c0:c1])
+        terms_left = {}
 
-        def drain(name, unit, h, cols=None, park_on_vector=False):
-            o = name[1]
+        def add_term(name, x, n, h):
+            key = name, n, h
+            opening = key not in held
+            if opening:
+                take_bank(key)
+                terms_left[key] = len(WEIGHT[name])
+            terms_left[key] = terms_left[key] - 1
+            tiles = BANK // CHUNKS[h][1]
+            for side in range(tiles):
+                mx_pass(key, side * HALF, WEIGHT[name][x], n + side, x, h,
+                        opening and side == 0, terms_left[key] == 0 and side == tiles - 1)
+
+        def twin(names, n, h, first=0, last=None):
+            key = names, n, h
+            steps = TWIN[names]
+            if first == 0:
+                take_bank(key)
+            for step in range(first, len(steps) if last is None else last):
+                w, xs, side = steps[step]
+                mx_pass(key, side * HALF, w, n, xs, h, step == 0, step == len(steps) - 1)
+
+        def sides_of(key):
+            name, n, h = key
+            if h == WIDE:
+                return [(name, n)]
+            if name in WEIGHT:
+                return [(name, n), (name, n + 1)]
+            return [(name[0], n), (name[1], n)]
+
+        def park(name, n, h):
+            key = name, n, h
+            bank, acc = held[key]
             t0, width = CHUNKS[h]
-            lo, hi = cols or (0, width)
-            bank, acc = open_sums[name, unit, h, lo]
-            if (o, unit, h) not in parked:
-                if width == BANK:
-                    parked[o, unit, h] = result[o, unit][:, t0 : t0 + width]
-                else:
-                    spare = sb.tile([P, BANK], F32, name="parked_%s%d%d" % (o, unit, h), align_bytes=ALIGN)
-                    parked[o, unit, h] = spare[:]
-                if park_on_vector:
-                    nc.vector.tensor_copy(out=parked[o, unit, h], in_=acc[:])
-                else:
-                    nc.scalar.copy(out=parked[o, unit, h], in_=acc[:])
+            if h == WIDE:
+                spot = result_cols(name[1], n, h)
             else:
-                other = parked[o, unit, h]
-                plus, minus = (acc, other) if name[0] == "p" else (other, acc)
-                for n in tiles_of(unit, h):
-                    col = 32 * n + PARTS.index(o)
-                    a0 = (n * width) % BANK
-                    nc.vector.scalar_tensor_tensor(
-                        out=result[o, n][:, t0 + lo : t0 + hi], in0=plus[:, a0 + lo : a0 + hi],
-                        scalar=bias_cols[:, col : col + 1], in1=minus[:, a0 + lo : a0 + hi], op0=ADD, op1=SUB,
-                    )
-                    if t0 >= T // 2:
-                        store(o, n, t0 + lo if (o, n) in early else 0, t0 + hi)
+                label = "spare_%s%d%d" % (sides_of(key)[0][0], n, h)
+                tag = label if h == FIRST else head_tags[len(parked) // 2 - len(head_tags)]
+                spare = sb.tile([P, BANK], F32, name=label, tag=tag, align_bytes=ALIGN)
+                spot = spare[:]
+            nc.scalar.copy(out=spot, in_=acc[:])
+            for side, (s, m) in enumerate(sides_of(key)):
+                parked[s, m, h] = spot[:, side * width : (side + 1) * width]
             free_banks.append(bank)
 
-        def finish(name, unit, h, first_term=0, cols=None):
-            for term in range(first_term, len(SUMS[name])):
-                product(name, unit, h, term, cols)
-            drain(name, unit, h, cols)
+        def store(o, half, tiles=slice(0, TILES), cols=slice(0, BANK)):
+            rows = out_hbm[o].rearrange("(p j) t -> p j t", j=TILES)[:, :, half * BANK : (half + 1) * BANK]
+            nc.sync.dma_start(out=rows[:, tiles, cols], in_=result[o, half][:, tiles, cols])
 
-        narrow = {}
-
-        def narrow_pass(kind, unit, h, step):
-            w, xs, side, tile_step = NARROW[kind][1][step]
-            if step == 0:
-                bank = free_banks[0]
-                free_banks.remove(bank)
-                narrow[kind, unit, h] = bank, ps.tile([P, BANK], F32, name="bank%d" % bank)
-            acc = narrow[kind, unit, h][1]
-            n = unit + tile_step
-            wb = word_bytes[w]
-            lone = kind == "mi"
-            width = P if (wb == 2 and len(xs) == 1 and not lone) else len(xs) * HALF
-            for c0 in range(0, len(xs) * HALF, width):
-                nc.tensor.matmul_mx(
-                    out=acc[:, side * HALF + c0 : side * HALF + c0 + width],
-                    lhsT=w_words[w][:, n * P * wb : (n + 1) * P * wb].bitcast(word_dtype[w]),
-                    lhsT_scale=w_scales[w][:, n * P : (n + 1) * P],
-                    rhs=x_codes[xs, h][:, c0 : c0 + width].bitcast(FP8X4),
-                    rhs_scale=x_scales[xs, h][:, c0 : c0 + width],
-                    start=lone or (step == 0 and c0 == 0),
-                    stop=lone or step == len(NARROW[kind][1]) - 1,
+        def combine(name, n, h, from_psum=True):
+            key = name, n, h
+            bank, acc = held[key]
+            t0, width = CHUNKS[h]
+            for side, (s, m) in enumerate(sides_of(key)):
+                o = s[1]
+                mine = acc[:, side * width : (side + 1) * width] if from_psum else parked[s, m, h]
+                if s[0] == "p":
+                    plus, minus = mine, parked["m" + o, m, h]
+                else:
+                    plus, minus = parked["p" + o, m, h], mine
+                nc.vector.scalar_tensor_tensor(
+                    out=result_cols(o, m, h), in0=plus, scalar=bias(o, m), in1=minus, op0=ADD, op1=SUB,
                 )
+            if from_psum:
+                free_banks.append(bank)
 
-        def narrow_drain(kind, unit, h, park_on_vector=False):
-            bank, acc = narrow[kind, unit, h]
-            t0 = CHUNKS[h][0]
-            sums = [(name, unit + tile_step) for name, tile_step in NARROW[kind][0]]
-            if (sums[0][0][1], sums[0][1], h) not in parked:
-                spare = sb.tile([P, BANK], F32, name="parked_%s%d%d" % (kind, unit, h), align_bytes=ALIGN)
-                if park_on_vector:
-                    nc.vector.tensor_copy(out=spare[:], in_=acc[:])
-                else:
-                    nc.scalar.copy(out=spare[:], in_=acc[:])
-                for side, (name, n) in enumerate(sums):
-                    parked[name[1], n, h] = spare[:, side * HALF : (side + 1) * HALF]
+        def close_piece(name, n, cols):
+            o = name[1]
+            key = name, n, cols.start
+            take_bank(key)
+            bank, acc = held[key]
+            sums = acc[:, : cols.stop - cols.start]
+            spot = result_cols(o, n, WIDE)[:, cols]
+            terms = list(WEIGHT[name].items())
+            for step, (x, w) in enumerate(terms):
+                mx_pass(key, 0, w, n, x, WIDE, step == 0, step == len(terms) - 1, cols)
+            if name[0] == "p":
+                nc.scalar.copy(out=spot, in_=sums)
             else:
-                for side, (name, n) in enumerate(sums):
-                    o = name[1]
-                    mine = acc[:, side * HALF : (side + 1) * HALF]
-                    plus, minus = (mine, parked[o, n, h]) if name[0] == "p" else (parked[o, n, h], mine)
-                    col = 32 * n + PARTS.index(o)
-                    nc.vector.scalar_tensor_tensor(
-                        out=result[o, n][:, t0 : t0 + HALF], in0=plus,
-                        scalar=bias_cols[:, col : col + 1], in1=minus, op0=ADD, op1=SUB,
-                    )
-                    if h == 1 and (o, n) in early:
-                        store(o, n, 0, T // 2)
+                nc.vector.scalar_tensor_tensor(out=spot, in0=spot, scalar=bias(o, n), in1=sums, op0=ADD, op1=SUB)
+                store(o, 1, slice(n, n + 1), cols)
             free_banks.append(bank)
 
-        def passes(kind, unit, h, first, last):
-            for step in range(first, last):
-                narrow_pass(kind, unit, h, step)
-            if last == len(NARROW[kind][1]):
-                narrow_drain(kind, unit, h)
+        pairs = range(0, TILES, 2)
 
-        def with_weight(w, names, n, h):
-            for name in names:
-                product(name, n, h, [term[0] for term in SUMS[name]].index(w))
-                if terms_done[name, n, h, 0] == len(SUMS[name]):
-                    drain(name, n, h)
-
-        def prepare(x, h, vector_cols):
-            if vector_cols < BANK:
-                cast(x, h, vector_cols, BANK, True)
-            cast(x, h, 0, 256, False)
-            cast(x, h, 256, vector_cols, False)
-            quantize(x, h, 0, 256)
-            quantize(x, h, 256, BANK)
-
-        early = [(o, n) for n in SPLIT for o in PARTS] + [("k", 3), ("i", 3)]
-
-        nc.vector.memset(planes[:].bitcast(I32), 0)
-        nc.vector.memset(bias_rows[:], 0.0)
-        load_words("r")
-        for w in PARTS:
-            stage_scales(w)
-        load_x("r", 0)
-        load_x("j", 0)
-        for r in range(1, QUADS):
-            place_scales(r)
+        clear_scales("k")
+        nc.vector.memset(zeros[:].bitcast(I32), 0)
+        clear_scales("j")
         load_words("k")
+        stage_scales("k")
+        load_x("r", FIRST)
+        load_x("j", FIRST)
+        stage_scales("j")
         load_words("j")
-        load_x("k", 0)
-        load_x("i", 0)
-        load_words("i")
-        for h in (1, 2):
-            for x in ARRIVAL:
-                load_x(x, h)
-                if (x, h) == ("j", 1):
-                    for o in PARTS:
-                        load_bias(o)
-
-        warm_codes = x_codes["i", 2]
-        warm_scales = x_scales["i", 2]
-        zeros = grouped["i", 2][:, : HALF * PACK]
-        nc.vector.memset(zeros.bitcast(I32), 0)
         for c0 in (0, HALF):
             nc.vector.quantize_mx(
-                out=warm_codes[:, c0 : c0 + HALF].bitcast(FP8X4),
-                scales=warm_scales[:, c0 : c0 + HALF],
-                in_=zeros,
+                out=warm_codes[:, c0 : c0 + HALF].bitcast(FP8X4), scales=warm_scales[:, c0 : c0 + HALF], in_=zeros[:],
             )
+        clear_scales("r")
+        clear_scales("i")
+        stage_scales("r")
+        load_words("r")
+        load_x("k", FIRST)
+        stage_scales("i")
+        load_words("i")
+        load_x("i", FIRST)
+        load_x("r", SECOND)
+        for o in PARTS:
+            load_bias(o)
+        for x in PARTS[1:]:
+            load_x(x, SECOND)
+        for x in PARTS:
+            load_x(x, WIDE)
         warm_bank = ps.tile([P, BANK], F32, name="bank%d" % (BANKS - 1))
-        for rep in range(5):
+        for rep in range(WARM_PASSES):
             nc.tensor.matmul_mx(
-                out=warm_bank[:], lhsT=w_words["r"][:, : 4 * P].bitcast(FP8X4), lhsT_scale=warm_scales[:, :P],
-                rhs=warm_codes.bitcast(FP8X4), rhs_scale=warm_scales, start=True, stop=True,
+                out=warm_bank[:], lhsT=warm_codes[:, :P].bitcast(FP8X4), lhsT_scale=warm_scales[:, :P],
+                rhs=warm_codes[:].bitcast(FP8X4), rhs_scale=warm_scales[:], start=True, stop=True,
             )
 
-        share_cast("r", 0, 160)
-        quantize("r", 0)
-        for n in (0, 2):
-            passes("pr", n, 0, 0, 1)
-            narrow_pass("pr", n, 0, 1)
-        for n in (0, 2):
-            passes("pk", n, 0, 0, 2)
-        prepare_first("j")
-        for n in (0, 2):
-            narrow_drain("pr", n, 0)
+        deal_words("k", "scalar")
+        place_scales("k")
+        deal_scales("k")
+        share_cast("r", FIRST, 144)
+        quantize("r", FIRST)
+        share_cast("j", FIRST, 144)
+        place_scales("j")
+        quantize("j", FIRST)
+        deal_words("j", "scalar")
+        deal_scales("j")
+        for n in pairs:
+            add_term("pk", "r", n, FIRST)
+        for n in pairs:
+            add_term("mi", "j", n, FIRST)
+        place_scales("r")
+        deal_words("r", "vector")
+        deal_scales("r")
+        for n in pairs:
+            park("mi", n, FIRST)
         for n in range(TILES):
-            passes("pjmr", n, 0, 0, 1)
-        share_cast("k", 0, 160)
-        quantize("k", 0)
-        for n in (0, 2):
-            narrow_pass("mi", n, 0, 0)
-            narrow_pass("mi", n, 0, 1)
-        share_cast("i", 0, 160)
-        quantize("i", 0)
-        for n in (0, 2):
-            narrow_drain("mi", n, 0)
+            twin(("pj", "mr"), n, FIRST, 0, 1)
+        share_cast("k", FIRST, 144)
+        place_scales("i")
+        quantize("k", FIRST)
+        deal_scales("i")
+        deal_words("i", "vector")
         for n in range(TILES):
-            passes("pjmr", n, 0, 1, 2)
-        for n in (0, 2):
-            passes("pk", n, 0, 2, 4)
-        for n in (0, 2):
-            passes("pk", n, 0, 4, 6)
-        share_cast("r", 1, 256)
-        quantize("r", 1)
-        for n in (0, 2):
-            passes("mj", n, 0, 0, 2)
+            twin(("pj", "mr"), n, FIRST, 1, 2)
+        for n in pairs:
+            add_term("pr", "r", n, FIRST)
+            park("pr", n, FIRST)
+        for n in pairs:
+            add_term("pk", "k", n, FIRST)
+        share_cast("i", FIRST, 256)
+        quantize("i", FIRST)
+        for n in pairs:
+            add_term("pk", "j", n, FIRST)
+            park("pk", n, FIRST)
+        for x in "rk":
+            for n in pairs:
+                add_term("pi", x, n, FIRST)
+        share_cast("r", SECOND, 256)
+        quantize("r", SECOND)
+        for n in pairs:
+            add_term("mj", "k", n, FIRST)
+            park("mj", n, FIRST)
+        cast("scalar", "j", SECOND, 128, HALF)
+        for n in pairs:
+            add_term("pi", "i", n, FIRST)
+            combine("pi", n, FIRST)
+            if n == 0:
+                cast("vector", "j", SECOND, 0, 128)
+        quantize("j", SECOND)
+        share_cast("k", SECOND, 0)
+        share_cast("i", SECOND, 0)
         for n in range(TILES):
-            passes("pjmr", n, 0, 2, 3)
-        share_cast("j", 1, 256)
-        nc.vector.transpose(bias_cols[:], bias_rows[:])
-        quantize("j", 1)
-        share_cast("k", 1, 0)
-        share_cast("i", 1, 0)
+            twin(("pj", "mr"), n, FIRST, 2, 4)
+            if n < TILES - 1:
+                combine(("pj", "mr"), n, FIRST)
+            if n == 0:
+                quantize("k", SECOND)
+        quantize("i", SECOND)
+        for n in pairs:
+            add_term("mk", "i", n, FIRST)
+
         for n in range(TILES - 1):
-            passes("pjmr", n, 0, 3, 4)
+            twin(("pk", "mi"), n, SECOND, 0, 2)
+        for n in range(TILES):
+            twin(("pk", "mi"), n, SECOND, 2 if n < TILES - 1 else 0, 3)
+            if n == TILES - 1:
+                for m in pairs:
+                    combine("mk", m, FIRST)
+            park(("pk", "mi"), n, SECOND)
+            if n == 0:
+                combine(("pj", "mr"), TILES - 1, FIRST)
+        for c0 in range(0, BANK, P):
+            cast_on_gpsimd("r", WIDE, c0, c0 + P)
+        for n in range(TILES):
+            twin(("pr", "mj"), n, SECOND)
+            park(("pr", "mj"), n, SECOND)
+            twin(("mk", "pi"), n, SECOND)
+            combine(("mk", "pi"), n, SECOND)
             if n == 1:
-                quantize("k", 1)
-            passes("mkpi", n, 0, 0, 3)
-            if n == 2:
-                quantize("i", 1)
-        narrow_pass("pjmr", TILES - 1, 0, 3)
-        for step in range(3):
-            narrow_pass("mkpi", TILES - 1, 0, step)
-
-        for n in range(TILES - 1):
-            passes("late", n, 1, 0, 2)
-        passes("late", 0, 1, 2, 3)
-        passes("late", TILES - 1, 1, 0, 2)
-        for n in range(1, TILES):
-            passes("late", n, 1, 2, 3)
-        for kind in ("pjmr", "mkpi"):
-            narrow_drain(kind, TILES - 1, 0)
-        for n in (0, 2):
+                cast("scalar", "j", WIDE, 256, BANK)
+        store("k", 0)
+        store("i", 0)
+        quantize("r", WIDE)
+        cast("vector", "j", WIDE, 0, 256)
+        share_cast("k", WIDE, 0)
+        for n in range(TILES):
+            twin(("pj", "mr"), n, SECOND)
+            combine(("pj", "mr"), n, SECOND)
             if n == 0:
-                for c0 in range(0, BANK, P):
-                    cast_on_gpsimd("r", 2, c0, c0 + P)
-            else:
-                quantize("r", 2)
-                cast("j", 2, 0, HALF, False)
-            passes("pr", n, 1, 0, 2)
-            passes("mj", n, 1, 0, 2)
-            if n == 0:
-                cast("j", 2, HALF, BANK, True)
-            passes("mkpi", n, 1, 0, 3)
+                quantize("j", WIDE)
             if n == 2:
-                quantize("j", 2)
-                share_cast("k", 2, 0)
-                cast("i", 2, 384, BANK, True)
-            passes("mkpi", n + 1, 1, 0, 3)
-            for m in (n, n + 1):
-                for step in range(4):
-                    narrow_pass("pjmr", m, 1, step)
-                if n == 0:
-                    narrow_drain("pjmr", m, 1)
-        cast("i", 2, 0, 256, False)
-        cast("i", 2, 256, 384, False)
-        quantize("k", 2)
-        quantize("i", 2, 0, 256)
-        quantize("i", 2, 256, BANK)
+                quantize("k", WIDE)
+        store("j", 0)
+        store("r", 0)
+        share_cast("i", WIDE, 256)
+        quantize("i", WIDE)
 
-        first, second = WHOLE
-        for n in WHOLE:
-            product("pr", n, 2, 0)
-            product("pk", n, 2, 0)
-            product("pj", n, 2, 0)
-        for m in (2, 3):
-            drain("pr", m, 2)
-        for n in WHOLE:
-            product("pk", n, 2, 1)
-            product("pj", n, 2, 1)
-        for m in (3, 2):
-            narrow_drain("pjmr", m, 1)
-        finish("pk", first, 2, 2)
-        product("pk", second, 2, 2)
-        finish("mj", first, 2)
-        drain("pk", second, 2)
-        finish("mk", first, 2)
-        finish("mi", first, 2)
-        finish("pj", first, 2, 2)
-        finish("mr", first, 2)
-        finish("pi", first, 2)
-        finish("mj", second, 2)
-        finish("mk", second, 2)
-        finish("pj", second, 2, 2)
-        finish("mi", second, 2)
-        finish("mr", second, 2)
-        finish("pi", second, 2)
-        for n in SPLIT:
-            for lone, triple in (("pr", "mr"), ("mi", "pi"), ("mj", "pj"), ("mk", "pk")):
-                finish(lone, n, 2)
-                if (n, triple) == (SPLIT[-1], "pk"):
-                    finish(triple, n, 2, 0, (0, 256))
-                    finish(triple, n, 2, 0, (256, 512))
-                else:
-                    finish(triple, n, 2)
+        def close_wide(name, n, drain):
+            for x in WEIGHT[name]:
+                add_term(name, x, n, WIDE)
+            drain(name, n, WIDE)
+
+        for x in "rj":
+            for n in range(TILES):
+                add_term("pk", x, n, WIDE)
+        for n in range(TILES):
+            close_wide("mi", n, park)
+        for n in range(TILES):
+            add_term("pk", "k", n, WIDE)
+            park("pk", n, WIDE)
+        for n in range(TILES):
+            close_wide("mk", n, combine)
+        store("k", 1)
+        for n in range(TILES):
+            close_wide("pi", n, combine)
+        store("i", 1)
+        for n in range(TILES):
+            close_wide("mj", n, park)
+            close_wide("pj", n, combine)
+            if n % 2 == 1:
+                store("j", 1, slice(n - 1, n + 1))
+        for n in range(TILES // 2):
+            close_wide("pr", n, park)
+            close_wide("mr", n, combine)
+            store("r", 1, slice(n, n + 1))
+        for n, c0, c1 in ((2, 0, 256), (2, 256, 512), (3, 0, 256), (3, 256, 384), (3, 384, 512)):
+            for name in ("pr", "mr"):
+                close_piece(name, n, slice(c0, c1))

@@ -79,7 +79,9 @@ def tile_mix_quat_bias_kernel(
         w_words = {w: sb.tile([P, N * word_bytes[w]], U8, name="words_" + w, align_bytes=ALIGN) for w in PARTS}
         staged = {w: sb.tile([P, QUADS, N], U8, name="staged_" + w, align_bytes=ALIGN) for w in PARTS}
         w_scales = {w: sb.tile([P, N], U8, name="plane_" + w, align_bytes=ALIGN) for w in PARTS}
-        bias_cols = {o: sb.tile([P, TILES], F32, name="bias_" + o) for o in PARTS}
+        bias_rows = sb.tile([P, P], F32, name="bias_rows", align_bytes=ALIGN)
+        bias_dealt = sb.tile([P, P], F32, name="bias_dealt", align_bytes=ALIGN)
+        bias_cols = sb.tile([P, P], F32, name="bias_cols", align_bytes=ALIGN)
         zeros = sb.tile([P, HALF * PACK], BF16, name="zeros", align_bytes=ALIGN)
         warm_codes = sb.tile([P, BANK], U32, name="warm_codes", align_bytes=ALIGN)
         warm_scales = sb.tile([P, BANK], U8, name="warm_scales", align_bytes=ALIGN)
@@ -151,10 +153,18 @@ def tile_mix_quat_bias_kernel(
                 nc.vector.tensor_copy(out=dst, in_=src)
 
         def load_bias(o):
-            nc.sync.dma_start(out=bias_cols[o][:], in_=bias_hbm[o].rearrange("(p j) -> p j", j=TILES))
+            nc.sync.dma_start(out=bias_rows[PARTS.index(o) : P : QUAD, :], in_=bias_hbm[o].rearrange("(q c) -> q c", q=QUADS))
+
+        def turn_biases():
+            nc.vector.tensor_copy(
+                out=bias_dealt[:].rearrange("p (j c) -> p j c", j=TILES),
+                in_=bias_rows[:].rearrange("p (c j) -> p j c", j=TILES),
+            )
+            nc.vector.transpose(bias_cols[:], bias_dealt[:])
 
         def bias(o, n):
-            return bias_cols[o][:, n : n + 1]
+            col = QUAD * n + PARTS.index(o)
+            return bias_cols[:, col : col + 1]
 
         def cast(engine, x, h, c0, c1):
             src = raw[x, h][:, :, c0:c1].rearrange("p j (c i) -> p c j i", i=RUN)
@@ -312,6 +322,7 @@ def tile_mix_quat_bias_kernel(
             )
         clear_scales("r")
         clear_scales("i")
+        nc.vector.memset(bias_rows[:], 0.0)
         stage_scales("r")
         load_words("r")
         load_x("k", FIRST)
@@ -374,6 +385,7 @@ def tile_mix_quat_bias_kernel(
             for n in pairs:
                 add_term("pi", x, n, FIRST)
         share_cast("r", SECOND, 256)
+        turn_biases()
         quantize("r", SECOND)
         for n in pairs:
             add_term("mj", "k", n, FIRST)

@@ -29,9 +29,10 @@ RUN = 4
 PARTS = "rjki"
 FIRST, SECOND, WIDE = 0, 1, 2
 CHUNKS = ((0, HALF), (HALF, HALF), (BANK, BANK))
-WARM_PASSES = 5
+WARM_PASSES = 7
 QUAD = P // QUADS
 LINE = 16
+LATE = "jri"
 
 WEIGHT = {
     "pr": {"r": "r"},
@@ -77,7 +78,10 @@ def tile_mix_quat_bias_kernel(
 
         landed = {w: sb.tile([P, N * word_bytes[w]], U8, name="landed_" + w, align_bytes=ALIGN) for w in PARTS}
         w_words = {w: sb.tile([P, N * word_bytes[w]], U8, name="words_" + w, align_bytes=ALIGN) for w in PARTS}
-        staged = {w: sb.tile([P, QUADS, N], U8, name="staged_" + w, align_bytes=ALIGN) for w in PARTS}
+        staged = sb.tile([P, QUADS, N], U8, name="staged", align_bytes=ALIGN)
+        late_planes = sb.tile([P, len(LATE) * N], U8, name="late_planes", align_bytes=ALIGN)
+        placed = {w: late_planes[:, LATE.index(w) * N : (LATE.index(w) + 1) * N] for w in LATE}
+        placed["k"] = staged[:, 0, :]
         w_scales = {w: sb.tile([P, N], U8, name="plane_" + w, align_bytes=ALIGN) for w in PARTS}
         bias_rows = sb.tile([P, P], F32, name="bias_rows", align_bytes=ALIGN)
         bias_dealt = sb.tile([P, P], F32, name="bias_dealt", align_bytes=ALIGN)
@@ -117,13 +121,25 @@ def tile_mix_quat_bias_kernel(
         def load_words(w):
             nc.sync.dma_start(out=landed[w][:].bitcast(I32), in_=words_hbm[w].bitcast(I32))
 
-        def clear_scales(w):
-            nc.vector.memset(staged[w][:, 0, :].bitcast(I32), 0)
-
-        def stage_scales(w):
+        def stage_first_scales():
             nc.sync.dma_start(
-                out=staged[w][:PACK, :, :].bitcast(I32),
-                in_=scales_hbm[w].bitcast(I32).rearrange("(q r) n -> r q n", r=PACK),
+                out=staged[:PACK, :, :].bitcast(I32),
+                in_=scales_hbm["k"].bitcast(I32).rearrange("(q r) n -> r q n", r=PACK),
+            )
+
+        def place_first_scales():
+            for q in range(1, QUADS):
+                nc.vector.tensor_copy(
+                    out=staged[QUAD * q : QUAD * q + PACK, 0, :].bitcast(I32),
+                    in_=staged[:PACK, q, :].bitcast(I32),
+                )
+
+        def stage_late_scales(w):
+            nc.sync.dma_start(out=placed[w][0:P:8, :].bitcast(I32), in_=scales_hbm[w].bitcast(I32))
+
+        def place_late_scales(r):
+            nc.sync.dma_start(
+                out=late_planes[r:P:QUAD, :].bitcast(I32), in_=late_planes[8 * r : P : QUAD, :].bitcast(I32),
             )
 
         def deal(dst, src, run):
@@ -132,15 +148,8 @@ def tile_mix_quat_bias_kernel(
                 src.rearrange("p (c i j) -> p c j i", j=TILES, i=run),
             )
 
-        def place_scales(w):
-            for q in range(1, QUADS):
-                nc.vector.tensor_copy(
-                    out=staged[w][QUAD * q : QUAD * q + PACK, 0, :].bitcast(I32),
-                    in_=staged[w][:PACK, q, :].bitcast(I32),
-                )
-
         def deal_scales(w):
-            dst, src = deal(w_scales[w][:], staged[w][:, 0, :], LINE)
+            dst, src = deal(w_scales[w][:], placed[w], LINE)
             nc.vector.tensor_copy(out=dst, in_=src)
 
         def deal_words(w, engine):
@@ -199,7 +208,7 @@ def tile_mix_quat_bias_kernel(
         free_banks = list(range(BANKS))
         held = {}
         parked = {}
-        head_tags = ["zeros", "warm_codes", "landed_r", "landed_i"] + ["staged_" + w for w in PARTS]
+        head_tags = ["zeros", "warm_codes", "landed_r", "landed_i", "staged"]
 
         def take_bank(key):
             bank = free_banks[0]
@@ -259,7 +268,10 @@ def tile_mix_quat_bias_kernel(
                 spot = result_cols(name[1], n, h)
             else:
                 label = "spare_%s%d%d" % (sides_of(key)[0][0], n, h)
-                tag = label if h == FIRST else head_tags[len(parked) // 2 - len(head_tags)]
+                tag = label
+                if h == SECOND and head_tags:
+                    tag = head_tags[0]
+                    head_tags.remove(tag)
                 spare = sb.tile([P, BANK], F32, name=label, tag=tag, align_bytes=ALIGN)
                 spot = spare[:]
             nc.scalar.copy(out=spot, in_=acc[:])
@@ -307,28 +319,27 @@ def tile_mix_quat_bias_kernel(
 
         pairs = range(0, TILES, 2)
 
-        clear_scales("k")
+        nc.vector.memset(placed["k"].bitcast(I32), 0)
+        nc.vector.memset(late_planes[:].bitcast(I32), 0)
         nc.vector.memset(zeros[:].bitcast(I32), 0)
-        clear_scales("j")
+        nc.vector.memset(bias_rows[:], 0.0)
         load_words("k")
-        stage_scales("k")
+        stage_first_scales()
         load_x("r", FIRST)
+        for w in LATE:
+            stage_late_scales(w)
         load_x("j", FIRST)
-        stage_scales("j")
         load_words("j")
+        for r in range(1, PACK):
+            place_late_scales(r)
+        load_words("r")
+        load_x("k", FIRST)
+        load_words("i")
+        load_x("i", FIRST)
         for c0 in (0, HALF):
             nc.vector.quantize_mx(
                 out=warm_codes[:, c0 : c0 + HALF].bitcast(FP8X4), scales=warm_scales[:, c0 : c0 + HALF], in_=zeros[:],
             )
-        clear_scales("r")
-        clear_scales("i")
-        nc.vector.memset(bias_rows[:], 0.0)
-        stage_scales("r")
-        load_words("r")
-        load_x("k", FIRST)
-        stage_scales("i")
-        load_words("i")
-        load_x("i", FIRST)
         load_x("r", SECOND)
         for o in PARTS:
             load_bias(o)
@@ -344,12 +355,11 @@ def tile_mix_quat_bias_kernel(
             )
 
         deal_words("k", "scalar")
-        place_scales("k")
+        place_first_scales()
         deal_scales("k")
         share_cast("r", FIRST, 144)
         quantize("r", FIRST)
         share_cast("j", FIRST, 144)
-        place_scales("j")
         quantize("j", FIRST)
         deal_words("j", "scalar")
         deal_scales("j")
@@ -357,17 +367,15 @@ def tile_mix_quat_bias_kernel(
             add_term("pk", "r", n, FIRST)
         for n in pairs:
             add_term("mi", "j", n, FIRST)
-        place_scales("r")
-        deal_words("r", "vector")
         deal_scales("r")
+        deal_words("r", "vector")
         for n in pairs:
             park("mi", n, FIRST)
         for n in range(TILES):
             twin(("pj", "mr"), n, FIRST, 0, 1)
         share_cast("k", FIRST, 144)
-        place_scales("i")
-        quantize("k", FIRST)
         deal_scales("i")
+        quantize("k", FIRST)
         deal_words("i", "vector")
         for n in range(TILES):
             twin(("pj", "mr"), n, FIRST, 1, 2)

@@ -24,15 +24,16 @@ HALF = BANK // 2
 TILES = N // P
 BANKS = 8
 QUADS = 4
+QUAD = P // QUADS
 ALIGN = 256
 RUN = 4
+LINE = 16
 PARTS = "rjki"
+LATE = "jri"
 FIRST, SECOND, WIDE = 0, 1, 2
 CHUNKS = ((0, HALF), (HALF, HALF), (BANK, BANK))
-WARM_PASSES = 7
-QUAD = P // QUADS
-LINE = 16
-LATE = "jri"
+WARM_PASSES = 8
+QUICK_SPLIT = 192
 
 WEIGHT = {
     "pr": {"r": "r"},
@@ -76,71 +77,47 @@ def tile_mix_quat_bias_kernel(
         ps = ctx.enter_context(tc.psum_pool(name="ps", bufs=1))
         ctx.enter_context(tc.manual_schedule())
 
-        landed = {w: sb.tile([P, N * word_bytes[w]], U8, name="landed_" + w, align_bytes=ALIGN) for w in PARTS}
-        w_words = {w: sb.tile([P, N * word_bytes[w]], U8, name="words_" + w, align_bytes=ALIGN) for w in PARTS}
-        staged = sb.tile([P, QUADS, N], U8, name="staged", align_bytes=ALIGN)
-        late_planes = sb.tile([P, len(LATE) * N], U8, name="late_planes", align_bytes=ALIGN)
+        def sbuf(name, shape, dtype, tag=""):
+            return sb.tile(shape, dtype, name=name, tag=tag or name, align_bytes=ALIGN)
+
+        landed = {w: sbuf("landed_" + w, [P, N * word_bytes[w]], U8) for w in PARTS}
+        w_words = {w: sbuf("words_" + w, [P, N * word_bytes[w]], U8) for w in PARTS}
+        staged = sbuf("staged", [P, QUADS, N], U8)
+        late_planes = sbuf("late_planes", [P, len(LATE) * N], U8)
         placed = {w: late_planes[:, LATE.index(w) * N : (LATE.index(w) + 1) * N] for w in LATE}
         placed["k"] = staged[:, 0, :]
-        w_scales = {w: sb.tile([P, N], U8, name="plane_" + w, align_bytes=ALIGN) for w in PARTS}
-        bias_rows = sb.tile([P, P], F32, name="bias_rows", align_bytes=ALIGN)
-        bias_dealt = sb.tile([P, P], F32, name="bias_dealt", align_bytes=ALIGN)
-        bias_cols = sb.tile([P, P], F32, name="bias_cols", align_bytes=ALIGN)
-        zeros = sb.tile([P, HALF * PACK], BF16, name="zeros", align_bytes=ALIGN)
-        warm_codes = sb.tile([P, BANK], U32, name="warm_codes", align_bytes=ALIGN)
-        warm_scales = sb.tile([P, BANK], U8, name="warm_scales", align_bytes=ALIGN)
-        raw, grouped, x_codes, x_scales = {}, {}, {}, {}
+        w_scales = {w: sbuf("plane_" + w, [P, N], U8) for w in PARTS}
+        bias_cols = {o: sbuf("bias_" + o, [P, TILES], F32) for o in PARTS}
+        zeros = sbuf("zeros", [P, HALF * PACK], BF16)
+        warm_codes = sbuf("warm_codes", [P, BANK], U32)
+        warm_scales = sbuf("warm_scales", [P, BANK], U8)
+        x_codes, x_scales = {}, {}
         for h, (t0, width) in enumerate(CHUNKS):
-            for x in PARTS:
-                raw[x, h] = sb.tile([P, PACK, width], F32, name="raw_%s%d" % (x, h), align_bytes=ALIGN)
-                if (x, h) != ("i", SECOND):
-                    grouped[x, h] = sb.tile([P, width * PACK], BF16, name="grouped_%s%d" % (x, h), align_bytes=ALIGN)
             for pair in ("rj", "ik"):
-                codes = sb.tile([P, 2 * width], U32, name="codes_%s%d" % (pair, h), align_bytes=ALIGN)
-                scales = sb.tile([P, 2 * width], U8, name="xscales_%s%d" % (pair, h), align_bytes=ALIGN)
+                codes = sbuf("codes_%s%d" % (pair, h), [P, 2 * width], U32)
+                scales = sbuf("xscales_%s%d" % (pair, h), [P, 2 * width], U8)
                 x_codes[pair, h] = codes[:]
                 x_scales[pair, h] = scales[:]
                 for side in range(2):
                     x_codes[pair[side], h] = codes[:, side * width : (side + 1) * width]
                     x_scales[pair[side], h] = scales[:, side * width : (side + 1) * width]
-        grouped["i", SECOND] = grouped["r", WIDE][:, : HALF * PACK]
-        result = {}
-        for o in PARTS:
-            for half in range(2):
-                result[o, half] = sb.tile([P, TILES, BANK], F32, name="result_%s%d" % (o, half), align_bytes=ALIGN)
+        result = {(o, half): sbuf("result_%s%d" % (o, half), [P, TILES, BANK], F32) for o in PARTS for half in range(2)}
 
-        def result_cols(o, n, h):
+        def result_cols(o, tiles, h):
             t0, width = CHUNKS[h]
-            return result[o, t0 // BANK][:, n, t0 % BANK : t0 % BANK + width]
+            return result[o, t0 // BANK][:, tiles, t0 % BANK : t0 % BANK + width]
 
-        def load_x(x, h):
+        raw = {}
+
+        def load_x(x, h, c0=0, c1=None):
             t0, width = CHUNKS[h]
-            src = x_hbm[x].rearrange("(p j) t -> p j t", j=PACK)[:, :, t0 : t0 + width]
-            nc.sync.dma_start(out=raw[x, h][:], in_=src)
+            c1 = width if c1 is None else c1
+            raw[x, h, c0] = sbuf("raw_%s%d_%d" % (x, h, c0), [P, PACK, c1 - c0], F32)
+            src = x_hbm[x].rearrange("(p j) t -> p j t", j=PACK)[:, :, t0 + c0 : t0 + c1]
+            nc.sync.dma_start(out=raw[x, h, c0][:], in_=src)
 
         def load_words(w):
             nc.sync.dma_start(out=landed[w][:].bitcast(I32), in_=words_hbm[w].bitcast(I32))
-
-        def stage_first_scales():
-            nc.sync.dma_start(
-                out=staged[:PACK, :, :].bitcast(I32),
-                in_=scales_hbm["k"].bitcast(I32).rearrange("(q r) n -> r q n", r=PACK),
-            )
-
-        def place_first_scales():
-            for q in range(1, QUADS):
-                nc.vector.tensor_copy(
-                    out=staged[QUAD * q : QUAD * q + PACK, 0, :].bitcast(I32),
-                    in_=staged[:PACK, q, :].bitcast(I32),
-                )
-
-        def stage_late_scales(w):
-            nc.sync.dma_start(out=placed[w][0:P:8, :].bitcast(I32), in_=scales_hbm[w].bitcast(I32))
-
-        def place_late_scales(r):
-            nc.sync.dma_start(
-                out=late_planes[r:P:QUAD, :].bitcast(I32), in_=late_planes[8 * r : P : QUAD, :].bitcast(I32),
-            )
 
         def deal(dst, src, run):
             return (
@@ -161,54 +138,64 @@ def tile_mix_quat_bias_kernel(
                 dst, src = deal(w_words[w][:].bitcast(I32), landed[w][:].bitcast(I32), RUN)
                 nc.vector.tensor_copy(out=dst, in_=src)
 
-        def load_bias(o):
-            nc.sync.dma_start(out=bias_rows[PARTS.index(o) : P : QUAD, :], in_=bias_hbm[o].rearrange("(q c) -> q c", q=QUADS))
-
-        def turn_biases():
-            nc.vector.tensor_copy(
-                out=bias_dealt[:].rearrange("p (j c) -> p j c", j=TILES),
-                in_=bias_rows[:].rearrange("p (c j) -> p j c", j=TILES),
-            )
-            nc.vector.transpose(bias_cols[:], bias_dealt[:])
-
         def bias(o, n):
-            col = QUAD * n + PARTS.index(o)
-            return bias_cols[:, col : col + 1]
+            return bias_cols[o][:, n : n + 1]
 
-        def cast(engine, x, h, c0, c1):
-            src = raw[x, h][:, :, c0:c1].rearrange("p j (c i) -> p c j i", i=RUN)
-            dst = grouped[x, h][:, c0 * PACK : c1 * PACK].rearrange("p (c i j) -> p c j i", i=RUN, j=PACK)
-            if engine == "scalar":
-                nc.scalar.copy(out=dst, in_=src)
+        def cast(engine, dst, src):
+            if engine == "gpsimd":
+                nc.gpsimd.tensor_scalar(
+                    out=dst.rearrange("p (c j) -> p c j", j=PACK), in0=src.rearrange("p j c -> p c j"),
+                    scalar1=1.0, scalar2=0.0, op0=MULT, op1=ADD,
+                )
             else:
-                nc.vector.tensor_copy(out=dst, in_=src)
+                src = src.rearrange("p j (c i) -> p c j i", i=RUN)
+                dst = dst.rearrange("p (c i j) -> p c j i", i=RUN, j=PACK)
+                if engine == "scalar":
+                    nc.scalar.copy(out=dst, in_=src)
+                else:
+                    nc.vector.tensor_copy(out=dst, in_=src)
 
-        def cast_on_gpsimd(x, h, c0, c1):
-            nc.gpsimd.tensor_scalar(
-                out=grouped[x, h][:, c0 * PACK : c1 * PACK].rearrange("p (c j) -> p c j", j=PACK),
-                in0=raw[x, h][:, :, c0:c1].rearrange("p j c -> p c j"),
-                scalar1=1.0, scalar2=0.0, op0=MULT, op1=ADD,
-            )
+        grouped = {}
 
-        def share_cast(x, h, split, c0=0, c1=None):
-            c1 = CHUNKS[h][1] if c1 is None else c1
-            if split < c1:
-                cast("scalar", x, h, split, c1)
-            if split > c0:
-                cast("vector", x, h, c0, split)
+        def cast_shared(x, h, c0=0, share=0, tag=""):
+            src = raw[x, h, c0]
+            width = src.shape[2]
+            grouped[x, h, c0] = dst = sbuf("grouped_%s%d_%d" % (x, h, c0), [P, width * PACK], BF16, tag)
+            if share < width:
+                cast("scalar", dst[:, share * PACK :], src[:, :, share:])
+            if share > 0:
+                cast("vector", dst[:, : share * PACK], src[:, :, :share])
 
-        def quantize(x, h, c0=0, c1=None):
-            c1 = CHUNKS[h][1] if c1 is None else c1
-            nc.vector.quantize_mx(
-                out=x_codes[x, h][:, c0:c1].bitcast(FP8X4),
-                scales=x_scales[x, h][:, c0:c1],
-                in_=grouped[x, h][:, c0 * PACK : c1 * PACK],
-            )
+        def cast_and_quantize_quickly(x):
+            src = raw[x, FIRST, 0]
+            dst = sbuf("grouped_%s" % x, [P, HALF * PACK], BF16)
+            cast("scalar", dst[:, QUICK_SPLIT * PACK :], src[:, :, QUICK_SPLIT:])
+            for c0, c1 in ((0, P), (P, QUICK_SPLIT)):
+                cast("vector", dst[:, c0 * PACK : c1 * PACK], src[:, :, c0:c1])
+            for c0 in (0, P):
+                grouped[x, FIRST, c0] = dst[:, c0 * PACK : (c0 + P) * PACK]
+                quantize(x, FIRST, c0)
+
+        def cast_half(engine, x, h, side=None):
+            half = CHUNKS[h][1] // 2
+            c0 = half * (int(engine == "scalar") if side is None else side)
+            name = "grouped_%s%d_%d" % (x, h, c0)
+            grouped[x, h, c0] = dst = sbuf(name, [P, half * PACK], BF16, "by_gpsimd" if engine == "gpsimd" and c0 == 0 else name)
+            cast(engine, dst[:], raw[x, h, 0][:, :, c0 : c0 + half])
+
+        def quantize(x, h, c0=0):
+            src = grouped[x, h, c0]
+            c1 = c0 + src.shape[1] // PACK
+            nc.vector.quantize_mx(out=x_codes[x, h][:, c0:c1].bitcast(FP8X4), scales=x_scales[x, h][:, c0:c1], in_=src[:])
+
+        def quantize_halves(x, h):
+            quantize(x, h, 0)
+            quantize(x, h, CHUNKS[h][1] // 2)
 
         free_banks = list(range(BANKS))
         held = {}
         parked = {}
-        head_tags = ["zeros", "warm_codes", "landed_r", "landed_i", "staged"]
+        cols_left = {}
 
         def take_bank(key):
             bank = free_banks[0]
@@ -229,19 +216,18 @@ def tile_mix_quat_bias_kernel(
                 stop=stop,
             )
 
-        terms_left = {}
-
-        def add_term(name, x, n, h):
+        def add_term(name, x, n, h, cols=None):
             key = name, n, h
+            width = CHUNKS[h][1]
+            cols = cols or slice(0, width)
             opening = key not in held
             if opening:
                 take_bank(key)
-                terms_left[key] = len(WEIGHT[name])
-            terms_left[key] = terms_left[key] - 1
-            tiles = BANK // CHUNKS[h][1]
-            for side in range(tiles):
-                mx_pass(key, side * HALF, WEIGHT[name][x], n + side, x, h,
-                        opening and side == 0, terms_left[key] == 0 and side == tiles - 1)
+                cols_left[key] = len(WEIGHT[name]) * BANK
+            for side in range(BANK // width):
+                cols_left[key] = cols_left[key] - (cols.stop - cols.start)
+                mx_pass(key, side * width + cols.start, WEIGHT[name][x], n + side, x, h,
+                        opening and side == 0, cols_left[key] == 0, cols)
 
         def twin(names, n, h, first=0, last=None):
             key = names, n, h
@@ -260,36 +246,34 @@ def tile_mix_quat_bias_kernel(
                 return [(name, n), (name, n + 1)]
             return [(name[0], n), (name[1], n)]
 
-        def park(name, n, h):
+        def park(name, n, h, engine="scalar"):
             key = name, n, h
             bank, acc = held[key]
-            t0, width = CHUNKS[h]
-            if h == WIDE:
-                spot = result_cols(name[1], n, h)
+            sides = sides_of(key)
+            if h == SECOND:
+                spot = sbuf("spare_%s%d" % (sides[0][0], n), [P, 2, HALF], F32)[:]
             else:
-                label = "spare_%s%d%d" % (sides_of(key)[0][0], n, h)
-                tag = label
-                if h == SECOND and head_tags:
-                    tag = head_tags[0]
-                    head_tags.remove(tag)
-                spare = sb.tile([P, BANK], F32, name=label, tag=tag, align_bytes=ALIGN)
-                spot = spare[:]
-            nc.scalar.copy(out=spot, in_=acc[:])
-            for side, (s, m) in enumerate(sides_of(key)):
-                parked[s, m, h] = spot[:, side * width : (side + 1) * width]
+                spot = result_cols(name[1], slice(n, n + len(sides)), h)
+            src = acc[:].rearrange("p (s c) -> p s c", s=len(sides))
+            if engine == "scalar":
+                nc.scalar.copy(out=spot, in_=src)
+            else:
+                nc.vector.tensor_copy(out=spot, in_=src)
+            for side, (s, m) in enumerate(sides):
+                parked[s, m, h] = spot[:, side, :]
             free_banks.append(bank)
 
         def store(o, half, tiles=slice(0, TILES), cols=slice(0, BANK)):
             rows = out_hbm[o].rearrange("(p j) t -> p j t", j=TILES)[:, :, half * BANK : (half + 1) * BANK]
             nc.sync.dma_start(out=rows[:, tiles, cols], in_=result[o, half][:, tiles, cols])
 
-        def combine(name, n, h, from_psum=True):
+        def combine(name, n, h):
             key = name, n, h
             bank, acc = held[key]
-            t0, width = CHUNKS[h]
+            width = CHUNKS[h][1]
             for side, (s, m) in enumerate(sides_of(key)):
                 o = s[1]
-                mine = acc[:, side * width : (side + 1) * width] if from_psum else parked[s, m, h]
+                mine = acc[:, side * width : (side + 1) * width]
                 if s[0] == "p":
                     plus, minus = mine, parked["m" + o, m, h]
                 else:
@@ -297,8 +281,7 @@ def tile_mix_quat_bias_kernel(
                 nc.vector.scalar_tensor_tensor(
                     out=result_cols(o, m, h), in0=plus, scalar=bias(o, m), in1=minus, op0=ADD, op1=SUB,
                 )
-            if from_psum:
-                free_banks.append(bank)
+            free_banks.append(bank)
 
         def close_piece(name, n, cols):
             o = name[1]
@@ -319,34 +302,45 @@ def tile_mix_quat_bias_kernel(
 
         pairs = range(0, TILES, 2)
 
+        def terms(name, x, h, cols=None, drain=None):
+            for n in pairs if h == FIRST else range(TILES):
+                add_term(name, x, n, h, cols)
+                if drain:
+                    drain(name, n, h)
+
         nc.vector.memset(placed["k"].bitcast(I32), 0)
         nc.vector.memset(late_planes[:].bitcast(I32), 0)
         nc.vector.memset(zeros[:].bitcast(I32), 0)
-        nc.vector.memset(bias_rows[:], 0.0)
         load_words("k")
-        stage_first_scales()
-        load_x("r", FIRST)
+        nc.sync.dma_start(
+            out=staged[:PACK, :, :].bitcast(I32),
+            in_=scales_hbm["k"].bitcast(I32).rearrange("(q r) n -> r q n", r=PACK),
+        )
         for w in LATE:
-            stage_late_scales(w)
-        load_x("j", FIRST)
+            nc.sync.dma_start(out=placed[w][0:P:8, :].bitcast(I32), in_=scales_hbm[w].bitcast(I32))
+        load_x("r", FIRST)
         load_words("j")
+        deal_words("k", "scalar")
         for r in range(1, PACK):
-            place_late_scales(r)
+            nc.sync.dma_start(
+                out=late_planes[r:P:QUAD, :].bitcast(I32), in_=late_planes[8 * r : P : QUAD, :].bitcast(I32),
+            )
+        load_x("j", FIRST, 0, P)
+        load_x("j", FIRST, P, HALF)
         load_words("r")
-        load_x("k", FIRST)
         load_words("i")
+        load_x("k", FIRST)
         load_x("i", FIRST)
+        for x in PARTS:
+            load_x(x, SECOND)
+            nc.sync.dma_start(out=bias_cols[x][:], in_=bias_hbm[x].rearrange("(p j) -> p j", j=TILES))
+        for x in PARTS:
+            load_x(x, WIDE)
+
         for c0 in (0, HALF):
             nc.vector.quantize_mx(
                 out=warm_codes[:, c0 : c0 + HALF].bitcast(FP8X4), scales=warm_scales[:, c0 : c0 + HALF], in_=zeros[:],
             )
-        load_x("r", SECOND)
-        for o in PARTS:
-            load_bias(o)
-        for x in PARTS[1:]:
-            load_x(x, SECOND)
-        for x in PARTS:
-            load_x(x, WIDE)
         warm_bank = ps.tile([P, BANK], F32, name="bank%d" % (BANKS - 1))
         for rep in range(WARM_PASSES):
             nc.tensor.matmul_mx(
@@ -354,103 +348,90 @@ def tile_mix_quat_bias_kernel(
                 rhs=warm_codes[:].bitcast(FP8X4), rhs_scale=warm_scales[:], start=True, stop=True,
             )
 
-        deal_words("k", "scalar")
-        place_first_scales()
+        for q in range(1, QUADS):
+            nc.vector.tensor_copy(
+                out=staged[QUAD * q : QUAD * q + PACK, 0, :].bitcast(I32), in_=staged[:PACK, q, :].bitcast(I32),
+            )
         deal_scales("k")
-        share_cast("r", FIRST, 144)
-        quantize("r", FIRST)
-        share_cast("j", FIRST, 144)
-        quantize("j", FIRST)
+        cast_and_quantize_quickly("r")
         deal_words("j", "scalar")
         deal_scales("j")
-        for n in pairs:
-            add_term("pk", "r", n, FIRST)
-        for n in pairs:
-            add_term("mi", "j", n, FIRST)
+        terms("pk", "r", FIRST)
+        terms("pj", "r", FIRST)
+        cast_shared("j", FIRST, 0, P)
+        quantize("j", FIRST, 0)
+        cast_shared("j", FIRST, P, P // 2)
+        quantize("j", FIRST, P)
         deal_scales("r")
-        deal_words("r", "vector")
-        for n in pairs:
-            park("mi", n, FIRST)
-        for n in range(TILES):
-            twin(("pj", "mr"), n, FIRST, 0, 1)
-        share_cast("k", FIRST, 144)
+        for c0 in (0, P):
+            for name in ("mi", "mr"):
+                terms(name, "j", FIRST, slice(c0, c0 + P))
+        deal_words("r", "scalar")
         deal_scales("i")
-        quantize("k", FIRST)
-        deal_words("i", "vector")
-        for n in range(TILES):
-            twin(("pj", "mr"), n, FIRST, 1, 2)
-        for n in pairs:
-            add_term("pr", "r", n, FIRST)
-            park("pr", n, FIRST)
-        for n in pairs:
-            add_term("pk", "k", n, FIRST)
-        share_cast("i", FIRST, 256)
+        deal_words("i", "scalar")
+        park("mi", 0, FIRST, "vector")
+        park("mi", 2, FIRST)
+        terms("pj", "j", FIRST)
+        cast_and_quantize_quickly("k")
+        terms("pr", "r", FIRST, drain=park)
+        terms("pk", "j", FIRST)
+        cast_shared("i", FIRST, 0, HALF)
         quantize("i", FIRST)
-        for n in pairs:
-            add_term("pk", "j", n, FIRST)
-            park("pk", n, FIRST)
-        for x in "rk":
-            for n in pairs:
-                add_term("pi", x, n, FIRST)
-        share_cast("r", SECOND, 256)
-        turn_biases()
+        terms("pk", "k", FIRST, drain=park)
+        terms("mr", "k", FIRST)
+        cast_shared("r", SECOND, 0, HALF)
         quantize("r", SECOND)
+        terms("mj", "k", FIRST, drain=park)
+        terms("mr", "i", FIRST)
+        cast_shared("j", SECOND, 0, P)
         for n in pairs:
-            add_term("mj", "k", n, FIRST)
-            park("mj", n, FIRST)
-        cast("scalar", "j", SECOND, 128, HALF)
-        for n in pairs:
-            add_term("pi", "i", n, FIRST)
-            combine("pi", n, FIRST)
-            if n == 0:
-                cast("vector", "j", SECOND, 0, 128)
+            combine("mr", n, FIRST)
         quantize("j", SECOND)
-        share_cast("k", SECOND, 0)
-        share_cast("i", SECOND, 0)
-        for n in range(TILES):
-            twin(("pj", "mr"), n, FIRST, 2, 4)
-            if n < TILES - 1:
-                combine(("pj", "mr"), n, FIRST)
-            if n == 0:
-                quantize("k", SECOND)
-        quantize("i", SECOND)
+        cast_shared("k", SECOND, 0, 0)
+        terms("pj", "i", FIRST)
+        terms("mk", "i", FIRST)
+        for x in "rki":
+            terms("pi", x, FIRST)
         for n in pairs:
-            add_term("mk", "i", n, FIRST)
+            combine("pj", n, FIRST)
+        quantize("k", SECOND)
+        cast_shared("i", SECOND, 0, 0, "by_gpsimd")
+        combine("mk", 0, FIRST)
+        quantize("i", SECOND)
+        for side in range(2):
+            cast_half("gpsimd", "r", WIDE, side)
+        combine("mk", 2, FIRST)
 
-        for n in range(TILES - 1):
+        for n in range(TILES // 2):
             twin(("pk", "mi"), n, SECOND, 0, 2)
         for n in range(TILES):
-            twin(("pk", "mi"), n, SECOND, 2 if n < TILES - 1 else 0, 3)
-            if n == TILES - 1:
-                for m in pairs:
-                    combine("mk", m, FIRST)
+            twin(("pk", "mi"), n, SECOND, 2 if n < TILES // 2 else 0, 3)
             park(("pk", "mi"), n, SECOND)
-            if n == 0:
-                combine(("pj", "mr"), TILES - 1, FIRST)
-        for c0 in range(0, BANK, P):
-            cast_on_gpsimd("r", WIDE, c0, c0 + P)
+        for n in pairs:
+            combine("pi", n, FIRST)
         for n in range(TILES):
             twin(("pr", "mj"), n, SECOND)
             park(("pr", "mj"), n, SECOND)
             twin(("mk", "pi"), n, SECOND)
             combine(("mk", "pi"), n, SECOND)
+            if n == 0:
+                cast_half("scalar", "j", WIDE)
             if n == 1:
-                cast("scalar", "j", WIDE, 256, BANK)
+                quantize_halves("r", WIDE)
+                cast_half("gpsimd", "j", WIDE)
         store("k", 0)
         store("i", 0)
-        quantize("r", WIDE)
-        cast("vector", "j", WIDE, 0, 256)
-        share_cast("k", WIDE, 0)
+        cast_half("scalar", "k", WIDE)
         for n in range(TILES):
             twin(("pj", "mr"), n, SECOND)
             combine(("pj", "mr"), n, SECOND)
             if n == 0:
-                quantize("j", WIDE)
-            if n == 2:
-                quantize("k", WIDE)
+                quantize_halves("j", WIDE)
+                cast_half("gpsimd", "k", WIDE)
         store("j", 0)
         store("r", 0)
-        share_cast("i", WIDE, 256)
+        quantize_halves("k", WIDE)
+        cast_shared("i", WIDE, 0, 0)
         quantize("i", WIDE)
 
         def close_wide(name, n, drain):
@@ -459,15 +440,12 @@ def tile_mix_quat_bias_kernel(
             drain(name, n, WIDE)
 
         for x in "rj":
-            for n in range(TILES):
-                add_term("pk", x, n, WIDE)
+            terms("pk", x, WIDE)
         for n in range(TILES):
-            close_wide("mi", n, park)
-        for n in range(TILES):
-            add_term("pk", "k", n, WIDE)
-            park("pk", n, WIDE)
-        for n in range(TILES):
-            close_wide("mk", n, combine)
+            add_term("mi", "j", n, WIDE)
+            park("mi", n, WIDE, "vector" if n % 2 else "scalar")
+        terms("pk", "k", WIDE, drain=park)
+        terms("mk", "i", WIDE, drain=combine)
         store("k", 1)
         for n in range(TILES):
             close_wide("pi", n, combine)

@@ -29,7 +29,8 @@ ALIGN = 256
 RUN = 4
 LINE = 16
 PARTS = "rjki"
-LATE = "jri"
+EARLY = "kj"
+LATE = "ri"
 FIRST, SECOND, WIDE = 0, 1, 2
 CHUNKS = ((0, HALF), (HALF, HALF), (BANK, BANK))
 WARM_PASSES = 8
@@ -82,10 +83,12 @@ def tile_mix_quat_bias_kernel(
 
         landed = {w: sbuf("landed_" + w, [P, N * word_bytes[w]], U8) for w in PARTS}
         w_words = {w: sbuf("words_" + w, [P, N * word_bytes[w]], U8) for w in PARTS}
-        staged = sbuf("staged", [P, QUADS, N], U8)
+        staged = sbuf("staged", [PACK, QUADS, len(EARLY) * N], U8)
+        early_planes = sbuf("early_planes", [P, len(EARLY) * N], U8)
         late_planes = sbuf("late_planes", [P, len(LATE) * N], U8)
         placed = {w: late_planes[:, LATE.index(w) * N : (LATE.index(w) + 1) * N] for w in LATE}
-        placed["k"] = staged[:, 0, :]
+        for w in EARLY:
+            placed[w] = early_planes[:, EARLY.index(w) * N : (EARLY.index(w) + 1) * N]
         w_scales = {w: sbuf("plane_" + w, [P, N], U8) for w in PARTS}
         bias_cols = {o: sbuf("bias_" + o, [P, TILES], F32) for o in PARTS}
         zeros = sbuf("zeros", [P, HALF * PACK], BF16)
@@ -166,12 +169,15 @@ def tile_mix_quat_bias_kernel(
             if share > 0:
                 cast("vector", dst[:, : share * PACK], src[:, :, :share])
 
-        def cast_and_quantize_quickly(x):
+        def cast_and_quantize_quickly(x, split=QUICK_SPLIT, between=""):
             src = raw[x, FIRST, 0]
             dst = sbuf("grouped_%s" % x, [P, HALF * PACK], BF16)
-            cast("scalar", dst[:, QUICK_SPLIT * PACK :], src[:, :, QUICK_SPLIT:])
-            for c0, c1 in ((0, P), (P, QUICK_SPLIT)):
-                cast("vector", dst[:, c0 * PACK : c1 * PACK], src[:, :, c0:c1])
+            cast("scalar", dst[:, split * PACK :], src[:, :, split:])
+            for c0, c1 in ((0, P), (P, split)):
+                if c1 > c0:
+                    cast("vector", dst[:, c0 * PACK : c1 * PACK], src[:, :, c0:c1])
+            for w in between:
+                deal_scales(w)
             for c0 in (0, P):
                 grouped[x, FIRST, c0] = dst[:, c0 * PACK : (c0 + P) * PACK]
                 quantize(x, FIRST, c0)
@@ -308,26 +314,24 @@ def tile_mix_quat_bias_kernel(
                 if drain:
                     drain(name, n, h)
 
-        nc.vector.memset(placed["k"].bitcast(I32), 0)
-        nc.vector.memset(late_planes[:].bitcast(I32), 0)
         nc.vector.memset(zeros[:].bitcast(I32), 0)
+        nc.vector.memset(late_planes[:].bitcast(I32), 0)
+        for w in EARLY:
+            nc.sync.dma_start(
+                out=staged[:, :, EARLY.index(w) * N : (EARLY.index(w) + 1) * N].bitcast(I32),
+                in_=scales_hbm[w].bitcast(I32).rearrange("(q r) n -> r q n", r=PACK),
+            )
         load_words("k")
-        nc.sync.dma_start(
-            out=staged[:PACK, :, :].bitcast(I32),
-            in_=scales_hbm["k"].bitcast(I32).rearrange("(q r) n -> r q n", r=PACK),
-        )
-        for w in LATE:
-            nc.sync.dma_start(out=placed[w][0:P:8, :].bitcast(I32), in_=scales_hbm[w].bitcast(I32))
         load_x("r", FIRST)
         load_words("j")
-        deal_words("k", "scalar")
+        for w in LATE:
+            nc.sync.dma_start(out=placed[w][0:P:8, :].bitcast(I32), in_=scales_hbm[w].bitcast(I32))
+        load_x("j", FIRST)
+        load_words("r")
         for r in range(1, PACK):
             nc.sync.dma_start(
                 out=late_planes[r:P:QUAD, :].bitcast(I32), in_=late_planes[8 * r : P : QUAD, :].bitcast(I32),
             )
-        load_x("j", FIRST, 0, P)
-        load_x("j", FIRST, P, HALF)
-        load_words("r")
         load_words("i")
         load_x("k", FIRST)
         load_x("i", FIRST)
@@ -341,6 +345,7 @@ def tile_mix_quat_bias_kernel(
             nc.vector.quantize_mx(
                 out=warm_codes[:, c0 : c0 + HALF].bitcast(FP8X4), scales=warm_scales[:, c0 : c0 + HALF], in_=zeros[:],
             )
+        nc.vector.memset(early_planes[:].bitcast(I32), 0)
         warm_bank = ps.tile([P, BANK], F32, name="bank%d" % (BANKS - 1))
         for rep in range(WARM_PASSES):
             nc.tensor.matmul_mx(
@@ -348,24 +353,20 @@ def tile_mix_quat_bias_kernel(
                 rhs=warm_codes[:].bitcast(FP8X4), rhs_scale=warm_scales[:], start=True, stop=True,
             )
 
-        for q in range(1, QUADS):
+        for q in (1, 2, 3, 0):
             nc.vector.tensor_copy(
-                out=staged[QUAD * q : QUAD * q + PACK, 0, :].bitcast(I32), in_=staged[:PACK, q, :].bitcast(I32),
+                out=early_planes[QUAD * q : QUAD * q + PACK, :].bitcast(I32), in_=staged[:, q, :].bitcast(I32),
             )
-        deal_scales("k")
-        cast_and_quantize_quickly("r")
+        deal_words("k", "scalar")
+        cast_and_quantize_quickly("r", P, "k")
         deal_words("j", "scalar")
         deal_scales("j")
         terms("pk", "r", FIRST)
         terms("pj", "r", FIRST)
-        cast_shared("j", FIRST, 0, P)
-        quantize("j", FIRST, 0)
-        cast_shared("j", FIRST, P, P // 2)
-        quantize("j", FIRST, P)
+        cast_and_quantize_quickly("j")
         deal_scales("r")
-        for c0 in (0, P):
-            for name in ("mi", "mr"):
-                terms(name, "j", FIRST, slice(c0, c0 + P))
+        for name in ("mi", "mr"):
+            terms(name, "j", FIRST)
         deal_words("r", "scalar")
         deal_scales("i")
         deal_words("i", "scalar")

@@ -9,7 +9,6 @@ F32 = mybir.dt.float32
 BF16 = mybir.dt.bfloat16
 I32 = mybir.dt.int32
 U32 = mybir.dt.uint32
-U16 = mybir.dt.uint16
 U8 = mybir.dt.uint8
 FP8X4 = mybir.dt.float8_e4m3fn_x4
 FP4X4 = mybir.dt.float4_e2m1fn_x4
@@ -27,7 +26,6 @@ QUADS = 4
 QUAD = P // QUADS
 ALIGN = 256
 RUN = 4
-LINE = 16
 PARTS = "rjki"
 EARLY = "kj"
 LATE = "ri"
@@ -81,16 +79,15 @@ def tile_mix_quat_bias_kernel(
         def sbuf(name, shape, dtype, tag=""):
             return sb.tile(shape, dtype, name=name, tag=tag or name, align_bytes=ALIGN)
 
-        landed = {w: sbuf("landed_" + w, [P, N * word_bytes[w]], U8) for w in PARTS}
         w_words = {w: sbuf("words_" + w, [P, N * word_bytes[w]], U8) for w in PARTS}
         staged = sbuf("staged", [PACK, QUADS, len(EARLY) * N], U8)
         early_planes = sbuf("early_planes", [P, len(EARLY) * N], U8)
         late_planes = sbuf("late_planes", [P, len(LATE) * N], U8)
-        placed = {w: late_planes[:, LATE.index(w) * N : (LATE.index(w) + 1) * N] for w in LATE}
+        w_scales = {w: late_planes[:, LATE.index(w) * N : (LATE.index(w) + 1) * N] for w in LATE}
         for w in EARLY:
-            placed[w] = early_planes[:, EARLY.index(w) * N : (EARLY.index(w) + 1) * N]
-        w_scales = {w: sbuf("plane_" + w, [P, N], U8) for w in PARTS}
-        bias_cols = {o: sbuf("bias_" + o, [P, TILES], F32) for o in PARTS}
+            w_scales[w] = early_planes[:, EARLY.index(w) * N : (EARLY.index(w) + 1) * N]
+        bias_rows = sbuf("bias_rows", [P, QUAD], F32)
+        bias_cols = sbuf("bias_cols", [P, QUAD], F32)
         zeros = sbuf("zeros", [P, HALF * PACK], BF16)
         warm_codes = sbuf("warm_codes", [P, BANK], U32)
         warm_scales = sbuf("warm_scales", [P, BANK], U8)
@@ -120,29 +117,16 @@ def tile_mix_quat_bias_kernel(
             nc.sync.dma_start(out=raw[x, h, c0][:], in_=src)
 
         def load_words(w):
-            nc.sync.dma_start(out=landed[w][:].bitcast(I32), in_=words_hbm[w].bitcast(I32))
+            nc.sync.dma_start(out=w_words[w][:].bitcast(I32), in_=words_hbm[w].bitcast(I32))
 
-        def deal(dst, src, run):
-            return (
-                dst.rearrange("p (j c i) -> p c j i", j=TILES, i=run),
-                src.rearrange("p (c i j) -> p c j i", j=TILES, i=run),
+        def load_bias(o):
+            nc.sync.dma_start(
+                out=bias_rows[PARTS.index(o) : P : 8, :], in_=bias_hbm[o].rearrange("(n q c) -> q n c", n=TILES, q=QUADS),
             )
 
-        def deal_scales(w):
-            dst, src = deal(w_scales[w][:], placed[w], LINE)
-            nc.vector.tensor_copy(out=dst, in_=src)
-
-        def deal_words(w, engine):
-            if engine == "scalar":
-                word = U32 if word_bytes[w] == 4 else U16
-                dst, src = deal(w_words[w][:].bitcast(word), landed[w][:].bitcast(word), LINE // word_bytes[w])
-                nc.scalar.copy(out=dst, in_=src)
-            else:
-                dst, src = deal(w_words[w][:].bitcast(I32), landed[w][:].bitcast(I32), RUN)
-                nc.vector.tensor_copy(out=dst, in_=src)
-
         def bias(o, n):
-            return bias_cols[o][:, n : n + 1]
+            col = 8 * n + PARTS.index(o)
+            return bias_cols[:, col : col + 1]
 
         def cast(engine, dst, src):
             if engine == "gpsimd":
@@ -169,15 +153,13 @@ def tile_mix_quat_bias_kernel(
             if share > 0:
                 cast("vector", dst[:, : share * PACK], src[:, :, :share])
 
-        def cast_and_quantize_quickly(x, split=QUICK_SPLIT, between=""):
+        def cast_and_quantize_quickly(x, split=QUICK_SPLIT):
             src = raw[x, FIRST, 0]
             dst = sbuf("grouped_%s" % x, [P, HALF * PACK], BF16)
             cast("scalar", dst[:, split * PACK :], src[:, :, split:])
             for c0, c1 in ((0, P), (P, split)):
                 if c1 > c0:
                     cast("vector", dst[:, c0 * PACK : c1 * PACK], src[:, :, c0:c1])
-            for w in between:
-                deal_scales(w)
             for c0 in (0, P):
                 grouped[x, FIRST, c0] = dst[:, c0 * PACK : (c0 + P) * PACK]
                 quantize(x, FIRST, c0)
@@ -269,9 +251,9 @@ def tile_mix_quat_bias_kernel(
                 parked[s, m, h] = spot[:, side, :]
             free_banks.append(bank)
 
-        def store(o, half, tiles=slice(0, TILES), cols=slice(0, BANK)):
-            rows = out_hbm[o].rearrange("(p j) t -> p j t", j=TILES)[:, :, half * BANK : (half + 1) * BANK]
-            nc.sync.dma_start(out=rows[:, tiles, cols], in_=result[o, half][:, tiles, cols])
+        def store(o, half, n, cols=slice(0, BANK)):
+            rows = out_hbm[o][n * P : (n + 1) * P, half * BANK : (half + 1) * BANK]
+            nc.sync.dma_start(out=rows[:, cols], in_=result[o, half][:, n, cols])
 
         def combine(name, n, h):
             key = name, n, h
@@ -303,7 +285,7 @@ def tile_mix_quat_bias_kernel(
                 nc.scalar.copy(out=spot, in_=sums)
             else:
                 nc.vector.scalar_tensor_tensor(out=spot, in0=spot, scalar=bias(o, n), in1=sums, op0=ADD, op1=SUB)
-                store(o, 1, slice(n, n + 1), cols)
+                store(o, 1, n, cols)
             free_banks.append(bank)
 
         pairs = range(0, TILES, 2)
@@ -314,30 +296,35 @@ def tile_mix_quat_bias_kernel(
                 if drain:
                     drain(name, n, h)
 
-        nc.vector.memset(zeros[:].bitcast(I32), 0)
         nc.vector.memset(late_planes[:].bitcast(I32), 0)
+        nc.vector.memset(zeros[:].bitcast(I32), 0)
+        nc.vector.memset(bias_rows[:], 0.0)
         for w in EARLY:
             nc.sync.dma_start(
                 out=staged[:, :, EARLY.index(w) * N : (EARLY.index(w) + 1) * N].bitcast(I32),
                 in_=scales_hbm[w].bitcast(I32).rearrange("(q r) n -> r q n", r=PACK),
             )
-        load_words("k")
-        load_x("r", FIRST)
-        load_words("j")
         for w in LATE:
-            nc.sync.dma_start(out=placed[w][0:P:8, :].bitcast(I32), in_=scales_hbm[w].bitcast(I32))
+            nc.sync.dma_start(out=w_scales[w][0:P:8, :].bitcast(I32), in_=scales_hbm[w].bitcast(I32))
+        load_x("r", FIRST)
+        load_words("k")
         load_x("j", FIRST)
-        load_words("r")
+        load_words("j")
         for r in range(1, PACK):
             nc.sync.dma_start(
                 out=late_planes[r:P:QUAD, :].bitcast(I32), in_=late_planes[8 * r : P : QUAD, :].bitcast(I32),
             )
+        load_words("r")
         load_words("i")
         load_x("k", FIRST)
+        load_bias("r")
         load_x("i", FIRST)
-        for x in PARTS:
+        load_bias("j")
+        load_bias("k")
+        load_x("r", SECOND)
+        load_bias("i")
+        for x in PARTS[1:]:
             load_x(x, SECOND)
-            nc.sync.dma_start(out=bias_cols[x][:], in_=bias_hbm[x].rearrange("(p j) -> p j", j=TILES))
         for x in PARTS:
             load_x(x, WIDE)
 
@@ -357,19 +344,12 @@ def tile_mix_quat_bias_kernel(
             nc.vector.tensor_copy(
                 out=early_planes[QUAD * q : QUAD * q + PACK, :].bitcast(I32), in_=staged[:, q, :].bitcast(I32),
             )
-        deal_words("k", "scalar")
-        cast_and_quantize_quickly("r", P, "k")
-        deal_words("j", "scalar")
-        deal_scales("j")
+        cast_and_quantize_quickly("r")
         terms("pk", "r", FIRST)
         terms("pj", "r", FIRST)
         cast_and_quantize_quickly("j")
-        deal_scales("r")
         for name in ("mi", "mr"):
             terms(name, "j", FIRST)
-        deal_words("r", "scalar")
-        deal_scales("i")
-        deal_words("i", "scalar")
         park("mi", 0, FIRST, "vector")
         park("mi", 2, FIRST)
         terms("pj", "j", FIRST)
@@ -381,6 +361,7 @@ def tile_mix_quat_bias_kernel(
         terms("pk", "k", FIRST, drain=park)
         terms("mr", "k", FIRST)
         cast_shared("r", SECOND, 0, HALF)
+        nc.vector.transpose(bias_cols[:], bias_rows[:])
         quantize("r", SECOND)
         terms("mj", "k", FIRST, drain=park)
         terms("mr", "i", FIRST)
@@ -415,22 +396,22 @@ def tile_mix_quat_bias_kernel(
             park(("pr", "mj"), n, SECOND)
             twin(("mk", "pi"), n, SECOND)
             combine(("mk", "pi"), n, SECOND)
+            for o in "ki":
+                store(o, 0, n)
             if n == 0:
                 cast_half("scalar", "j", WIDE)
             if n == 1:
                 quantize_halves("r", WIDE)
                 cast_half("gpsimd", "j", WIDE)
-        store("k", 0)
-        store("i", 0)
         cast_half("scalar", "k", WIDE)
         for n in range(TILES):
             twin(("pj", "mr"), n, SECOND)
             combine(("pj", "mr"), n, SECOND)
+            for o in "jr":
+                store(o, 0, n)
             if n == 0:
                 quantize_halves("j", WIDE)
                 cast_half("gpsimd", "k", WIDE)
-        store("j", 0)
-        store("r", 0)
         quantize_halves("k", WIDE)
         cast_shared("i", WIDE, 0, 0)
         quantize("i", WIDE)
@@ -446,20 +427,18 @@ def tile_mix_quat_bias_kernel(
             add_term("mi", "j", n, WIDE)
             park("mi", n, WIDE, "vector" if n % 2 else "scalar")
         terms("pk", "k", WIDE, drain=park)
-        terms("mk", "i", WIDE, drain=combine)
-        store("k", 1)
-        for n in range(TILES):
-            close_wide("pi", n, combine)
-        store("i", 1)
+        for name in ("mk", "pi"):
+            for n in range(TILES):
+                close_wide(name, n, combine)
+                store(name[1], 1, n)
         for n in range(TILES):
             close_wide("mj", n, park)
             close_wide("pj", n, combine)
-            if n % 2 == 1:
-                store("j", 1, slice(n - 1, n + 1))
+            store("j", 1, n)
         for n in range(TILES // 2):
             close_wide("pr", n, park)
             close_wide("mr", n, combine)
-            store("r", 1, slice(n, n + 1))
+            store("r", 1, n)
         for n, c0, c1 in ((2, 0, 256), (2, 256, 512), (3, 0, 256), (3, 256, 384), (3, 384, 512)):
             for name in ("pr", "mr"):
                 close_piece(name, n, slice(c0, c1))

@@ -31,7 +31,7 @@ EARLY = "kj"
 LATE = "ri"
 FIRST, SECOND, WIDE = 0, 1, 2
 CHUNKS = ((0, HALF), (HALF, HALF), (BANK, BANK))
-WARM_PASSES = 8
+WARM_PASSES = 6
 QUICK_SPLIT = 192
 
 WEIGHT = {
@@ -82,7 +82,8 @@ def tile_mix_quat_bias_kernel(
         w_words = {w: sbuf("words_" + w, [P, N * word_bytes[w]], U8) for w in PARTS}
         staged = sbuf("staged", [PACK, QUADS, len(EARLY) * N], U8)
         early_planes = sbuf("early_planes", [P, len(EARLY) * N], U8)
-        late_planes = sbuf("late_planes", [P, len(LATE) * N], U8)
+        late_staged = sbuf("late_staged", [P, QUADS, len(LATE) * N], U8)
+        late_planes = late_staged[:, 0, :]
         w_scales = {w: late_planes[:, LATE.index(w) * N : (LATE.index(w) + 1) * N] for w in LATE}
         for w in EARLY:
             w_scales[w] = early_planes[:, EARLY.index(w) * N : (EARLY.index(w) + 1) * N]
@@ -296,34 +297,37 @@ def tile_mix_quat_bias_kernel(
                 if drain:
                     drain(name, n, h)
 
-        nc.vector.memset(late_planes[:].bitcast(I32), 0)
+        def stage_scales(tile, weights):
+            for slot, w in enumerate(weights):
+                nc.sync.dma_start(
+                    out=tile[:PACK, :, slot * N : (slot + 1) * N].bitcast(I32),
+                    in_=scales_hbm[w].bitcast(I32).rearrange("(q r) n -> r q n", r=PACK),
+                )
+
+        def place_scales(planes, tile, quadrants):
+            for q in quadrants:
+                nc.vector.tensor_copy(
+                    out=planes[QUAD * q : QUAD * q + PACK, :].bitcast(I32), in_=tile[:PACK, q, :].bitcast(I32),
+                )
+
         nc.vector.memset(zeros[:].bitcast(I32), 0)
-        nc.vector.memset(bias_rows[:], 0.0)
-        for w in EARLY:
-            nc.sync.dma_start(
-                out=staged[:, :, EARLY.index(w) * N : (EARLY.index(w) + 1) * N].bitcast(I32),
-                in_=scales_hbm[w].bitcast(I32).rearrange("(q r) n -> r q n", r=PACK),
-            )
-        for w in LATE:
-            nc.sync.dma_start(out=w_scales[w][0:P:8, :].bitcast(I32), in_=scales_hbm[w].bitcast(I32))
+        nc.vector.memset(late_planes.bitcast(I32), 0)
+        stage_scales(staged, EARLY)
         load_x("r", FIRST)
         load_words("k")
         load_x("j", FIRST)
         load_words("j")
-        for r in range(1, PACK):
-            nc.sync.dma_start(
-                out=late_planes[r:P:QUAD, :].bitcast(I32), in_=late_planes[8 * r : P : QUAD, :].bitcast(I32),
-            )
+        stage_scales(late_staged, LATE)
         load_words("r")
         load_words("i")
         load_x("k", FIRST)
+        nc.vector.memset(bias_rows[:], 0.0)
         load_bias("r")
-        load_x("i", FIRST)
         load_bias("j")
+        load_x("i", FIRST)
         load_bias("k")
-        load_x("r", SECOND)
         load_bias("i")
-        for x in PARTS[1:]:
+        for x in PARTS:
             load_x(x, SECOND)
         for x in PARTS:
             load_x(x, WIDE)
@@ -340,55 +344,53 @@ def tile_mix_quat_bias_kernel(
                 rhs=warm_codes[:].bitcast(FP8X4), rhs_scale=warm_scales[:], start=True, stop=True,
             )
 
-        for q in (1, 2, 3, 0):
-            nc.vector.tensor_copy(
-                out=early_planes[QUAD * q : QUAD * q + PACK, :].bitcast(I32), in_=staged[:, q, :].bitcast(I32),
-            )
+        place_scales(early_planes, staged, (1, 2, 3, 0))
         cast_and_quantize_quickly("r")
         terms("pk", "r", FIRST)
         terms("pj", "r", FIRST)
         cast_and_quantize_quickly("j")
-        for name in ("mi", "mr"):
-            terms(name, "j", FIRST)
-        park("mi", 0, FIRST, "vector")
-        park("mi", 2, FIRST)
+        place_scales(late_planes, late_staged, (1, 2, 3))
+        terms("mi", "j", FIRST, drain=park)
+        terms("mr", "j", FIRST)
         terms("pj", "j", FIRST)
+        terms("pk", "j", FIRST)
         cast_and_quantize_quickly("k")
         terms("pr", "r", FIRST, drain=park)
-        terms("pk", "j", FIRST)
         cast_shared("i", FIRST, 0, HALF)
+        nc.vector.transpose(bias_cols[:], bias_rows[:])
         quantize("i", FIRST)
         terms("pk", "k", FIRST, drain=park)
         terms("mr", "k", FIRST)
         cast_shared("r", SECOND, 0, HALF)
-        nc.vector.transpose(bias_cols[:], bias_rows[:])
-        quantize("r", SECOND)
         terms("mj", "k", FIRST, drain=park)
         terms("mr", "i", FIRST)
+        quantize("r", SECOND)
         cast_shared("j", SECOND, 0, P)
         for n in pairs:
             combine("mr", n, FIRST)
         quantize("j", SECOND)
-        cast_shared("k", SECOND, 0, 0)
+        cast_shared("k", SECOND)
         terms("pj", "i", FIRST)
         terms("mk", "i", FIRST)
         for x in "rki":
             terms("pi", x, FIRST)
         for n in pairs:
             combine("pj", n, FIRST)
-        quantize("k", SECOND)
+            if n == 0:
+                quantize("k", SECOND)
         cast_shared("i", SECOND, 0, 0, "by_gpsimd")
         combine("mk", 0, FIRST)
         quantize("i", SECOND)
         for side in range(2):
             cast_half("gpsimd", "r", WIDE, side)
-        combine("mk", 2, FIRST)
 
         for n in range(TILES // 2):
             twin(("pk", "mi"), n, SECOND, 0, 2)
         for n in range(TILES):
             twin(("pk", "mi"), n, SECOND, 2 if n < TILES // 2 else 0, 3)
             park(("pk", "mi"), n, SECOND)
+            if n == 0:
+                combine("mk", 2, FIRST)
         for n in pairs:
             combine("pi", n, FIRST)
         for n in range(TILES):
@@ -400,20 +402,19 @@ def tile_mix_quat_bias_kernel(
                 store(o, 0, n)
             if n == 0:
                 cast_half("scalar", "j", WIDE)
-            if n == 1:
+            if n == 2:
                 quantize_halves("r", WIDE)
                 cast_half("gpsimd", "j", WIDE)
-        cast_half("scalar", "k", WIDE)
+        cast_shared("k", WIDE)
         for n in range(TILES):
             twin(("pj", "mr"), n, SECOND)
             combine(("pj", "mr"), n, SECOND)
             for o in "jr":
                 store(o, 0, n)
-            if n == 0:
+            if n == 1:
                 quantize_halves("j", WIDE)
-                cast_half("gpsimd", "k", WIDE)
-        quantize_halves("k", WIDE)
-        cast_shared("i", WIDE, 0, 0)
+        quantize("k", WIDE)
+        cast_shared("i", WIDE, 0, P)
         quantize("i", WIDE)
 
         def close_wide(name, n, drain):

@@ -28,10 +28,10 @@ ALIGN = 256
 RUN = 4
 PARTS = "rjki"
 EARLY = "kj"
-LATE = "ri"
+LATE_ROW = {"r": 4, "i": 8}
 FIRST, SECOND, WIDE = 0, 1, 2
 CHUNKS = ((0, HALF), (HALF, HALF), (BANK, BANK))
-WARM_PASSES = 6
+WARM_PASSES = 7
 QUICK_SPLIT = 192
 
 WEIGHT = {
@@ -82,9 +82,9 @@ def tile_mix_quat_bias_kernel(
         w_words = {w: sbuf("words_" + w, [P, N * word_bytes[w]], U8) for w in PARTS}
         staged = sbuf("staged", [PACK, QUADS, len(EARLY) * N], U8)
         early_planes = sbuf("early_planes", [P, len(EARLY) * N], U8)
-        late_staged = sbuf("late_staged", [P, QUADS, len(LATE) * N], U8)
+        late_staged = sbuf("late_staged", [P, QUADS, N], U8)
         late_planes = late_staged[:, 0, :]
-        w_scales = {w: late_planes[:, LATE.index(w) * N : (LATE.index(w) + 1) * N] for w in LATE}
+        w_scales = {w: late_planes[LATE_ROW[w] :, :] for w in LATE_ROW}
         for w in EARLY:
             w_scales[w] = early_planes[:, EARLY.index(w) * N : (EARLY.index(w) + 1) * N]
         bias_rows = sbuf("bias_rows", [P, QUAD], F32)
@@ -297,31 +297,36 @@ def tile_mix_quat_bias_kernel(
                 if drain:
                     drain(name, n, h)
 
-        def stage_scales(tile, weights):
-            for slot, w in enumerate(weights):
-                nc.sync.dma_start(
-                    out=tile[:PACK, :, slot * N : (slot + 1) * N].bitcast(I32),
-                    in_=scales_hbm[w].bitcast(I32).rearrange("(q r) n -> r q n", r=PACK),
-                )
+        def stage_scales(w, rows):
+            nc.sync.dma_start(
+                out=rows.bitcast(I32), in_=scales_hbm[w].bitcast(I32).rearrange("(q r) n -> r q n", r=PACK),
+            )
 
-        def place_scales(planes, tile, quadrants):
+        def place_scales(planes, tile, quadrants, rows):
             for q in quadrants:
                 nc.vector.tensor_copy(
-                    out=planes[QUAD * q : QUAD * q + PACK, :].bitcast(I32), in_=tile[:PACK, q, :].bitcast(I32),
+                    out=planes[QUAD * q : QUAD * q + rows, :].bitcast(I32), in_=tile[:rows, q, :].bitcast(I32),
                 )
 
         nc.vector.memset(zeros[:].bitcast(I32), 0)
-        nc.vector.memset(late_planes.bitcast(I32), 0)
-        stage_scales(staged, EARLY)
+        for slot, w in enumerate(EARLY):
+            stage_scales(w, staged[:, :, slot * N : (slot + 1) * N])
+        for c0 in (0, HALF):
+            nc.vector.quantize_mx(
+                out=warm_codes[:, c0 : c0 + HALF].bitcast(FP8X4), scales=warm_scales[:, c0 : c0 + HALF], in_=zeros[:],
+            )
+        nc.vector.memset(late_staged[:].bitcast(I32), 0)
+        nc.vector.memset(early_planes[:].bitcast(I32), 0)
+        nc.vector.memset(bias_rows[:], 0.0)
         load_x("r", FIRST)
         load_words("k")
         load_x("j", FIRST)
         load_words("j")
-        stage_scales(late_staged, LATE)
+        for w, row in LATE_ROW.items():
+            stage_scales(w, late_staged[row : row + PACK, :, :])
         load_words("r")
         load_words("i")
         load_x("k", FIRST)
-        nc.vector.memset(bias_rows[:], 0.0)
         load_bias("r")
         load_bias("j")
         load_x("i", FIRST)
@@ -332,11 +337,6 @@ def tile_mix_quat_bias_kernel(
         for x in PARTS:
             load_x(x, WIDE)
 
-        for c0 in (0, HALF):
-            nc.vector.quantize_mx(
-                out=warm_codes[:, c0 : c0 + HALF].bitcast(FP8X4), scales=warm_scales[:, c0 : c0 + HALF], in_=zeros[:],
-            )
-        nc.vector.memset(early_planes[:].bitcast(I32), 0)
         warm_bank = ps.tile([P, BANK], F32, name="bank%d" % (BANKS - 1))
         for rep in range(WARM_PASSES):
             nc.tensor.matmul_mx(
@@ -344,13 +344,15 @@ def tile_mix_quat_bias_kernel(
                 rhs=warm_codes[:].bitcast(FP8X4), rhs_scale=warm_scales[:], start=True, stop=True,
             )
 
-        place_scales(early_planes, staged, (1, 2, 3, 0))
+        place_scales(early_planes, staged, (1, 2, 3, 0), PACK)
         cast_and_quantize_quickly("r")
         terms("pk", "r", FIRST)
         terms("pj", "r", FIRST)
         cast_and_quantize_quickly("j")
-        place_scales(late_planes, late_staged, (1, 2, 3))
-        terms("mi", "j", FIRST, drain=park)
+        place_scales(late_planes, late_staged, (1, 2, 3), QUAD)
+        terms("mi", "j", FIRST)
+        park("mi", 0, FIRST)
+        park("mi", 2, FIRST, "vector")
         terms("mr", "j", FIRST)
         terms("pj", "j", FIRST)
         terms("pk", "j", FIRST)

from contextlib import ExitStack

import concourse.mybir as mybir

K, N, T = 512, 512, 1024
FLOPS = 16 * 2 * K * N * T

F32 = mybir.dt.float32
BF16 = mybir.dt.bfloat16
I32 = mybir.dt.int32
U32 = mybir.dt.uint32
U8 = mybir.dt.uint8
FP8X4 = mybir.dt.float8_e4m3fn_x4
FP4X4 = mybir.dt.float4_e2m1fn_x4
ADD = mybir.AluOpType.add
MULT = mybir.AluOpType.mult
SUB = mybir.AluOpType.subtract

P = 128
PACK = 4
BANK = 512
HALF = BANK // 2
TILES = N // P
BANKS = 8
QUADS = 4
QUAD = P // QUADS
ALIGN = 256
RUN = 4
PARTS = "rjki"
EARLY = "kj"
LATE_ROW = {"r": 4, "i": 8}
FIRST, SECOND, WIDE = 0, 1, 2
CHUNKS = ((0, HALF), (HALF, HALF), (BANK, BANK))
WARM_PASSES = 7
QUICK_SPLIT = 192

WEIGHT = {
    "pr": {"r": "r"},
    "mr": {"j": "j", "k": "k", "i": "i"},
    "pi": {"r": "i", "k": "j", "i": "r"},
    "mi": {"j": "k"},
    "pj": {"r": "j", "j": "r", "i": "k"},
    "mj": {"k": "i"},
    "pk": {"r": "k", "j": "i", "k": "r"},
    "mk": {"i": "j"},
}
TWIN = {
    ("pk", "mi"): (("k", "rj", 0), ("i", "j", 0), ("r", "k", 0)),
    ("pr", "mj"): (("r", "r", 0), ("i", "k", 1)),
    ("mk", "pi"): (("j", "ik", 0), ("i", "r", 1), ("r", "i", 1)),
    ("pj", "mr"): (("j", "rj", 0), ("r", "j", 0), ("k", "ik", 0), ("i", "i", 1)),
}


def tile_mix_quat_bias_kernel(
    tc, xr, xi, xj, xk,
    wr_words, wr_scales, wi_words, wi_scales, wj_words, wj_scales, wk_words, wk_scales,
    br, bi, bj, bk, out_0, out_1, out_2, out_3,
):
    nc = tc.nc
    x_hbm = {"r": xr, "i": xi, "j": xj, "k": xk}
    words_hbm = {
        "r": wr_words[0].rearrange("p n t -> p (n t)"),
        "i": wi_words[0].rearrange("p n t -> p (n t)"),
        "j": wj_words[0],
        "k": wk_words[0],
    }
    scales_hbm = {"r": wr_scales[0], "i": wi_scales[0], "j": wj_scales[0], "k": wk_scales[0]}
    bias_hbm = {"r": br, "i": bi, "j": bj, "k": bk}
    out_hbm = {"r": out_0, "i": out_1, "j": out_2, "k": out_3}
    word_bytes = {"r": 4, "i": 4, "j": 2, "k": 2}
    word_dtype = {"r": FP8X4, "i": FP8X4, "j": FP4X4, "k": FP4X4}

    with ExitStack() as ctx:
        sb = ctx.enter_context(tc.tile_pool(name="sb", bufs=1))
        ps = ctx.enter_context(tc.psum_pool(name="ps", bufs=1))
        ctx.enter_context(tc.manual_schedule())

        def sbuf(name, shape, dtype, tag=""):
            return sb.tile(shape, dtype, name=name, tag=tag or name, align_bytes=ALIGN)

        w_words = {w: sbuf("words_" + w, [P, N * word_bytes[w]], U8) for w in PARTS}
        staged = sbuf("staged", [PACK, QUADS, len(EARLY) * N], U8)
        early_planes = sbuf("early_planes", [P, len(EARLY) * N], U8)
        late_staged = sbuf("late_staged", [P, QUADS, N], U8)
        late_planes = late_staged[:, 0, :]
        w_scales = {w: late_planes[LATE_ROW[w] :, :] for w in LATE_ROW}
        for w in EARLY:
            w_scales[w] = early_planes[:, EARLY.index(w) * N : (EARLY.index(w) + 1) * N]
        bias_rows = sbuf("bias_rows", [P, QUAD], F32)
        bias_cols = sbuf("bias_cols", [P, QUAD], F32)
        zeros = sbuf("zeros", [P, HALF * PACK], BF16)
        warm_codes = sbuf("warm_codes", [P, BANK], U32)
        warm_scales = sbuf("warm_scales", [P, BANK], U8)
        x_codes, x_scales = {}, {}
        for h, (t0, width) in enumerate(CHUNKS):
            for pair in ("rj", "ik"):
                codes = sbuf("codes_%s%d" % (pair, h), [P, 2 * width], U32)
                scales = sbuf("xscales_%s%d" % (pair, h), [P, 2 * width], U8)
                x_codes[pair, h] = codes[:]
                x_scales[pair, h] = scales[:]
                for side in range(2):
                    x_codes[pair[side], h] = codes[:, side * width : (side + 1) * width]
                    x_scales[pair[side], h] = scales[:, side * width : (side + 1) * width]
        result = {(o, half): sbuf("result_%s%d" % (o, half), [P, TILES, BANK], F32) for o in PARTS for half in range(2)}

        def result_cols(o, tiles, h):
            t0, width = CHUNKS[h]
            return result[o, t0 // BANK][:, tiles, t0 % BANK : t0 % BANK + width]

        raw = {}

        def load_x(x, h, c0=0, c1=None):
            t0, width = CHUNKS[h]
            c1 = width if c1 is None else c1
            raw[x, h, c0] = sbuf("raw_%s%d_%d" % (x, h, c0), [P, PACK, c1 - c0], F32)
            src = x_hbm[x].rearrange("(p j) t -> p j t", j=PACK)[:, :, t0 + c0 : t0 + c1]
            nc.sync.dma_start(out=raw[x, h, c0][:], in_=src)

        def load_words(w):
            nc.sync.dma_start(out=w_words[w][:].bitcast(I32), in_=words_hbm[w].bitcast(I32))

        def load_bias(o):
            nc.sync.dma_start(
                out=bias_rows[PARTS.index(o) : P : 8, :], in_=bias_hbm[o].rearrange("(n q c) -> q n c", n=TILES, q=QUADS),
            )

        def bias(o, n):
            col = 8 * n + PARTS.index(o)
            return bias_cols[:, col : col + 1]

        def cast(engine, dst, src):
            if engine == "gpsimd":
                nc.gpsimd.tensor_scalar(
                    out=dst.rearrange("p (c j) -> p c j", j=PACK), in0=src.rearrange("p j c -> p c j"),
                    scalar1=1.0, scalar2=0.0, op0=MULT, op1=ADD,
                )
            else:
                src = src.rearrange("p j (c i) -> p c j i", i=RUN)
                dst = dst.rearrange("p (c i j) -> p c j i", i=RUN, j=PACK)
                if engine == "scalar":
                    nc.scalar.copy(out=dst, in_=src)
                else:
                    nc.vector.tensor_copy(out=dst, in_=src)

        grouped = {}

        def cast_shared(x, h, c0=0, share=0, tag=""):
            src = raw[x, h, c0]
            width = src.shape[2]
            grouped[x, h, c0] = dst = sbuf("grouped_%s%d_%d" % (x, h, c0), [P, width * PACK], BF16, tag)
            if share < width:
                cast("scalar", dst[:, share * PACK :], src[:, :, share:])
            if share > 0:
                cast("vector", dst[:, : share * PACK], src[:, :, :share])

        def cast_and_quantize_quickly(x, split=QUICK_SPLIT):
            src = raw[x, FIRST, 0]
            dst = sbuf("grouped_%s" % x, [P, HALF * PACK], BF16)
            cast("scalar", dst[:, split * PACK :], src[:, :, split:])
            for c0, c1 in ((0, P), (P, split)):
                if c1 > c0:
                    cast("vector", dst[:, c0 * PACK : c1 * PACK], src[:, :, c0:c1])
            for c0 in (0, P):
                grouped[x, FIRST, c0] = dst[:, c0 * PACK : (c0 + P) * PACK]
                quantize(x, FIRST, c0)

        def cast_half(engine, x, h, side=None):
            half = CHUNKS[h][1] // 2
            c0 = half * (int(engine == "scalar") if side is None else side)
            name = "grouped_%s%d_%d" % (x, h, c0)
            grouped[x, h, c0] = dst = sbuf(name, [P, half * PACK], BF16, "by_gpsimd" if engine == "gpsimd" and c0 == 0 else name)
            cast(engine, dst[:], raw[x, h, 0][:, :, c0 : c0 + half])

        def quantize(x, h, c0=0):
            src = grouped[x, h, c0]
            c1 = c0 + src.shape[1] // PACK
            nc.vector.quantize_mx(out=x_codes[x, h][:, c0:c1].bitcast(FP8X4), scales=x_scales[x, h][:, c0:c1], in_=src[:])

        def quantize_halves(x, h):
            quantize(x, h, 0)
            quantize(x, h, CHUNKS[h][1] // 2)

        free_banks = list(range(BANKS))
        held = {}
        parked = {}
        cols_left = {}

        def take_bank(key):
            bank = free_banks[0]
            free_banks.remove(bank)
            held[key] = bank, ps.tile([P, BANK], F32, name="bank%d" % bank)

        def mx_pass(key, col, w, n, xs, h, start, stop, cols=None):
            wb = word_bytes[w]
            cols = cols or slice(0, len(xs) * CHUNKS[h][1])
            width = cols.stop - cols.start
            nc.tensor.matmul_mx(
                out=held[key][1][:, col : col + width],
                lhsT=w_words[w][:, n * P * wb : (n + 1) * P * wb].bitcast(word_dtype[w]),
                lhsT_scale=w_scales[w][:, n * P : (n + 1) * P],
                rhs=x_codes[xs, h][:, cols].bitcast(FP8X4),
                rhs_scale=x_scales[xs, h][:, cols],
                start=start,
                stop=stop,
            )

        def add_term(name, x, n, h, cols=None):
            key = name, n, h
            width = CHUNKS[h][1]
            cols = cols or slice(0, width)
            opening = key not in held
            if opening:
                take_bank(key)
                cols_left[key] = len(WEIGHT[name]) * BANK
            for side in range(BANK // width):
                cols_left[key] = cols_left[key] - (cols.stop - cols.start)
                mx_pass(key, side * width + cols.start, WEIGHT[name][x], n + side, x, h,
                        opening and side == 0, cols_left[key] == 0, cols)

        def twin(names, n, h, first=0, last=None):
            key = names, n, h
            steps = TWIN[names]
            if first == 0:
                take_bank(key)
            for step in range(first, len(steps) if last is None else last):
                w, xs, side = steps[step]
                mx_pass(key, side * HALF, w, n, xs, h, step == 0, step == len(steps) - 1)

        def sides_of(key):
            name, n, h = key
            if h == WIDE:
                return [(name, n)]
            if name in WEIGHT:
                return [(name, n), (name, n + 1)]
            return [(name[0], n), (name[1], n)]

        def park(name, n, h, engine="scalar"):
            key = name, n, h
            bank, acc = held[key]
            sides = sides_of(key)
            if h == SECOND:
                spot = sbuf("spare_%s%d" % (sides[0][0], n), [P, 2, HALF], F32)[:]
            else:
                spot = result_cols(name[1], slice(n, n + len(sides)), h)
            src = acc[:].rearrange("p (s c) -> p s c", s=len(sides))
            if engine == "scalar":
                nc.scalar.copy(out=spot, in_=src)
            else:
                nc.vector.tensor_copy(out=spot, in_=src)
            for side, (s, m) in enumerate(sides):
                parked[s, m, h] = spot[:, side, :]
            free_banks.append(bank)

        def store(o, half, n, cols=slice(0, BANK)):
            rows = out_hbm[o][n * P : (n + 1) * P, half * BANK : (half + 1) * BANK]
            nc.sync.dma_start(out=rows[:, cols], in_=result[o, half][:, n, cols])

        def combine(name, n, h):
            key = name, n, h
            bank, acc = held[key]
            width = CHUNKS[h][1]
            for side, (s, m) in enumerate(sides_of(key)):
                o = s[1]
                mine = acc[:, side * width : (side + 1) * width]
                if s[0] == "p":
                    plus, minus = mine, parked["m" + o, m, h]
                else:
                    plus, minus = parked["p" + o, m, h], mine
                nc.vector.scalar_tensor_tensor(
                    out=result_cols(o, m, h), in0=plus, scalar=bias(o, m), in1=minus, op0=ADD, op1=SUB,
                )
            free_banks.append(bank)

        def close_piece(name, n, cols):
            o = name[1]
            key = name, n, cols.start
            take_bank(key)
            bank, acc = held[key]
            sums = acc[:, : cols.stop - cols.start]
            spot = result_cols(o, n, WIDE)[:, cols]
            terms = list(WEIGHT[name].items())
            for step, (x, w) in enumerate(terms):
                mx_pass(key, 0, w, n, x, WIDE, step == 0, step == len(terms) - 1, cols)
            if name[0] == "p":
                nc.scalar.copy(out=spot, in_=sums)
            else:
                nc.vector.scalar_tensor_tensor(out=spot, in0=spot, scalar=bias(o, n), in1=sums, op0=ADD, op1=SUB)
                store(o, 1, n, cols)
            free_banks.append(bank)

        pairs = range(0, TILES, 2)

        def terms(name, x, h, cols=None, drain=None):
            for n in pairs if h == FIRST else range(TILES):
                add_term(name, x, n, h, cols)
                if drain:
                    drain(name, n, h)

        def stage_scales(w, rows):
            nc.sync.dma_start(
                out=rows.bitcast(I32), in_=scales_hbm[w].bitcast(I32).rearrange("(q r) n -> r q n", r=PACK),
            )

        def place_scales(planes, tile, quadrants, rows):
            for q in quadrants:
                nc.vector.tensor_copy(
                    out=planes[QUAD * q : QUAD * q + rows, :].bitcast(I32), in_=tile[:rows, q, :].bitcast(I32),
                )

        nc.vector.memset(zeros[:].bitcast(I32), 0)
        for slot, w in enumerate(EARLY):
            stage_scales(w, staged[:, :, slot * N : (slot + 1) * N])
        for c0 in (0, HALF):
            nc.vector.quantize_mx(
                out=warm_codes[:, c0 : c0 + HALF].bitcast(FP8X4), scales=warm_scales[:, c0 : c0 + HALF], in_=zeros[:],
            )
        nc.vector.memset(late_staged[:].bitcast(I32), 0)
        nc.vector.memset(early_planes[:].bitcast(I32), 0)
        nc.vector.memset(bias_rows[:], 0.0)
        load_x("r", FIRST)
        load_words("k")
        load_x("j", FIRST)
        load_words("j")
        for w, row in LATE_ROW.items():
            stage_scales(w, late_staged[row : row + PACK, :, :])
        load_words("r")
        load_words("i")
        load_x("k", FIRST)
        load_bias("r")
        load_bias("j")
        load_x("i", FIRST)
        load_bias("k")
        load_bias("i")
        for x in PARTS:
            load_x(x, SECOND)
        for x in PARTS:
            load_x(x, WIDE)

        warm_bank = ps.tile([P, BANK], F32, name="bank%d" % (BANKS - 1))
        for rep in range(WARM_PASSES):
            nc.tensor.matmul_mx(
                out=warm_bank[:], lhsT=warm_codes[:, :P].bitcast(FP8X4), lhsT_scale=warm_scales[:, :P],
                rhs=warm_codes[:].bitcast(FP8X4), rhs_scale=warm_scales[:], start=True, stop=True,
            )

        place_scales(early_planes, staged, (1, 2, 3, 0), PACK)
        cast_and_quantize_quickly("r")
        terms("pk", "r", FIRST)
        terms("pj", "r", FIRST)
        cast_and_quantize_quickly("j")
        place_scales(late_planes, late_staged, (1, 2, 3), QUAD)
        terms("mi", "j", FIRST)
        park("mi", 0, FIRST)
        park("mi", 2, FIRST, "vector")
        terms("mr", "j", FIRST)
        terms("pj", "j", FIRST)
        terms("pk", "j", FIRST)
        cast_and_quantize_quickly("k")
        terms("pr", "r", FIRST, drain=park)
        cast_shared("i", FIRST, 0, HALF)
        nc.vector.transpose(bias_cols[:], bias_rows[:])
        quantize("i", FIRST)
        terms("pk", "k", FIRST, drain=park)
        terms("mr", "k", FIRST)
        cast_shared("r", SECOND, 0, HALF)
        terms("mj", "k", FIRST, drain=park)
        terms("mr", "i", FIRST)
        quantize("r", SECOND)
        cast_shared("j", SECOND, 0, P)
        for n in pairs:
            combine("mr", n, FIRST)
        quantize("j", SECOND)
        cast_shared("k", SECOND)
        terms("pj", "i", FIRST)
        terms("mk", "i", FIRST)
        for x in "rki":
            terms("pi", x, FIRST)
        for n in pairs:
            combine("pj", n, FIRST)
            if n == 0:
                quantize("k", SECOND)
        cast_shared("i", SECOND, 0, 0, "by_gpsimd")
        combine("mk", 0, FIRST)
        quantize("i", SECOND)
        for side in range(2):
            cast_half("gpsimd", "r", WIDE, side)

        for n in range(TILES // 2):
            twin(("pk", "mi"), n, SECOND, 0, 2)
        for n in range(TILES):
            twin(("pk", "mi"), n, SECOND, 2 if n < TILES // 2 else 0, 3)
            park(("pk", "mi"), n, SECOND)
            if n == 0:
                combine("mk", 2, FIRST)
        for n in pairs:
            combine("pi", n, FIRST)
        for n in range(TILES):
            twin(("pr", "mj"), n, SECOND)
            park(("pr", "mj"), n, SECOND)
            twin(("mk", "pi"), n, SECOND)
            combine(("mk", "pi"), n, SECOND)
            for o in "ki":
                store(o, 0, n)
            if n == 0:
                cast_half("scalar", "j", WIDE)
            if n == 2:
                quantize_halves("r", WIDE)
                cast_half("gpsimd", "j", WIDE)
        cast_shared("k", WIDE)
        for n in range(TILES):
            twin(("pj", "mr"), n, SECOND)
            combine(("pj", "mr"), n, SECOND)
            for o in "jr":
                store(o, 0, n)
            if n == 1:
                quantize_halves("j", WIDE)
        quantize("k", WIDE)
        cast_shared("i", WIDE, 0, P)
        quantize("i", WIDE)

        def close_wide(name, n, drain):
            for x in WEIGHT[name]:
                add_term(name, x, n, WIDE)
            drain(name, n, WIDE)

        for x in "rj":
            terms("pk", x, WIDE)
        for n in range(TILES):
            add_term("mi", "j", n, WIDE)
            park("mi", n, WIDE, "vector" if n % 2 else "scalar")
        terms("pk", "k", WIDE, drain=park)
        for name in ("mk", "pi"):
            for n in range(TILES):
                close_wide(name, n, combine)
                store(name[1], 1, n)
        for n in range(TILES):
            close_wide("mj", n, park)
            close_wide("pj", n, combine)
            store("j", 1, n)
        for n in range(TILES // 2):
            close_wide("pr", n, park)
            close_wide("mr", n, combine)
            store("r", 1, n)
        for n, c0, c1 in ((2, 0, 256), (2, 256, 512), (3, 0, 256), (3, 256, 384), (3, 384, 512)):
            for name in ("pr", "mr"):
                close_piece(name, n, slice(c0, c1))
